import numpy as np, ml_dtypes
CORES = [24,25,26,27,28,29,30,31]
N = 8
import mx_ref
BF = ml_dtypes.bfloat16
def entries(a):
    return np.ascontiguousarray(a.T).reshape(-1)
def table(e):
    return np.ascontiguousarray(np.reshape(e, (-1, 16)).T).astype(np.int32)
def pick(q, e):
    c = np.concatenate([q[0].reshape(128, -1, 4), np.zeros((128, 1, 4), np.uint8)], axis=1); s = np.concatenate([q[1], np.ones((16, 1), np.uint8)], axis=1)
    return (np.ascontiguousarray(c[:, e].reshape(128, -1)), np.ascontiguousarray(s[:, e]))
def join(*qs):
    return (np.concatenate([q[0] for q in qs], axis=1), np.concatenate([q[1] for q in qs], axis=1))
def put(q, e, v):
    c, s = q[0].reshape(128, -1, 4).copy(), q[1].copy(); c[:, e] = v[0].reshape(128, -1, 4); s[:, e] = v[1]
    return (c.reshape(128, -1), s)
def pk(c, s):
    return (np.ascontiguousarray(c), mx_ref.live(s))
def emit(q):
    return q[0], q[1]
def packed(v, rng):
    q = [mx_ref.quantize(np.ascontiguousarray(v[r])) for r in range(N)]
    return np.stack([a for a, b in q]), np.stack([mx_ref.plane(b, rng) for a, b in q])
def f(rng, *shape):
    return mx_ref.flush((rng.standard_normal(shape, dtype=np.float32) * np.exp2(rng.integers(-2, 3, shape[:-1] + (1,)))).astype(BF))
def wide(rng, *shape, cols=0):
    v = rng.standard_normal(shape, dtype=np.float32) * np.exp2(rng.integers(-12, 13, shape)).astype(np.float32)
    if cols: v *= np.repeat(np.exp2(rng.integers(-cols, cols + 1, shape[:-2] + (1, shape[-1] // 4))) * (rng.random(shape[:-2] + (1, shape[-1] // 4)) > 0.0625), 4, axis=-1).astype(np.float32)
    return mx_ref.flush(v.astype(BF))
C, CB, CAPP, S = 512, 128, 80, 512
def counts(rng, total, cap, least):
    n = np.array(least)
    while n.sum() < total: n[rng.choice(np.flatnonzero(n < cap))] += 1
    return n
def runs(rng, least, cap):
    n = np.zeros((N, N), int)
    for s in range(N)[::-1]: n[s] = counts(rng, C, np.minimum(cap[s], CAPP + n[N - 1]), least[s])
    return n
def keeps(rng, n, fall=0, least=np.zeros((N, N), int)):
    k = np.zeros((N, N), int)
    for s in range(N)[::-1]:
        above = k.sum(axis=0)
        k[s] = np.clip(np.minimum(rng.integers(0, 2 * n[s] // 3 + 1), n[s] - fall), np.maximum(n[s] - above, least[s]), np.minimum(np.minimum(n[s], CAPP), S - above))
    return k
def lists(rng, n, k, ends=False, narrow=False):
    p = np.sort(rng.choice(65536 - 2 * N * S, N - 1, replace=False)) + 2 * S * np.arange(1, N)
    if ends: p[0] = int(k[:, 0].sum()) + 2 + int(rng.integers(0, 4))
    if narrow: p[-1] = 65535
    lo, hi = np.append(0, p), np.append(p, 65536)
    keys = [[] for s in range(N)]
    for d in range(N):
        e, i, j = int(ends), -1, -1
        u = lo[d] + e + rng.choice(int(hi[d] - lo[d]) - 2 * e, int(k[:, d].sum()), replace=False)
        at = np.append(np.cumsum(k[::-1, d])[::-1], 0)[1:]
        if ends:
            low, c = np.flatnonzero(n[:, d] - k[:, d] > 1), np.flatnonzero(k[:, d] > 1)
            c = c[c > low[0]]
            if d in (0, N - 1): c = c[c < N - 1]
            i = rng.choice(c); j = rng.choice(low[low < i])
            u[at[i]] = lo[d]; u[at[i] + 1] = hi[d] - 1
        for s in range(N):
            m = at[i] + np.arange(2) if s == j else np.zeros(0, int)
            old = np.concatenate([m, rng.permutation(np.setdiff1d(np.arange(at[s]), m))])[:n[s, d] - k[s, d]]
            keys[s].append(u[np.concatenate([old, at[s] + np.arange(k[s, d])])])
    return {"ky": np.stack([table(np.sort(np.concatenate(v))) for v in keys]), "sp": np.stack([table(np.append(p, np.full(17 - N, 65535)))] * N)}
def setup_inputs(rng):
    kc, ks = packed(f(rng, N, 128, 4 * C), rng)
    n = runs(rng, rng.integers(1, CAPP // 2 + 1, (N, N)), np.full((N, N), CB))
    return {"kc": kc, "ks": ks, "w": f(rng, N, 128, 512), **lists(rng, n, keeps(rng, n))}
def setup_inputs_single(rng):
    least, cap = rng.integers(1, CAPP // 2 + 1, (N, N)), np.full((N, N), CB)
    least[:, N - 1] = rng.integers(0, 2, N); least[rng.permutation(N - 1)[:2], N - 1] = 1; cap[:, N - 1] = least[:, N - 1]
    n = runs(rng, least, cap)
    return {**setup_inputs(rng), **lists(rng, n, keeps(rng, n), narrow=True)}
def setup_inputs_narrow(rng):
    least, cap = rng.integers(1, CAPP // 2 + 1, (N, N)), np.full((N, N), CB)
    least[:, N - 1] = 0; cap[:, N - 1] = 0
    n = runs(rng, least, cap)
    return {**setup_inputs(rng), **lists(rng, n, keeps(rng, n), narrow=True)}
def setup_inputs_full(rng):
    h = int(rng.integers(0, N)); least = np.ones((N, N), int)
    a = np.append(h, rng.permutation(np.delete(np.arange(N), h)))[:(C - N) // CAPP]
    least[N - 1, a] = CAPP
    for s in range(N - 1): least[s, np.append(h, rng.permutation(a[1:]))[:(C - N) // CB]] = CB
    n = runs(rng, least, np.full((N, N), CB)); k = keeps(rng, n)
    v = np.zeros(N, int); v[N - 2:] = CAPP; v[rng.permutation(N - 2)[:S // CAPP - 2]] = CAPP
    k[:, h] = counts(rng, S, CAPP, v)
    return {**setup_inputs(rng), **lists(rng, n, k)}
def setup_inputs_edges(rng):
    q = int(rng.integers(1, N)); h = int(rng.choice(np.delete(np.arange(N - 1), min(q, N - 2))))
    least, cap = rng.integers(2, CAPP // 2 + 1, (N, N)), np.full((N, N), CB)
    least[h, q] = 0; cap[h, q] = 0
    few = rng.integers(2, 5, N)
    few[rng.permutation(np.setdiff1d(np.arange(N), [int(rng.integers(0, N - 2)), N - 2]))[:int(rng.integers(2, N - 1))]] = 0
    least[:, 0] = few; cap[:, 0] = few
    n = runs(rng, least, cap)
    two = np.zeros((N, N), int); two[N - 2, [0, N - 1]] = 2
    return {**setup_inputs(rng), **lists(rng, n, keeps(rng, n, 2, two), ends=True)}
def setup_inputs_spread(rng):
    d = setup_inputs(rng); d["kc"], d["ks"] = packed(wide(rng, N, 128, 4 * C, cols=8), rng); return d
def check_inputs(d):
    b = []
    p = entries(d["sp"][0]).astype(np.int64); g = p[:N - 1]
    if (d["sp"] != d["sp"][:1]).any() or (p[N - 1:] != 65535).any() or g.min() < 1 or g.max() > 65535 or (np.diff(g) <= 0).any(): b.append("sp")
    lo, hi = np.append(0, g), np.append(g, 65536)
    k = [entries(d["ky"][s]).astype(np.int64) for s in range(N)]
    bad = any(v.min() < 0 or v.max() > 65535 or (np.diff(v) <= 0).any() for v in k)
    x, s = np.concatenate(k), np.repeat(np.arange(N), C)
    o = np.argsort(x, kind="stable"); o = o[np.append(x[o][1:] != x[o][:-1], True)]
    x, s = x[o], s[o]
    for q in range(N):
        m = (x >= lo[q]) & (x < hi[q])
        if max(((v >= lo[q]) & (v < hi[q])).sum() for v in k) > CB or m.sum() > S or np.bincount(s[m], minlength=N).max() > CAPP: bad = True
    if bad: b.append("ky")
    return b
def reference(kc, ks, w, ky, sp):
    every = join(*[pk(kc[s], ks[s]) for s in range(N)])
    keys = np.concatenate([entries(ky[s]) for s in range(N)])
    oc, osc = np.zeros((N, 128, 4 * S), np.uint8), np.zeros((N, 16, S), np.uint8)
    ok, y = np.zeros((N, 2, S), np.float32), np.zeros((N, 128, S), np.float32)
    for d in range(N):
        p = entries(sp[d])[:N - 1]
        lo, hi = np.append(0, p)[d], np.append(p, 65536)[d]
        e = np.flatnonzero((keys >= lo) & (keys < hi))
        e = e[np.argsort(keys[e], kind="stable")]
        e = e[np.append(keys[e][1:] != keys[e][:-1], True)[:e.size]]
        a = np.full(S, -1); a[:e.size] = e
        kept = pick(every, a)
        oc[d], osc[d] = emit(kept)
        ok[d, 0] = np.where(a >= 0, keys[a], -1); ok[d, 1] = np.where(a >= 0, a // C, -1)
        y[d] = mx_ref.matmul(mx_ref.quantize(np.ascontiguousarray(w[d])), kept)
    return {"oc": oc, "osc": osc, "ok": ok, "y": y}

@@ -1,0 +1,401 @@
+from concourse.bass import DstId, RemoteDMATransfer
+from concourse.mybir import dt, AluOpType, AxisListType, ActivationFunctionType
+
+SCRATCH = {"mykd": ("dram", [128, 8], "int32"), "kd0": ("dram", [4, 128, 8], "int32"), "kd1": ("dram", [4, 128, 8], "int32"),
+           "acc": ("psum", [128, 1024], "float32")}
+SIZES = {
+    (128, "float32"): "tkf:32 blo:32 m0:512 xb:512 xg:256 val:256 vk:256 vc:256 vd:256 ta0:32 ta1:32 bl0:32 bl1:32 ps:32 it:1040 ix:112 im:80 mh:40 ico:160 irk:240 "
+                      "cst:80 jf:5 pd:5 jt:10 s0:16 wi:1040 wt:768 qk:24 qi:32 xt:32 yy:64 ot:64 kx:24 mm:640 xf:640 x6:16 nx6:16 sm:5 "
+                      "pm:5 kg:80 va2:80 w2:960 w2t:512 t3:48 sr:32 sx:32 sy:64 so:64 yf:656 yo:512",
+    (32, "float32"): "tr:16 spf:1 spm:32 spb:32 d7:112 d7s:112 rs7:112 d96:20 c4:64 a2:32 kb:20 f1:16 nk:16 zz:20 pl:64 pt:64 cc:64 cy:32 "
+                     "pq:16 pf:16 c5:64 a5:32 c6:128 a6:64 k2:32 ro:32",
+    (128, "bfloat16"): "cm0:512 cm1:512 ct0:512 ct1:512 cs0:512 cs1:512 eq:512 et:512 es:512 rs32:512 rs16:512 rs160:640 zb:512 wb:512 jk:1920 cb:1280 cbs:1280",
+    (128, "int32"): "tk:32 ti0:32 ti1:32 pi:8", (32, "int32"): "spi:1",
+    (128, "uint16"): "xu:512 of0:16 of1:16 mb:32 mo:40 oxn:32 oxg:16 ovk:16 okg:6 ox6:2 pw:16 off:48 pu:6 of2:32",
+    (128, "float8_e4m3fn_x4"): "zc:128 kcs:512 qc:640 lc:656 fc:512 wc:128",
+    (128, "uint8"): "zs:128 kss:512 qs:640 ls:672 fz:512 wz:128"}
+for (_p, _d), _l in SIZES.items():
+    for _x in _l.split():
+        SCRATCH[_x.split(":")[0]] = ("sbuf", [_p, int(_x.split(":")[1])], _d)
+SEMAPHORES = ["vs", "ss", "ts", "gs", "dk", "dt", "dsp", "dw", "dkc", "dz", "dta", "dtb", "dkx", "doc", "doc2", "dos", "dy", "dy2", "dy3", "dok",
+              "rk", "rx", "rc", "rs", "loc"]
+
+
+def rank_program(g, core, T, topo):
+    s = T.rank_of(core)
+    if s is None:
+        return
+    A, N = AluOpType, len(T.cores)
+    AF = ActivationFunctionType
+    q_of = {"v": g.vector, "s": g.scalar, "t": g.tensor, "g": g, "y": g.sync}
+    own = {"v": "vs", "s": "ss", "t": "ts", "g": "gs"}
+    tot = {n: 0 for n in SEMAPHORES}
+    seen = {q: {} for q in q_of}
+    wr, rd = {}, {}
+
+    def need(q, r, w, add=False):
+        deps = [(d, 0) for t in r for d in wr.get(t, [])]
+        deps += [(d, 1) for t in w for d in wr.get(t, []) + rd.get(t, [])]
+        for (sem, n), order in deps:
+            if order and add and own.get(q) == sem:
+                continue
+            n = tot[sem] if n is None else n
+            if seen[q].get(sem, 0) < n:
+                q_of[q].wait_ge(T.sem[sem], n)
+                seen[q][sem] = n
+
+    def note(me, r, w, add=False):
+        for t in r:
+            rd.setdefault(t, []).append(me)
+        for t in w:
+            wr[t] = wr.get(t, []) + [me] if add else [me]
+            if not add:
+                rd[t] = []
+
+    def E(q, call, r, w, *args, add=False, **kw):
+        need(q, r, w, add)
+        sem = own[q]
+        call(*args, **kw).then_inc(T.sem[sem], 1)
+        tot[sem] += 1
+        note((sem, tot[sem]), r, w, add)
+
+    def D(q, sem, out, in_, r, w, add=True):
+        need(q, r, [] if add == "par" else w)
+        q_of[q].dma_start(out, in_).then_inc(T.sem[sem], 16)
+        tot[sem] += 16
+        note((sem, None), r, w, True)
+
+    V, S = g.vector, g.scalar
+
+    def copy(r, w, out, in_, add=False): E("v", V.tensor_copy, r, w, out, in_, add=add)
+    def tt(r, w, out, a, b, op, add=False): E("v", V.tensor_tensor, r, w, out, a, b, op, add=add)
+    def ts(r, w, out, a, s1, op, s2=None, op1=None, add=False):
+        if op1 is None: E("v", V.tensor_scalar, r, w, out, a, s1, None, op, add=add)
+        else: E("v", V.tensor_scalar, r, w, out, a, s1, s2, op, op1, add=add)
+    def tp(r, w, out, in_, add=False): E("v", V.transpose, r, w, out, in_, add=add)
+    def scan(r, w, out, a, b, init, o0, o1, add=False): E("v", V.tensor_tensor_scan, r, w, out, a, b, init, o0, o1, add=add)
+    def fill(w, ap, c, add=False): E("v", V.memset, [], w, ap, c, add=add)
+    def act(r, w, out, in_, fn=AF.Copy, **kw): E("s", S.activation, r, w, out, in_, fn, **kw)
+    def iota(w, ap, pat, base, mult=0):
+        E("g", g.iota, [], w, ap, pat, base, mult, allow_small_or_imprecise_dtypes=True)
+
+    later = []
+
+    def gap(n=1):
+        for _ in range(min(n, len(later))):
+            later.pop(0)()
+
+    def fused(pairs, sem, per, r):
+        need("g", r, [])
+        tr = []
+        for i, (c, dst, src) in enumerate(pairs):
+            rid, pid, _ = topo.addr(c)
+            e = topo.engines(core, c)[per * i:per * (i + 1)]
+            tr.append(RemoteDMATransfer(dst_ids=[DstId(rid=rid, pnc=pid)], dma_engine_mask=sum(1 << k for k in e),
+                                        remote_sem=T.sem[sem], src=src, dst=dst))
+        g.remote_dma_fused(tr, local_sem=T.sem.loc)
+        tot["loc"] += per * len(pairs)
+
+    passes = [h for h in (0, 1) if any(2 * a + h > s for a in range(4))]
+    first = {h: min(a for a in range(4) if 2 * a + h > s) for h in passes}
+    odd = s % 2
+
+    if s > 0:
+        for k in (0, 1):
+            D("y" if k == 0 else "s", "dk", T.mykd[64 * k:64 * k + 64, :], T.ky[:], [], ["mykd"], "par")
+    for k in range(8):
+        D("y" if k % 2 == 0 else "s", "dt", T.tk[16 * k:16 * k + 16, :], T.ky[:], [], ["tk"], "par")
+    for k in (0, 1):
+        D("y", "dsp", T.spi[16 * k:16 * k + 16, :], T.sp[:], [], ["spi"], "par")
+    D("y", "dkc", T.kcs[:].bitcast(dt.uint8), T.kc[:], [], ["kcs"], "par")
+    D("y", "dkc", T.kss[:], T.ks[:], [], ["kss"], "par")
+    D("y", "dw", T.wb[:], T.w[:], [], ["wb"], "par")
+
+    iota(["pi"], T.pi[:, 0:1], [[0, 1]], 0, 1)
+    iota(["imb"], T.ix[:, 0:32], [[1, 16], [0, 2]], 0)
+    iota(["ixn"], T.ix[:, 48:80], [[64, 8], [16, 2], [32, 2]], 0)
+    iota(["ixg"], T.ix[:, 80:96], [[64, 8], [16, 2]], 0)
+    iota(["ivk"], T.ix[:, 96:112], [[32, 16]], 0)
+    if s > 0:
+        fused([(T.cores[r], T["kd%d" % odd][s // 2], T.mykd[:]) for r in range(s)], "rk", 1, ["mykd"])
+    iota(["vc"], T.vc[:], [[1, 16], [16, 16]], 0)
+    iota(["d96"], T.d96[:], [[0, 20]], 0)
+    if not passes:
+        iota(["kb"], T.kb[:], [[0, 20]], 1)
+    iota(["kb"], T.kb[:, 0:1], [[0, 1]], 0)
+    iota(["im2"], T.im[:, 40:80], [[0, 4], [1, 5], [0, 2]], 0)
+    iota(["im"], T.im[:, 0:40], [[6, 4], [1, 5], [0, 2]], 0)
+    iota(["tr"], T.tr[:], [[16, 16]], 768, 1)
+    for n, c in (("zz", 20), ("pl", 64), ("cc", 64), ("qi", 32)):
+        iota([n], T[n][:], [[0, c]], 0)
+    iota(["ikg"], T.ix[:, 32:37], [[32, 5]], 0)
+    iota(["irk"], T.irk[:, 0:80], [[1, 5], [0, 16]], 0)
+    iota(["it"], T.it[:], [[-1, 1040]], -(66000 + 768 * s))
+    iota(["ico"], T.ico[:, 0:80], [[32, 5], [1, 16]], 16)
+    iota(["jf"], T.jf[:, 0:3], [[32, 3]], 10897, 2)
+    iota(["jf2"], T.jf[:, 3:5], [[16, 2]], 10816, 1)
+    for n, c in (("sr", 32), ("k2", 32)):
+        iota([n], T[n][:], [[0, c]], 0)
+
+    for h in passes:
+        if first[h]:
+            fill(["ti%d" % h], T["ti%d" % h][0:32 * first[h], :], -1)
+    ts(["pi"], ["pi1"], T.pi[:, 1:2], T.pi[:, 0:1], 15, A.bitwise_and)
+    ts(["pi"], ["pi2"], T.pi[:, 2:3], T.pi[:, 0:1], 4, A.logical_shift_right, 1, A.bitwise_and)
+    ts(["pi"], ["pi3"], T.pi[:, 3:4], T.pi[:, 0:1], 5, A.logical_shift_right)
+    fill(["rs32"], T.rs32[:], 1.0)
+    fill(["rs7"], T.rs7[:], 1.0)
+    copy(["pi1", "pi2", "pi3"], ["ps"], T.ps[:, 0:3], T.pi[:, 1:4])
+    P = lambda k: T.ps[:, k:k + 1]
+    copy(["imb"], ["mb"], T.mb[:], T.ix[:, 0:32])
+    fill(["rs16"], T.rs16[:], 1.0)
+    ts(["ps"], ["ps3"], P(3), P(1), 16.0, A.mult, P(0), A.add)
+    ts(["ps"], ["ps4"], P(4), P(1), 32.0, A.mult, P(0), A.add)
+    ts(["ps"], ["ps7"], P(7), P(1), 256.0, A.mult)
+    ts(["ps"], ["ps10"], P(10), P(0), 0.0, A.is_equal)
+    ts(["ps"], ["ps11"], P(11), P(0), 0.0, A.not_equal, -1.0, A.mult)
+    ts(["ps"], ["ps14"], P(14), P(0), 0.0, A.not_equal)
+    ts(["ixn", "ps"], ["oxn"], T.oxn[:], T.ix[:, 48:80], P(0), A.add)
+    ts(["ixg", "ps4"], ["oxg"], T.oxg[:], T.ix[:, 80:96], P(4), A.add)
+    ts(["ivk", "ps3"], ["ovk"], T.ovk[:], T.ix[:, 96:112], P(3), A.add)
+    ts(["ps7", "ps10"], ["ps16"], P(16), P(7), P(10), A.mult)
+    fill(["rs7"], T.rs7[:, 0:112:7], 0.0)
+    fill(["rs32"], T.rs32[:, 0:512:32], 0.0)
+    fill(["rs16"], T.rs16[:, 0:512:16], 0.0)
+    copy(["tk"], ["tkf"], T.tkf[:], T.tk[:])
+    copy(["spi"], ["spf"], T.spf[:], T.spi[:])
+    tp(["tkf"], ["blo"], T.blo[:], T.tkf[:])
+    ts(["tkf", "spf"], ["spm"], T.spm[:], T.tkf[0:32, :], 0.0, A.mult, T.spf[:, 0:1], A.add)
+    copy(["blo", "mb"], ["m0"], T.m0[:], T.blo[:, 0:32].indirect(T.mb[:, 0:32]))
+    tp(["spm"], ["spb"], T.spb[:], T.spm[:])
+    tp(["m0"], ["xb"], T.xb[:], T.m0[:])
+    if passes:
+        act(["xb", "oxg"], ["xg"], T.xg[:], T.xb[:, 0:512].indirect(T.oxg[:, 0:16]))
+    act(["xb", "ovk", "ps11"], ["vk"], T.vk[:], T.xb[:, 0:512].indirect(T.ovk[:, 0:16]), scale=P(11))
+    act(["vc", "ps10", "ps16"], ["vd"], T.vd[:], T.vc[:], AF.Identity, scale=P(10), bias=P(16))
+    act(["it", "ps14"], ["wi"], T.wi[:], T.it[:], scale=P(14))
+    act(["it"], ["w2"], T.w2[:], T.it[:, 0:960], scale=0.0)
+    act(["it"], ["yfz"], T.yf[:, 0:16], T.it[:, 0:16], scale=0.0)
+    for e in range(N - 1):
+        ts(["blo", "spb"], ["d7"], T.d7[:, e:112:7], T.blo[0:32, 0:16], T.spb[:, e:e + 1], A.is_ge, 96.0, A.mult, add=True)
+    if passes:
+        copy(["xb", "oxn"], ["xu"], T.xu[:], T.xb[:, 0:512].indirect(T.oxn[:, 0:32]))
+    scan(["d7", "rs7"], ["d7s"], T.d7s[:], T.rs7[:], T.d7[:], 0.0, A.mult, A.add)
+    tt(["vk", "vd"], ["val"], T.val[:], T.vk[:], T.vd[:], A.add)
+    ts(["d7s"], ["d96"], T.d96[:, 0:16], T.d7s[:, 6:112:7], 16.0 * odd, A.add)
+    fill(["rs160"], T.rs160[:], 1.0)
+
+    later += [
+        lambda: ts(["im2", "ps"], ["mh"], T.mh[:], T.im[:, 40:80], P(1), A.add, 3.0, A.is_ge),
+        lambda: ts(["ps"], ["ps18"], P(18), P(0), P(1), A.add, 3.0, A.is_ge),
+        lambda: ts(["ps"], ["ps9"], P(9), P(2), 6.0, A.mult, P(0), A.add),
+        lambda: ts(["ps"], ["ps6"], P(6), P(1), 16.0, A.mult),
+        lambda: tt(["im", "mh"], ["mo"], T.mo[:], T.im[:, 0:40], T.mh[:], A.add),
+        lambda: ts(["ps", "ps3"], ["ps5"], P(5), P(2), 160.0, A.mult, P(3), A.add),
+        lambda: ts(["ps9", "ps18"], ["ps19"], P(19), P(9), P(18), A.add),
+        lambda: ts(["ps", "ps6"], ["ps15"], P(15), P(2), 160.0, A.mult, P(6), A.add),
+        lambda: ts(["ps"], ["ps8"], P(8), P(2), 2.0, A.mult, 1.0, A.add),
+        lambda: ts(["ps19"], ["ox6"], T.ox6[:, 0:1], P(19), 23.0, A.min),
+        lambda: ts(["ps"], ["ps13"], P(13), P(0), 2.0, A.is_equal),
+        lambda: ts(["ps"], ["ps12"], P(12), P(0), 1.0, A.is_equal, -1.0, A.mult),
+        lambda: ts(["ps15", "ps10"], ["ps17"], P(17), P(15), P(10), A.mult),
+        lambda: ts(["ikg", "ps5"], ["okg"], T.okg[:, 0:5], T.ix[:, 32:37], P(5), A.add),
+        lambda: ts(["irk", "ps"], ["irk1"], T.irk[:, 80:160], T.irk[:, 0:80], P(1), A.add, 3.0, A.is_ge),
+        lambda: ts(["ps8", "ps13", "ps12"], ["ps20"], P(20), P(8), P(13), A.mult, P(12), A.subtract),
+        lambda: fill(["rs160"], T.rs160[:, 0:640:160], 0.0)]
+
+    if passes:
+        tot["rk"] = N - 1 - s
+        wr["rk"] = [("rk", None)]
+        for h in passes:
+            a = first[h]
+            D("y", "dta" if h == 0 else "dtb", T["ti%d" % h][32 * a:128, :], T["kd%d" % h][a:4], ["rk"], ["ti%d" % h], True)
+        H = ["%d" % h for h in passes]
+        for h in H: copy(["ti" + h], ["ta" + h], T["ta" + h][:], T["ti" + h][:])
+        for h in H: tp(["ta" + h], ["bl" + h], T["bl" + h][:], T["ta" + h][:])
+        for h in H: ts(["xu", "bl" + h], ["cm" + h], T["cm" + h][:], T.xu[:], T["bl" + h][:, 0:1], A.is_ge)
+        for h in H: tp(["cm" + h], ["ct" + h], T["ct" + h][:], T["cm" + h][:])
+        for h in H: scan(["ct" + h, "rs32"], ["cs" + h], T["cs" + h][:], T.rs32[:], T["ct" + h][:], 0.0, A.mult, A.add)
+        for h in H: ts(["cs" + h], ["of" + h], T["of" + h][:], T["cs" + h][:, 31:512:32], 1.0, A.subtract, 0.0, A.max)
+        for i, h in enumerate(H):
+            tt(["ta" + h, "of" + h, "xg"], ["eq"], T.eq[:, 256 * i:256 * i + 256], T["ta" + h][:, 0:32].indirect(T["of" + h][:, 0:16]), T.xg[:], A.is_equal, add=True)
+        n = 256 * len(H)
+        tp(["eq"], ["et"], T.et[:, 0:n], T.eq[:, 0:n])
+        gap()
+        scan(["et", "rs16"], ["es"], T.es[:, 0:n], T.rs16[:, 0:n], T.et[:, 0:n], 0.0, A.mult, A.add)
+        gap()
+        if len(H) == 2: tt(["es"], ["s0"], T.s0[:], T.es[:, 15:256:16], T.es[:, 271:512:16], A.add)
+        else: copy(["es"], ["s0"], T.s0[:], T.es[:, 15:256:16])
+        gap()
+        quads = list(range(min(first.values()), 4))
+        nq = len(quads)
+        C4 = lambda i: T.c4[:, 16 * i:16 * i + 16]
+        for i, a in enumerate(quads):
+            at = [0, 2, 1, 3][i] if nq == 4 else i
+            if i < (nq + 1) // 2: copy(["s0"], ["c4"], C4(at), T.s0[32 * a:32 * a + 32, :], add=True)
+            else: ts(["s0"], ["c4"], C4(at), T.s0[32 * a:32 * a + 32, :], -1.0, A.mult, add=True)
+        gap()
+        if nq == 4:
+            tt(["c4"], ["a2"], T.a2[:], T.c4[:, 0:32], T.c4[:, 32:64], A.add)
+            gap()
+            x, y, r = T.a2[:, 0:16], T.a2[:, 16:32], ["a2"]
+        elif nq == 3:
+            tt(["c4"], ["a2"], T.a2[:, 0:16], C4(0), C4(1), A.add)
+            gap()
+            x, y, r = T.a2[:, 0:16], C4(2), ["a2", "c4"]
+        else:
+            x, y, r = C4(0), C4(1), ["c4"]
+        if nq == 1:
+            ts(r, ["kb"], T.kb[:, 1:17], x, 0.0, A.is_equal)
+            ts(r, ["f1"], T.f1[:], x, 0.0, A.is_gt)
+        else:
+            tt(r, ["kb"], T.kb[:, 1:17], x, y, A.is_equal)
+            tt(r, ["f1"], T.f1[:], x, y, A.not_equal)
+    scan(["kb", "zz"], ["pl"], T.pl[:, 0:17], T.kb[:, 0:17], T.zz[:, 0:17], 0.0, A.add, A.add)
+    scan(["kb", "d96"], ["pl"], T.pl[:, 32:49], T.kb[:, 0:17], T.d96[:, 0:17], 0.0, A.add, A.max, add=True)
+    gap()
+    tp(["pl"], ["pt"], T.pt[:], T.pl[:])
+    if passes: tt(["f1", "tr"], ["nk"], T.nk[:], T.f1[:], T.tr[:], A.mult)
+    scan(["pt"], ["cc"], T.cc[:, 1:33], T.pt[:, 0:32], T.pt[:, 32:64], 0.0, A.add, A.max)
+    gap()
+    tp(["cc"], ["cy"], T.cy[:], T.cc[:, 0:32])
+    gap()
+    scan(["kb", "d96", "cy"], ["pq"], T.pq[:], T.kb[:, 0:16], T.d96[:, 0:16], T.cy[:, 16:17], A.add, A.max)
+    src, tok = T.pq, "pq"
+    gap()
+    if passes:
+        tt(["pq", "nk"], ["pf"], T.pf[:], T.pq[:], T.nk[:], A.max)
+        src, tok = T.pf, "pf"
+        gap()
+    for a in range(4):
+        copy([tok], ["pw"], T.pw[32 * a:32 * a + 32, :], src[:], add=True)
+    gap()
+    E("v", V.tensor_copy, ["pw", "val"], ["wi"], T.wi[:, 0:1040].indirect(T.pw[:, 0:16]), T.val[:])
+    gap()
+    tp(["wi"], ["wt"], T.wt[:], T.wi[:, 0:768])
+    gap()
+    tt(["wt"], ["qk"], T.qk[:], T.wt[:, 1:768:32], T.wt[:, 17:768:32], A.max)
+    tt(["wt"], ["qi"], T.qi[:, 0:24], T.wt[:, 0:768:32], T.wt[:, 16:768:32], A.max)
+    peers = [(s + i) % N for i in range(1, N)]
+    fused([(T.cores[d], T.kx[:, 3 * s:3 * s + 3], T.qk[:, 3 * d:3 * d + 3]) for d in peers], "rx", 2, ["qk"])
+    D("y", "dkx", T.kx[:, 3 * s:3 * s + 3], T.qk[:, 3 * s:3 * s + 3], ["qk"], ["kx"], "par")
+    gap()
+    tp(["qi"], ["xt"], T.xt[:], T.qi[:])
+    gap()
+    for k in range(4):
+        copy(["xt"], ["yy"], T.yy[:, 16 * k:16 * k + 16], T.xt[:, 16 * (k // 2):16 * (k // 2) + 16], add=True)
+    gap()
+    tp(["yy"], ["ot"], T.ot[:], T.yy[:])
+    gap()
+    if odd:
+        copy(["ot"], ["off"], T.off[:, 0:48:2], T.ot[:, 32:56])
+        copy(["ot"], ["off"], T.off[:, 1:47:2], T.ot[:, 1:24], add=True)
+    else:
+        copy(["ot"], ["off"], T.off[:, 0:48:2], T.ot[:, 0:24])
+        copy(["ot"], ["off"], T.off[:, 1:48:2], T.ot[:, 32:56], add=True)
+    def pick(d, cbuf, sbuf, c, tc, tz):
+        E("v", V.tensor_copy, ["off", "kcs"], [tc], cbuf[:, c:c + 80].bitcast(dt.uint32), T.kcs[:, 0:512].bitcast(dt.uint32).indirect(T.off[:, 6 * d:6 * d + 5]))
+        act(["off", "kss"], [tz], sbuf[:, c:c + 80], T.kss[:, 0:512].indirect(T.off[:, 6 * d:6 * d + 5]))
+    for d in peers: pick(d, T.qc, T.qs, 80 * d, "qc%d" % d, "qs%d" % d)
+    pick(s, T.lc, T.ls, 16 + 80 * s, "lco", "lso")
+    me = 16 + 80 * s
+    for part in (peers[:1], peers[1:3], peers[3:]):
+        e = len(topo.engines(core, T.cores[part[0]])) // len(part)
+        fused([(T.cores[d], T.lc[:, me:me + 80].bitcast(dt.uint8), T.qc[:, 80 * d:80 * d + 80].bitcast(dt.uint8)) for d in part], "rc", e, ["qc%d" % d for d in part])
+        fused([(T.cores[d], T.ls[:, me:me + 80], T.qs[:, 80 * d:80 * d + 80]) for d in part], "rs", e, ["qs%d" % d for d in part])
+        for r in part:
+            tot["rc"] += e
+            tot["rs"] += e
+    gap(len(later))
+    act(["ico", "ps17", "ps10"], ["ico2"], T.ico[:, 80:160], T.ico[:, 0:80], AF.Identity, scale=P(10), bias=P(17))
+    act(["irk1", "ps20", "ps13"], ["irk2"], T.irk[:, 160:240], T.irk[:, 80:160], AF.Identity, scale=P(13), bias=P(20))
+    E("v", V.quantize_mx, ["wb"], ["wc", "wz"], T.wc[:], T.wz[:], T.wb[:])
+    fill(["zb"], T.zb[:], 0.0)
+    tt(["ico2", "irk2"], ["cst"], T.cst[:], T.ico[:, 80:160], T.irk[:, 160:240], A.add)
+    E("v", V.quantize_mx, ["zb"], ["zc", "zs"], T.zc[:], T.zs[:], T.zb[:])
+    D("y", "dz", T.lc[:, 0:1].bitcast(dt.uint8), T.zc[:, 0:1].bitcast(dt.uint8), ["zc"], ["lcz"], "par")
+    D("y", "dz", T.ls[:, 0:1], T.zs[:, 0:1], ["zs"], ["lsz"], "par")
+    tot["rx"] = 2 * (N - 1)
+    wr["rx"] = [("rx", None)]
+    act(["rx", "kx", "mo"], ["mmS"], T.mm[:, 256:640], T.kx[:, 0:24].indirect(T.mo[:, 16:40]))
+    copy(["rx", "kx", "ox6"], ["x6"], T.x6[:], T.kx[:, 0:24].indirect(T.ox6[:, 0:1]))
+    copy(["rx", "kx", "mo"], ["mmV"], T.mm[:, 0:256], T.kx[:, 0:24].indirect(T.mo[:, 0:16]))
+    ts(["x6"], ["nx6"], T.nx6[:], T.x6[:], -1.0, A.mult)
+    ts(["x6"], ["pd"], T.pd[:], T.x6[:, 0:5], -65536.0, A.is_lt)
+    tp(["mmV"], ["xfV"], T.xf[:, 0:256], T.mm[:, 0:256])
+    tp(["mmS"], ["xfS"], T.xf[:, 256:640], T.mm[:, 256:640])
+    xf = ["xfV", "xfS"]
+    tt(["pd", "jf", "jf2"], ["jt0"], T.jt[:, 5:10], T.pd[:], T.jf[:], A.mult)
+    def count(e):
+        act(xf + ["nx6"], ["jk%d" % e, "sm%d" % e], T.jk[:, 640 * e:640 * e + 640], T.xf[:], AF.Sign, bias=T.nx6[:, e:e + 1], accum_out=T.sm[:, e:e + 1])
+    count(0)
+    act(xf + ["okg", "ps12"], ["kg"], T.kg[:], T.xf[:, 0:640].indirect(T.okg[:, 0:5]), scale=P(12))
+    count(1)
+    count(2)
+    for k in (0, 1):
+        ts(xf + ["x6"], ["cb%d" % k], T.cb[:, 640 * k:640 * k + 640], T.xf[:], T.x6[:, 3 + k:4 + k], A.is_gt)
+    for k in (0, 1):
+        scan(["cb%d" % k, "rs160"], ["cbs%d" % k], T.cbs[:, 640 * k:640 * k + 640], T.rs160[:], T.cb[:, 640 * k:640 * k + 640], 0.0, A.mult, A.add)
+    tt(["kg", "cst"], ["va2"], T.va2[:], T.kg[:], T.cst[:], A.add)
+    ts(["jt0"], ["jt"], T.jt[:, 0:5], T.jt[:, 5:10], 10000.0, A.subtract)
+    for k in (0, 1):
+        E("v", V.tensor_reduce, ["cbs%d" % k], ["sm%d" % (3 + k)], T.sm[:, 3 + k:4 + k], T.cbs[:, 640 * k + 159:640 * k + 640:160], AxisListType.X, A.add)
+    tt(["sm%d" % e for e in range(5)] + ["jt"], ["pm"], T.pm[:], T.sm[:], T.jt[:, 0:5], A.max)
+    ts(["pm"], ["pu"], T.pu[:, 0:3], T.pm[:, 0:3], 639.0, A.add, 0.5, A.mult)
+    copy(["pm"], ["pu"], T.pu[:, 3:5], T.pm[:, 3:5], add=True)
+    E("v", V.tensor_copy, ["pu", "va2"], ["w2"], T.w2[:, 0:960].indirect(T.pu[:, 0:5]), T.va2[:])
+    tp(["w2"], ["w2t"], T.w2t[:], T.w2[:, 0:512])
+    def ok_rows():
+        tp(["k2"], ["ro"], T.ro[:], T.k2[:])
+        D("y", "dok", T.ok[0:1, :], T.ro[0:16, 0:32], ["ro"], ["ok"], "par")
+        D("y", "dok", T.ok[1:2, :], T.ro[16:32, 0:32], ["ro"], ["ok"], "par")
+    later += [lambda k=k: tt(["w2t"], ["t3k"], T.t3[:, 16 * k:16 * k + 16], T.w2t[:, k:512:32], T.w2t[:, 16 + k:512:32], A.add, add=True) for k in (1, 2)]
+    later += [lambda a=a: copy(["t3k"], ["c6"], T.c6[:, 32 * a:32 * a + 32], T.t3[32 * a:32 * a + 32, 16:48], add=True) for a in range(4)]
+    later += [
+        lambda: tt(["c6"], ["a6"], T.a6[:], T.c6[:, 0:64], T.c6[:, 64:128], A.add),
+        lambda: tt(["a6"], ["c6b"], T.c6[:, 0:32], T.a6[:, 0:32], T.a6[:, 32:64], A.add),
+        lambda: ts(["c6b"], ["k2"], T.k2[:], T.c6[:, 0:32], 1.0, A.subtract),
+        ok_rows]
+    for a in range(4):
+        tt(["w2t"], ["c5"], T.c5[:, 16 * a:16 * a + 16], T.w2t[32 * a:32 * a + 32, 0:512:32], T.w2t[32 * a:32 * a + 32, 16:512:32], A.add, add=True)
+    gap(2)
+    tt(["c5"], ["a5"], T.a5[:], T.c5[:, 0:32], T.c5[:, 32:64], A.add)
+    gap()
+    for a in range(4):
+        tt(["a5"], ["sr"], T.sr[32 * a:32 * a + 32, 0:16], T.a5[:, 0:16], T.a5[:, 16:32], A.add, add=a > 0)
+    gap()
+    tp(["sr"], ["sx"], T.sx[:], T.sr[:])
+    gap()
+    for k in range(4):
+        copy(["sx"], ["sy"], T.sy[:, 16 * k:16 * k + 16], T.sx[:, 16 * (k // 2):16 * (k // 2) + 16], add=True)
+    gap()
+    tp(["sy"], ["so"], T.so[:], T.sy[:])
+    gap()
+    copy(["so"], ["of2"], T.of2[:, 0:32:2], T.so[:, 0:16])
+    copy(["so"], ["of2"], T.of2[:, 1:32:2], T.so[:, 32:48], add=True)
+    wr["lca"], wr["lsa"] = [("rc", None)], [("rs", None)]
+    land, lands = ["lca", "lco", "lcz"], ["lsa", "lso", "lsz"]
+    for k in (0, 1):
+        c = 16 + 320 * k
+        E("t", g.tensor.matmul_mx, land + lands + ["wc", "wz"], ["acc%d" % k], T.acc[:, 512 * k:512 * k + 320], T.wc[:], T.wz[:], T.lc[:, c:c + 320], T.ls[:, c:c + 320], True, True)
+    for k in (0, 1):
+        act(["acc%d" % k], ["yf%d" % k], T.yf[:, 16 + 320 * k:336 + 320 * k], T.acc[:, 512 * k:512 * k + 320])
+    ys = ["yfz", "yf0", "yf1", "of2"]
+    def codes(k):
+        E("v", V.tensor_copy, land + ["of2"], ["fc%d" % k], T.fc[:, 256 * k:256 * k + 256].bitcast(dt.uint32), T.lc[:, 0:656].bitcast(dt.uint32).indirect(T.of2[:, 16 * k:16 * k + 16]))
+        D("y", ["doc", "doc2"][k], T.oc[:, 1024 * k:1024 * k + 1024], T.fc[:, 256 * k:256 * k + 256].bitcast(dt.uint8), ["fc%d" % k], ["oc"], "par")
+    codes(0)
+    act(ys, ["yo0"], T.yo[:, 0:256], T.yf[:, 0:656].indirect(T.of2[:, 0:16]))
+    D("y", "dy", T.y[:, 0:256], T.yo[:, 0:256], ["yo0"], ["y"], "par")
+    codes(1)
+    act(lands + ["of2"], ["fz"], T.fz[:], T.ls[:, 0:656].indirect(T.of2[:, 0:32]))
+    for k in range(4):
+        D("s", "dos", T.osc[4 * k:4 * k + 4, :], T.fz[32 * k:32 * k + 4, :], ["fz"], ["osc"], "par")
+    for k in (0, 1):
+        c = 256 + 128 * k
+        copy(ys, ["yo%d" % (1 + k)], T.yo[:, c:c + 128], T.yf[:, 0:656].indirect(T.of2[:, 16 + 8 * k:24 + 8 * k]))
+        D("y", ["dy2", "dy3"][k], T.y[:, c:c + 128], T.yo[:, c:c + 128], ["yo%d" % (1 + k)], ["y"], "par")
+    gap(len(later))
+    for n in SEMAPHORES:
+        if tot[n]:
+            g.wait_ge(T.sem[n], tot[n])

@@ -1,24 +1,22 @@
 from concourse.bass import DstId, RemoteDMATransfer
 from concourse.mybir import dt, AluOpType, AxisListType, ActivationFunctionType
 
-SCRATCH = {"mykd": ("dram", [128, 8], "int32"), "kd0": ("dram", [4, 128, 8], "int32"), "kd1": ("dram", [4, 128, 8], "int32"),
-           "acc": ("psum", [128, 1024], "float32")}
+SCRATCH = {"mykd": ("dram", [128, 8], "int32"), "kd": ("dram", [7, 128, 8], "int32"), "acc": ("psum", [128, 1024], "float32")}
 SIZES = {
-    (128, "float32"): "tkf:32 blo:32 m0:512 xb:512 xg:256 val:256 vk:256 vc:256 vd:256 ta0:32 ta1:32 bl0:32 bl1:32 ps:32 it:1040 ix:112 im:80 mh:40 ico:160 irk:240 "
-                      "cst:80 jf:5 pd:5 jt:10 s0:16 wi:1040 wt:768 qk:24 qi:32 xt:32 yy:64 ot:64 kx:24 mm:640 xf:640 x6:16 nx6:16 sm:5 "
-                      "pm:5 kg:80 va2:80 w2:960 w2t:512 t3:48 sr:32 sx:32 sy:64 so:64 yf:656 yo:512",
-    (32, "float32"): "tr:16 spf:1 spm:32 spb:32 d7:112 d7s:112 rs7:112 d96:20 c4:64 a2:32 kb:20 f1:16 nk:16 zz:20 pl:64 pt:64 cc:64 cy:32 "
-                     "pq:16 pf:16 c5:64 a5:32 c6:128 a6:64 k2:32 ro:32",
-    (128, "bfloat16"): "cm0:512 cm1:512 ct0:512 ct1:512 cs0:512 cs1:512 eq:512 et:512 es:512 rs32:512 rs16:512 rs160:640 zb:512 wb:512 jk:1920 cb:1280 cbs:1280",
-    (128, "int32"): "tk:32 ti0:32 ti1:32 pi:8", (32, "int32"): "spi:1",
-    (128, "uint16"): "xu:512 of0:16 of1:16 mb:32 mo:40 oxn:32 oxg:16 ovk:16 okg:6 ox6:2 pw:16 off:48 pu:6 of2:32",
+    (128, "float32"): "ldf:32 zt:48 m0:512 xb:512 xg:512 mv:256 val:256 pvf:2 ps:32 ix:96 im:80 mh:40 ic:80 cst:80 i8:8 wi:1184 wt:672 qk:24 qi:32 "
+                      "xt:32 yy:64 ot:64 kx:24 mm:640 xk:656 nx6:16 sm:4 kg:80 va2:80 w2:640 w2t:512 sx:32 sy:64 so:64 yf:656 yo:512 ko:512",
+    (32, "float32"): "spn:16 spb:16 tr:16 d7:112 d7s:112 rs7:112 d96:20 c4:64 rk4:64 rz4:64 ks4:68 f1:16 nk:16 pl:64 pt:64 cc:64 cy:32 pq:16 c5:64 cz:128",
+    (128, "bfloat16"): "cm0:512 cm1:512 ct0:512 ct1:512 cs0:256 cs1:256 eq:512 et:512 es:272 zb:512 wb:512 jk:1920 cb:1280 cbs:640",
+    (128, "int32"): "ti:64 piv:2 pi:8", (32, "int32"): "ld:32 spr:16",
+    (128, "uint16"): "xu:512 of1:32 mb:32 mo:40 oxg:32 omv:16 okg:6 ox6:2 ody:4 oof:4 oo2:2 pw:16 off:48 pu:6 of2:32",
     (128, "float8_e4m3fn_x4"): "zc:128 kcs:512 qc:640 lc:656 fc:512 wc:128",
     (128, "uint8"): "zs:128 kss:512 qs:640 ls:672 fz:512 wz:128"}
 for (_p, _d), _l in SIZES.items():
     for _x in _l.split():
         SCRATCH[_x.split(":")[0]] = ("sbuf", [_p, int(_x.split(":")[1])], _d)
-SEMAPHORES = ["vs", "ss", "ts", "gs", "dk", "dt", "dsp", "dw", "dkc", "dz", "dta", "dtb", "dkx", "doc", "doc2", "dos", "dy", "dy2", "dy3", "dok",
-              "rk", "rx", "rc", "rs", "loc"]
+SEMAPHORES = ["vs", "ss", "ts", "gs", "dk", "dt", "dsp", "dw", "dkc", "dz", "dpv", "dti", "dkx", "dlc", "doc0", "doc1", "dos", "dy0", "dy1", "dok",
+              "rk", "rx", "rc", "rs", "loc", "lk"]
+CHUNKS = ((0, 128), (128, 512))
 
 
 def rank_program(g, core, T, topo):
@@ -59,8 +57,8 @@ def rank_program(g, core, T, topo):
         tot[sem] += 1
         note((sem, tot[sem]), r, w, add)
 
-    def D(q, sem, out, in_, r, w, add=True):
-        need(q, r, [] if add == "par" else w)
+    def D(q, sem, out, in_, r, w, par=True):
+        need(q, r, [] if par else w)
         q_of[q].dma_start(out, in_).then_inc(T.sem[sem], 16)
         tot[sem] += 16
         note((sem, None), r, w, True)
@@ -85,7 +83,7 @@ def rank_program(g, core, T, topo):
         for _ in range(min(n, len(later))):
             later.pop(0)()
 
-    def fused(pairs, sem, per, r):
+    def fused(pairs, sem, per, r, loc="loc"):
         need("g", r, [])
         tr = []
         for i, (c, dst, src) in enumerate(pairs):
@@ -93,286 +91,239 @@ def rank_program(g, core, T, topo):
             e = topo.engines(core, c)[per * i:per * (i + 1)]
             tr.append(RemoteDMATransfer(dst_ids=[DstId(rid=rid, pnc=pid)], dma_engine_mask=sum(1 << k for k in e),
                                         remote_sem=T.sem[sem], src=src, dst=dst))
-        g.remote_dma_fused(tr, local_sem=T.sem.loc)
-        tot["loc"] += per * len(pairs)
+        g.remote_dma_fused(tr, local_sem=T.sem[loc])
+        tot[loc] += per * len(pairs)
 
-    passes = [h for h in (0, 1) if any(2 * a + h > s for a in range(4))]
-    first = {h: min(a for a in range(4) if 2 * a + h > s) for h in passes}
+    higher = N - 1 - s
+    lists = [n for n in (min(higher, 4), higher - 4) if n > 0]
+    NP = len(lists)
+    nq = lists[0] if lists else 1
     odd = s % 2
+    slot = lambda src, dst: src ^ (dst % 2)
 
     if s > 0:
         for k in (0, 1):
-            D("y" if k == 0 else "s", "dk", T.mykd[64 * k:64 * k + 64, :], T.ky[:], [], ["mykd"], "par")
-    for k in range(8):
-        D("y" if k % 2 == 0 else "s", "dt", T.tk[16 * k:16 * k + 16, :], T.ky[:], [], ["tk"], "par")
+            D("ys"[k], "dk", T.mykd[64 * k:64 * k + 64, :], T.ky[:], [], ["mykd"])
     for k in (0, 1):
-        D("y", "dsp", T.spi[16 * k:16 * k + 16, :], T.sp[:], [], ["spi"], "par")
-    D("y", "dkc", T.kcs[:].bitcast(dt.uint8), T.kc[:], [], ["kcs"], "par")
-    D("y", "dkc", T.kss[:], T.ks[:], [], ["kss"], "par")
-    D("y", "dw", T.wb[:], T.w[:], [], ["wb"], "par")
+        D("ys"[k], "dt", T.ld[8 * k:8 * k + 8, :], T.ky[:, 16 * k:16 * k + 16], [], ["ld"])
+    D("y", "dt", T.ld[16:32, :], T.ky[:], [], ["ld"])
+    D("s", "dsp", T.spr[0:1, :], T.sp[:], [], ["spr"])
 
     iota(["pi"], T.pi[:, 0:1], [[0, 1]], 0, 1)
     iota(["imb"], T.ix[:, 0:32], [[1, 16], [0, 2]], 0)
-    iota(["ixn"], T.ix[:, 48:80], [[64, 8], [16, 2], [32, 2]], 0)
-    iota(["ixg"], T.ix[:, 80:96], [[64, 8], [16, 2]], 0)
-    iota(["ivk"], T.ix[:, 96:112], [[32, 16]], 0)
+    iota(["ixg"], T.ix[:, 32:64], [[0, 2], [32, 8], [256, 2]], 0)
+    iota(["imv"], T.ix[:, 64:80], [[1, 8], [8, 2]], 0)
+    iota(["idz"], T.ix[:, 80:96], [[-256, 2], [-2, 8]], 0)
     if s > 0:
-        fused([(T.cores[r], T["kd%d" % odd][s // 2], T.mykd[:]) for r in range(s)], "rk", 1, ["mykd"])
-    iota(["vc"], T.vc[:], [[1, 16], [16, 16]], 0)
-    iota(["d96"], T.d96[:], [[0, 20]], 0)
-    if not passes:
-        iota(["kb"], T.kb[:], [[0, 20]], 1)
-    iota(["kb"], T.kb[:, 0:1], [[0, 1]], 0)
-    iota(["im2"], T.im[:, 40:80], [[0, 4], [1, 5], [0, 2]], 0)
-    iota(["im"], T.im[:, 0:40], [[6, 4], [1, 5], [0, 2]], 0)
-    iota(["tr"], T.tr[:], [[16, 16]], 768, 1)
-    for n, c in (("zz", 20), ("pl", 64), ("cc", 64), ("qi", 32)):
-        iota([n], T[n][:], [[0, c]], 0)
-    iota(["ikg"], T.ix[:, 32:37], [[32, 5]], 0)
-    iota(["irk"], T.irk[:, 0:80], [[1, 5], [0, 16]], 0)
-    iota(["it"], T.it[:], [[-1, 1040]], -(66000 + 768 * s))
-    iota(["ico"], T.ico[:, 0:80], [[32, 5], [1, 16]], 16)
-    iota(["jf"], T.jf[:, 0:3], [[32, 3]], 10897, 2)
-    iota(["jf2"], T.jf[:, 3:5], [[16, 2]], 10816, 1)
-    for n, c in (("sr", 32), ("k2", 32)):
-        iota([n], T[n][:], [[0, c]], 0)
+        fused([(T.cores[r], T.kd[s - r - 1], T.mykd[:]) for r in range(s)], "rk", 1, ["mykd"], "lk")
+    sent = tot["lk"]
 
-    for h in passes:
-        if first[h]:
-            fill(["ti%d" % h], T["ti%d" % h][0:32 * first[h], :], -1)
-    ts(["pi"], ["pi1"], T.pi[:, 1:2], T.pi[:, 0:1], 15, A.bitwise_and)
-    ts(["pi"], ["pi2"], T.pi[:, 2:3], T.pi[:, 0:1], 4, A.logical_shift_right, 1, A.bitwise_and)
-    ts(["pi"], ["pi3"], T.pi[:, 3:4], T.pi[:, 0:1], 5, A.logical_shift_right)
-    fill(["rs32"], T.rs32[:], 1.0)
-    fill(["rs7"], T.rs7[:], 1.0)
-    copy(["pi1", "pi2", "pi3"], ["ps"], T.ps[:, 0:3], T.pi[:, 1:4])
+    fill(["zb"], T.zb[:], 0.0)
+    for k, (sh, m) in enumerate(((0, 15), (4, 1), (5, 3), (0, 31), (0, 1), (1, 7))):
+        ts(["pi"], ["pi%d" % k], T.pi[:, 1 + k:2 + k], T.pi[:, 0:1], sh, A.logical_shift_right, m, A.bitwise_and)
+    E("v", V.quantize_mx, ["zb"], ["zc", "zs"], T.zc[:], T.zs[:], T.zb[:])
+    copy(["pi%d" % k for k in range(6)], ["ps"], T.ps[:, 0:6], T.pi[:, 1:7])
     P = lambda k: T.ps[:, k:k + 1]
     copy(["imb"], ["mb"], T.mb[:], T.ix[:, 0:32])
-    fill(["rs16"], T.rs16[:], 1.0)
-    ts(["ps"], ["ps3"], P(3), P(1), 16.0, A.mult, P(0), A.add)
-    ts(["ps"], ["ps4"], P(4), P(1), 32.0, A.mult, P(0), A.add)
-    ts(["ps"], ["ps7"], P(7), P(1), 256.0, A.mult)
-    ts(["ps"], ["ps10"], P(10), P(0), 0.0, A.is_equal)
-    ts(["ps"], ["ps11"], P(11), P(0), 0.0, A.not_equal, -1.0, A.mult)
-    ts(["ps"], ["ps14"], P(14), P(0), 0.0, A.not_equal)
-    ts(["ixn", "ps"], ["oxn"], T.oxn[:], T.ix[:, 48:80], P(0), A.add)
-    ts(["ixg", "ps4"], ["oxg"], T.oxg[:], T.ix[:, 80:96], P(4), A.add)
-    ts(["ivk", "ps3"], ["ovk"], T.ovk[:], T.ix[:, 96:112], P(3), A.add)
-    ts(["ps7", "ps10"], ["ps16"], P(16), P(7), P(10), A.mult)
+    ts(["ps"], ["ps6"], P(6), P(0), 0.0, A.is_equal, 32.0, A.mult)
+    ts(["ps"], ["ps7"], P(7), P(0), -16.0, A.mult, P(1), A.subtract)
+    ts(["ps"], ["ps8"], P(8), P(3), 32.0, A.add)
+    ts(["ixg", "ps"], ["oxg"], T.oxg[:], T.ix[:, 32:64], P(3), A.add)
+    ts(["imv", "ps6"], ["omv"], T.omv[:], T.ix[:, 64:80], P(6), A.add)
+    ts(["idz", "ps7"], ["ztc"], T.zt[:, 32:48], T.ix[:, 80:96], P(7), A.add)
+    for a in range(4):
+        copy(["ld"], ["ldf"], T.ldf[32 * a:32 * a + 32, :], T.ld[:], add=True)
+    ts(["spr"], ["spn"], T.spn[0:1, :], T.spr[0:1, :], -1.0, A.mult, 0.5, A.add)
+    tp(["ldf"], ["zt"], T.zt[:, 0:32], T.ldf[:])
+    fill(["rs7"], T.rs7[:], 1.0)
+    act(["zt", "mb"], ["m0b"], T.m0[:, 256:512], T.zt[:, 0:32].indirect(T.mb[:, 16:32]))
+    copy(["zt", "mb"], ["m0a"], T.m0[:, 0:256], T.zt[:, 0:32].indirect(T.mb[:, 0:16]))
     fill(["rs7"], T.rs7[:, 0:112:7], 0.0)
-    fill(["rs32"], T.rs32[:, 0:512:32], 0.0)
-    fill(["rs16"], T.rs16[:, 0:512:16], 0.0)
-    copy(["tk"], ["tkf"], T.tkf[:], T.tk[:])
-    copy(["spi"], ["spf"], T.spf[:], T.spi[:])
-    tp(["tkf"], ["blo"], T.blo[:], T.tkf[:])
-    ts(["tkf", "spf"], ["spm"], T.spm[:], T.tkf[0:32, :], 0.0, A.mult, T.spf[:, 0:1], A.add)
-    copy(["blo", "mb"], ["m0"], T.m0[:], T.blo[:, 0:32].indirect(T.mb[:, 0:32]))
-    tp(["spm"], ["spb"], T.spb[:], T.spm[:])
-    tp(["m0"], ["xb"], T.xb[:], T.m0[:])
-    if passes:
-        act(["xb", "oxg"], ["xg"], T.xg[:], T.xb[:, 0:512].indirect(T.oxg[:, 0:16]))
-    act(["xb", "ovk", "ps11"], ["vk"], T.vk[:], T.xb[:, 0:512].indirect(T.ovk[:, 0:16]), scale=P(11))
-    act(["vc", "ps10", "ps16"], ["vd"], T.vd[:], T.vc[:], AF.Identity, scale=P(10), bias=P(16))
-    act(["it", "ps14"], ["wi"], T.wi[:], T.it[:], scale=P(14))
-    act(["it"], ["w2"], T.w2[:], T.it[:, 0:960], scale=0.0)
-    act(["it"], ["yfz"], T.yf[:, 0:16], T.it[:, 0:16], scale=0.0)
+    tp(["m0a"], ["xba"], T.xb[:, 0:256], T.m0[:, 0:256])
+    tp(["m0b"], ["xbb"], T.xb[:, 256:512], T.m0[:, 256:512])
+    xb = ["xba", "xbb"]
+    if NP:
+        copy(["xba"], ["xu"], T.xu[:, 0:256], T.xb[:, 0:256], add=True)
+        copy(["xbb"], ["xu"], T.xu[:, 256:512], T.xb[:, 256:512], add=True)
+        for h, n in enumerate(lists):
+            for a in range(n, 4):
+                fill(["piv"], T.piv[32 * a:32 * a + 32, h:h + 1], 65536, add=True)
+                fill(["ti"], T.ti[32 * a:32 * a + 32, 32 * h:32 * h + 32], -1, add=True)
+        fill(["es0"], T.es[:, 0:1], 0.0)
+    act(["zt", "ztc", "omv"], ["mv"], T.mv[:], T.zt[:, 0:48].indirect(T.omv[:, 0:16]), scale=-1.0)
+    if NP:
+        act(xb + ["oxg"], ["xg"], T.xg[:, 0:256 * NP], T.xb[:, 0:512].indirect(T.oxg[:, 0:16 * NP]))
+    E("g", g.partition_broadcast, ["spn"], ["spb"], T.spb[:], T.spn[0:1, :], 32)
     for e in range(N - 1):
-        ts(["blo", "spb"], ["d7"], T.d7[:, e:112:7], T.blo[0:32, 0:16], T.spb[:, e:e + 1], A.is_ge, 96.0, A.mult, add=True)
-    if passes:
-        copy(["xb", "oxn"], ["xu"], T.xu[:], T.xb[:, 0:512].indirect(T.oxn[:, 0:32]))
-    scan(["d7", "rs7"], ["d7s"], T.d7s[:], T.rs7[:], T.d7[:], 0.0, A.mult, A.add)
-    tt(["vk", "vd"], ["val"], T.val[:], T.vk[:], T.vd[:], A.add)
-    ts(["d7s"], ["d96"], T.d96[:, 0:16], T.d7s[:, 6:112:7], 16.0 * odd, A.add)
-    fill(["rs160"], T.rs160[:], 1.0)
+        E("s", S.activation, ["zt", "spb"], ["d7"], T.d7[:, e:112:7], T.zt[0:32, 16:32], AF.Sign, bias=T.spb[:, e:e + 1], add=True)
+    iota(["ks4"], T.ks4[:], [[0, 68]], 0)
+    if not NP:
+        iota(["ks4"], T.ks4[:, 1:17], [[0, 16]], 1)
+    if nq > 1:
+        iota(["rk4"], T.rk4[:, 0:16 * nq], [[0, 16], [-1, nq]], 1)
+    for n, c in (("d96", 20), ("pl", 64), ("cc", 64)):
+        iota([n], T[n][:], [[0, c]], 0)
+    iota(["tr"], T.tr[:], [[1, 16]], 672, 16)
+    iota(["wi"], T.wi[:, 0:672], [[-1, 672]], -(66000 + 672 * s))
+    iota(["qi"], T.qi[:], [[0, 32]], 0)
+    iota(["i8"], T.i8[:, 0:4], [[0, 2], [16, 2]][::-1], 0)
+    iota(["i8b"], T.i8[:, 4:8], [[8, 4]], 0)
+    iota(["im2"], T.im[:, 40:80], [[0, 4], [1, 5], [0, 2]], 0)
+    iota(["im"], T.im[:, 0:40], [[6, 4], [1, 5], [0, 2]], 0)
+    iota(["ic"], T.ic[:], [[32, 5], [1, 16]], 0)
+    iota(["xk0"], T.xk[:, 0:16], [[0, 16]], 1)
+    iota(["yfz"], T.yf[:, 0:16], [[0, 16]], 0)
+    iota(["rz4"], T.rz4[:], [[0, 16], [1, 4]], 0)
+    iota(["cz"], T.cz[:], [[0, 128]], 0)
 
     later += [
+        lambda: tp(["mv"], ["val"], T.val[:], T.mv[:]),
+        lambda: scan(["d7", "rs7"], ["d7s"], T.d7s[:], T.rs7[:], T.d7[:], 0.0, A.mult, A.add),
+        lambda: ts(["d7s"], ["d96"], T.d96[:, 0:16], T.d7s[:, 6:112:7], 40.0, A.mult, 280.0 + 16 * odd, A.add),
+        lambda: ts(["ps"], ["ps10"], P(10), P(4), 32.0, A.mult, P(5), A.add),
+        lambda: ts(["ps"], ["ps11"], P(11), P(4), -31.0, A.mult, P(5), A.add),
+        lambda: ts(["i8", "ps"], ["ody"], T.ody[:], T.i8[:, 0:4], P(0), A.add),
+        lambda: ts(["i8b", "ps10", "ps11"], ["oof"], T.oof[:], T.i8[:, 4:8], P(10 + odd), A.add, 32.0 * odd, A.add),
         lambda: ts(["im2", "ps"], ["mh"], T.mh[:], T.im[:, 40:80], P(1), A.add, 3.0, A.is_ge),
         lambda: ts(["ps"], ["ps18"], P(18), P(0), P(1), A.add, 3.0, A.is_ge),
         lambda: ts(["ps"], ["ps9"], P(9), P(2), 6.0, A.mult, P(0), A.add),
-        lambda: ts(["ps"], ["ps6"], P(6), P(1), 16.0, A.mult),
         lambda: tt(["im", "mh"], ["mo"], T.mo[:], T.im[:, 0:40], T.mh[:], A.add),
-        lambda: ts(["ps", "ps3"], ["ps5"], P(5), P(2), 160.0, A.mult, P(3), A.add),
-        lambda: ts(["ps9", "ps18"], ["ps19"], P(19), P(9), P(18), A.add),
-        lambda: ts(["ps", "ps6"], ["ps15"], P(15), P(2), 160.0, A.mult, P(6), A.add),
-        lambda: ts(["ps"], ["ps8"], P(8), P(2), 2.0, A.mult, 1.0, A.add),
-        lambda: ts(["ps19"], ["ox6"], T.ox6[:, 0:1], P(19), 23.0, A.min),
-        lambda: ts(["ps"], ["ps13"], P(13), P(0), 2.0, A.is_equal),
-        lambda: ts(["ps"], ["ps12"], P(12), P(0), 1.0, A.is_equal, -1.0, A.mult),
-        lambda: ts(["ps15", "ps10"], ["ps17"], P(17), P(15), P(10), A.mult),
-        lambda: ts(["ikg", "ps5"], ["okg"], T.okg[:, 0:5], T.ix[:, 32:37], P(5), A.add),
-        lambda: ts(["irk", "ps"], ["irk1"], T.irk[:, 80:160], T.irk[:, 0:80], P(1), A.add, 3.0, A.is_ge),
-        lambda: ts(["ps8", "ps13", "ps12"], ["ps20"], P(20), P(8), P(13), A.mult, P(12), A.subtract),
-        lambda: fill(["rs160"], T.rs160[:, 0:640:160], 0.0)]
+        lambda: ts(["ps9", "ps18"], ["ox6"], T.ox6[:, 0:1], P(9), P(18), A.add, 23.0, A.min),
+        lambda: ts(["ps"], ["ps12"], P(12), P(2), 160.0, A.mult, P(3), A.add),
+        lambda: ts(["i8b", "ps10"], ["oo2"], T.oo2[:], T.i8[:, 4:6], P(10), A.add),
+        lambda: ts(["ps12"], ["ps13"], P(13), P(12), P(0), A.subtract, 16.0, A.add),
+        lambda: ts(["ic", "ps12"], ["okg"], T.okg[:, 0:5], T.ic[:, 0:80:16], P(12), A.add),
+        lambda: ts(["rz4"], ["rz4"], T.rz4[:], T.rz4[:], 1.0, A.min),
+        lambda: E("v", V.quantize_mx, ["wb"], ["wc", "wz"], T.wc[:], T.wz[:], T.wb[:])]
 
-    if passes:
-        tot["rk"] = N - 1 - s
+    if NP:
+        tot["rk"] = higher
         wr["rk"] = [("rk", None)]
-        for h in passes:
-            a = first[h]
-            D("y", "dta" if h == 0 else "dtb", T["ti%d" % h][32 * a:128, :], T["kd%d" % h][a:4], ["rk"], ["ti%d" % h], True)
-        H = ["%d" % h for h in passes]
-        for h in H: copy(["ti" + h], ["ta" + h], T["ta" + h][:], T["ti" + h][:])
-        for h in H: tp(["ta" + h], ["bl" + h], T["bl" + h][:], T["ta" + h][:])
-        for h in H: ts(["xu", "bl" + h], ["cm" + h], T["cm" + h][:], T.xu[:], T["bl" + h][:, 0:1], A.is_ge)
-        for h in H: tp(["cm" + h], ["ct" + h], T["ct" + h][:], T["cm" + h][:])
-        for h in H: scan(["ct" + h, "rs32"], ["cs" + h], T["cs" + h][:], T.rs32[:], T["ct" + h][:], 0.0, A.mult, A.add)
-        for h in H: ts(["cs" + h], ["of" + h], T["of" + h][:], T["cs" + h][:, 31:512:32], 1.0, A.subtract, 0.0, A.max)
-        for i, h in enumerate(H):
-            tt(["ta" + h, "of" + h, "xg"], ["eq"], T.eq[:, 256 * i:256 * i + 256], T["ta" + h][:, 0:32].indirect(T["of" + h][:, 0:16]), T.xg[:], A.is_equal, add=True)
-        n = 256 * len(H)
+        for h, n in enumerate(lists):
+            D("y", "dpv", T.piv[0:32 * n, h:h + 1], T.kd[4 * h:4 * h + n, 0:4, :], ["rk", "piv"], ["pva"])
+        for h, n in enumerate(lists):
+            D("y", "dti", T.ti[0:32 * n, 32 * h:32 * h + 32], T.kd[4 * h:4 * h + n], ["rk", "ti"], ["tia"])
+    if sent:
+        g.sync.wait_ge(T.sem.lk, sent)
+    D("y", "dkc", T.kcs[:].bitcast(dt.uint8), T.kc[:], [], ["kcs"])
+    D("y", "dkc", T.kss[:], T.ks[:], [], ["kss"])
+    D("y", "dw", T.wb[:], T.w[:], [], ["wb"])
+    D("y", "dz", T.lc[:, 0:1].bitcast(dt.uint8), T.zc[:, 0:1].bitcast(dt.uint8), ["zc"], ["lcz"])
+    D("y", "dz", T.ls[:, 0:1], T.zs[:, 0:1], ["zs"], ["lsz"])
+    act(["wi"], ["w2"], T.w2[:], T.wi[:, 0:640], scale=0.0)
+    kb = T.ks4[:, nq - 1:17 * nq:nq]
+    kept = T.ks4[:, 2 * nq - 1:17 * nq:nq]
+    if NP:
+        n = 256 * NP
+        gap()
+        copy(["piv", "pva"], ["pvf"], T.pvf[:, 0:NP], T.piv[:, 0:NP])
+        for h in range(NP):
+            ts(["xu", "pvf", "ps8"], ["cm%d" % h], T["cm%d" % h][:], T.xu[:], T.pvf[:, h:h + 1], A.is_ge, P([3, 8][h]), A.mult)
+        for c in (0, 1):
+            for h in range(NP):
+                tp(["cm%d" % h], ["ct%d" % c], T["ct%d" % c][:, 256 * h:256 * h + 256], T["cm%d" % h][:, 256 * c:256 * c + 256], add=True)
+        for c in (0, 1):
+            scan(["ct%d" % c], ["cs%d" % c], T["cs%d" % c][:, 0:n // 2], T["ct%d" % c][:, 0:n:2], T["ct%d" % c][:, 1:n:2], 0.0, A.max, A.max)
+        for c in (0, 1):
+            copy(["cs%d" % c], ["of1"], T.of1[:, c:16 * NP:2], T["cs%d" % c][:, 15:n // 2:16], add=True)
+        gap()
+        tt(["ti", "tia", "of1", "xg"], ["eq"], T.eq[:, 0:n], T.ti[:, 0:32 * NP].indirect(T.of1[:, 0:16 * NP]), T.xg[:, 0:n], A.is_equal)
+        gap()
         tp(["eq"], ["et"], T.et[:, 0:n], T.eq[:, 0:n])
         gap()
-        scan(["et", "rs16"], ["es"], T.es[:, 0:n], T.rs16[:, 0:n], T.et[:, 0:n], 0.0, A.mult, A.add)
+        if NP == 2: w = 16; scan(["et"], ["es"], T.es[:, 1:257], T.et[:, 0:256], T.et[:, 256:512], 0.0, A.add, A.add)
+        else: w = 8; scan(["et"], ["es"], T.es[:, 1:129], T.et[:, 0:256:2], T.et[:, 1:256:2], 0.0, A.add, A.add)
+        if nq > 1: ts(["rk4"], ["rk4"], T.rk4[:, 0:16 * nq], T.rk4[:, 0:16 * nq], 0.0, A.max)
+        for a in range(nq):
+            out, tok = (T.c4[:, a:16 * nq:nq], "c4") if nq > 1 else (kept, "ks4")
+            tt(["es", "es0"], [tok], out, T.es[32 * a:32 * a + 32, w:16 * w + 1:w], T.es[32 * a:32 * a + 32, 0:16 * w:w], A.is_equal, add=nq > 1)
         gap()
-        if len(H) == 2: tt(["es"], ["s0"], T.s0[:], T.es[:, 15:256:16], T.es[:, 271:512:16], A.add)
-        else: copy(["es"], ["s0"], T.s0[:], T.es[:, 15:256:16])
-        gap()
-        quads = list(range(min(first.values()), 4))
-        nq = len(quads)
-        C4 = lambda i: T.c4[:, 16 * i:16 * i + 16]
-        for i, a in enumerate(quads):
-            at = [0, 2, 1, 3][i] if nq == 4 else i
-            if i < (nq + 1) // 2: copy(["s0"], ["c4"], C4(at), T.s0[32 * a:32 * a + 32, :], add=True)
-            else: ts(["s0"], ["c4"], C4(at), T.s0[32 * a:32 * a + 32, :], -1.0, A.mult, add=True)
-        gap()
-        if nq == 4:
-            tt(["c4"], ["a2"], T.a2[:], T.c4[:, 0:32], T.c4[:, 32:64], A.add)
+        if nq > 1:
+            scan(["c4", "rk4"], ["ks4"], T.ks4[:, nq:17 * nq], T.rk4[:, 0:16 * nq], T.c4[:, 0:16 * nq], 0.0, A.max, A.min)
             gap()
-            x, y, r = T.a2[:, 0:16], T.a2[:, 16:32], ["a2"]
-        elif nq == 3:
-            tt(["c4"], ["a2"], T.a2[:, 0:16], C4(0), C4(1), A.add)
-            gap()
-            x, y, r = T.a2[:, 0:16], C4(2), ["a2", "c4"]
-        else:
-            x, y, r = C4(0), C4(1), ["c4"]
-        if nq == 1:
-            ts(r, ["kb"], T.kb[:, 1:17], x, 0.0, A.is_equal)
-            ts(r, ["f1"], T.f1[:], x, 0.0, A.is_gt)
-        else:
-            tt(r, ["kb"], T.kb[:, 1:17], x, y, A.is_equal)
-            tt(r, ["f1"], T.f1[:], x, y, A.not_equal)
-    scan(["kb", "zz"], ["pl"], T.pl[:, 0:17], T.kb[:, 0:17], T.zz[:, 0:17], 0.0, A.add, A.add)
-    scan(["kb", "d96"], ["pl"], T.pl[:, 32:49], T.kb[:, 0:17], T.d96[:, 0:17], 0.0, A.add, A.max, add=True)
-    gap()
+    else:
+        gap(3)
+    scan(["ks4", "d96"], ["pl"], T.pl[:, 32:49], kb, T.d96[:, 0:17], 0.0, A.add, A.max)
+    E("v", V.tensor_reduce, ["ks4"], ["pl"], T.pl[:, 16:17], kb, AxisListType.X, A.add, add=True)
+    ts(["ks4"], ["f1"], T.f1[:], kept, -4096.0, A.mult)
     tp(["pl"], ["pt"], T.pt[:], T.pl[:])
-    if passes: tt(["f1", "tr"], ["nk"], T.nk[:], T.f1[:], T.tr[:], A.mult)
+    tt(["f1", "tr"], ["nk"], T.nk[:], T.f1[:], T.tr[:], A.add)
     scan(["pt"], ["cc"], T.cc[:, 1:33], T.pt[:, 0:32], T.pt[:, 32:64], 0.0, A.add, A.max)
     gap()
     tp(["cc"], ["cy"], T.cy[:], T.cc[:, 0:32])
     gap()
-    scan(["kb", "d96", "cy"], ["pq"], T.pq[:], T.kb[:, 0:16], T.d96[:, 0:16], T.cy[:, 16:17], A.add, A.max)
-    src, tok = T.pq, "pq"
+    scan(["ks4", "d96", "cy"], ["pq"], T.pq[:], T.ks4[:, nq - 1:16 * nq:nq], T.d96[:, 0:16], T.cy[:, 16:17], A.add, A.max)
     gap()
-    if passes:
-        tt(["pq", "nk"], ["pf"], T.pf[:], T.pq[:], T.nk[:], A.max)
-        src, tok = T.pf, "pf"
-        gap()
     for a in range(4):
-        copy([tok], ["pw"], T.pw[32 * a:32 * a + 32, :], src[:], add=True)
+        tt(["pq", "nk"], ["pw"], T.pw[32 * a:32 * a + 32, :], T.pq[:], T.nk[:], A.max, add=True)
     gap()
-    E("v", V.tensor_copy, ["pw", "val"], ["wi"], T.wi[:, 0:1040].indirect(T.pw[:, 0:16]), T.val[:])
+    E("v", V.tensor_copy, ["pw", "val", "w2"], ["wi"], T.wi[:, 0:1184].indirect(T.pw[:, 0:16]), T.val[:])
     gap()
-    tp(["wi"], ["wt"], T.wt[:], T.wi[:, 0:768])
+    tp(["wi"], ["wt"], T.wt[:], T.wi[:, 0:672])
     gap()
-    tt(["wt"], ["qk"], T.qk[:], T.wt[:, 1:768:32], T.wt[:, 17:768:32], A.max)
-    tt(["wt"], ["qi"], T.qi[:, 0:24], T.wt[:, 0:768:32], T.wt[:, 16:768:32], A.max)
+    tt(["wt"], ["qk"], T.qk[:, 0:21], T.wt[:, 1:672:32], T.wt[:, 17:672:32], A.max)
+    tt(["wt"], ["qi"], T.qi[:, 0:21], T.wt[:, 0:672:32], T.wt[:, 16:672:32], A.max)
     peers = [(s + i) % N for i in range(1, N)]
-    fused([(T.cores[d], T.kx[:, 3 * s:3 * s + 3], T.qk[:, 3 * d:3 * d + 3]) for d in peers], "rx", 2, ["qk"])
-    D("y", "dkx", T.kx[:, 3 * s:3 * s + 3], T.qk[:, 3 * s:3 * s + 3], ["qk"], ["kx"], "par")
+    keys = lambda d: (T.kx[:, 3 * slot(s, d):3 * slot(s, d) + 3], T.qk[:, (5 * d + odd) // 2:(5 * d + odd) // 2 + 3])
+    fused([(T.cores[d],) + keys(d) for d in peers], "rx", 2, ["qk"])
+    D("y", "dkx", *keys(s), ["qk"], ["kx"])
     gap()
     tp(["qi"], ["xt"], T.xt[:], T.qi[:])
     gap()
-    for k in range(4):
-        copy(["xt"], ["yy"], T.yy[:, 16 * k:16 * k + 16], T.xt[:, 16 * (k // 2):16 * (k // 2) + 16], add=True)
+    copy(["xt", "ody"], ["yy"], T.yy[:], T.xt[:, 0:32].indirect(T.ody[:, 0:4]))
     gap()
     tp(["yy"], ["ot"], T.ot[:], T.yy[:])
     gap()
-    if odd:
-        copy(["ot"], ["off"], T.off[:, 0:48:2], T.ot[:, 32:56])
-        copy(["ot"], ["off"], T.off[:, 1:47:2], T.ot[:, 1:24], add=True)
-    else:
-        copy(["ot"], ["off"], T.off[:, 0:48:2], T.ot[:, 0:24])
-        copy(["ot"], ["off"], T.off[:, 1:48:2], T.ot[:, 32:56], add=True)
-    def pick(d, cbuf, sbuf, c, tc, tz):
-        E("v", V.tensor_copy, ["off", "kcs"], [tc], cbuf[:, c:c + 80].bitcast(dt.uint32), T.kcs[:, 0:512].bitcast(dt.uint32).indirect(T.off[:, 6 * d:6 * d + 5]))
-        act(["off", "kss"], [tz], sbuf[:, c:c + 80], T.kss[:, 0:512].indirect(T.off[:, 6 * d:6 * d + 5]))
-    for d in peers: pick(d, T.qc, T.qs, 80 * d, "qc%d" % d, "qs%d" % d)
-    pick(s, T.lc, T.ls, 16 + 80 * s, "lco", "lso")
-    me = 16 + 80 * s
-    for part in (peers[:1], peers[1:3], peers[3:]):
+    copy(["ot", "oof"], ["off"], T.off[:], T.ot[:, 0:64].indirect(T.oof[:, 0:3]))
+    gap()
+    pairs = [(s // 2 + i) % 4 for i in (1, 2, 3, 4)]
+    for u in pairs:
+        E("v", V.tensor_copy, ["off", "kcs"], ["qc%d" % u], T.qc[:, 160 * u:160 * u + 160].bitcast(dt.uint32), T.kcs[:, 0:512].bitcast(dt.uint32).indirect(T.off[:, 10 * u:10 * u + 10]))
+        act(["off", "kss"], ["qs%d" % u], T.qs[:, 160 * u:160 * u + 160], T.kss[:, 0:512].indirect(T.off[:, 10 * u:10 * u + 10]))
+    codes_to = lambda d: (T.lc[:, 16 + 80 * slot(s, d):96 + 80 * slot(s, d)].bitcast(dt.uint8), T.qc[:, 80 * d:80 * d + 80].bitcast(dt.uint8))
+    scales_to = lambda d: (T.ls[:, 16 + 80 * slot(s, d):96 + 80 * slot(s, d)], T.qs[:, 80 * d:80 * d + 80])
+    for us in (pairs[:1], pairs[1:3], pairs[3:]):
+        part = [d for u in us for d in (2 * u, 2 * u + 1) if d != s]
         e = len(topo.engines(core, T.cores[part[0]])) // len(part)
-        fused([(T.cores[d], T.lc[:, me:me + 80].bitcast(dt.uint8), T.qc[:, 80 * d:80 * d + 80].bitcast(dt.uint8)) for d in part], "rc", e, ["qc%d" % d for d in part])
-        fused([(T.cores[d], T.ls[:, me:me + 80], T.qs[:, 80 * d:80 * d + 80]) for d in part], "rs", e, ["qs%d" % d for d in part])
-        for r in part:
-            tot["rc"] += e
-            tot["rs"] += e
+        fused([(T.cores[d],) + codes_to(d) for d in part], "rc", e, ["qc%d" % u for u in us])
+        fused([(T.cores[d],) + scales_to(d) for d in part], "rs", e, ["qs%d" % u for u in us])
+        tot["rc"] += e * len(part)
+        tot["rs"] += e * len(part)
+    D("y", "dlc", *codes_to(s), ["qc%d" % pairs[3]], ["lco"])
+    D("y", "dlc", *scales_to(s), ["qs%d" % pairs[3]], ["lso"])
     gap(len(later))
-    act(["ico", "ps17", "ps10"], ["ico2"], T.ico[:, 80:160], T.ico[:, 0:80], AF.Identity, scale=P(10), bias=P(17))
-    act(["irk1", "ps20", "ps13"], ["irk2"], T.irk[:, 160:240], T.irk[:, 80:160], AF.Identity, scale=P(13), bias=P(20))
-    E("v", V.quantize_mx, ["wb"], ["wc", "wz"], T.wc[:], T.wz[:], T.wb[:])
-    fill(["zb"], T.zb[:], 0.0)
-    tt(["ico2", "irk2"], ["cst"], T.cst[:], T.ico[:, 80:160], T.irk[:, 160:240], A.add)
-    E("v", V.quantize_mx, ["zb"], ["zc", "zs"], T.zc[:], T.zs[:], T.zb[:])
-    D("y", "dz", T.lc[:, 0:1].bitcast(dt.uint8), T.zc[:, 0:1].bitcast(dt.uint8), ["zc"], ["lcz"], "par")
-    D("y", "dz", T.ls[:, 0:1], T.zs[:, 0:1], ["zs"], ["lsz"], "par")
+    act(["ic", "ps13"], ["cst"], T.cst[:], T.ic[:], AF.Identity, bias=P(13))
     tot["rx"] = 2 * (N - 1)
     wr["rx"] = [("rx", None)]
+    xf = T.xk[:, 16:656]
     act(["rx", "kx", "mo"], ["mmS"], T.mm[:, 256:640], T.kx[:, 0:24].indirect(T.mo[:, 16:40]))
-    copy(["rx", "kx", "ox6"], ["x6"], T.x6[:], T.kx[:, 0:24].indirect(T.ox6[:, 0:1]))
     copy(["rx", "kx", "mo"], ["mmV"], T.mm[:, 0:256], T.kx[:, 0:24].indirect(T.mo[:, 0:16]))
-    ts(["x6"], ["nx6"], T.nx6[:], T.x6[:], -1.0, A.mult)
-    ts(["x6"], ["pd"], T.pd[:], T.x6[:, 0:5], -65536.0, A.is_lt)
-    tp(["mmV"], ["xfV"], T.xf[:, 0:256], T.mm[:, 0:256])
-    tp(["mmS"], ["xfS"], T.xf[:, 256:640], T.mm[:, 256:640])
-    xf = ["xfV", "xfS"]
-    tt(["pd", "jf", "jf2"], ["jt0"], T.jt[:, 5:10], T.pd[:], T.jf[:], A.mult)
-    def count(e):
-        act(xf + ["nx6"], ["jk%d" % e, "sm%d" % e], T.jk[:, 640 * e:640 * e + 640], T.xf[:], AF.Sign, bias=T.nx6[:, e:e + 1], accum_out=T.sm[:, e:e + 1])
-    count(0)
-    act(xf + ["okg", "ps12"], ["kg"], T.kg[:], T.xf[:, 0:640].indirect(T.okg[:, 0:5]), scale=P(12))
-    count(1)
-    count(2)
+    ts(["rx", "kx", "ox6"], ["nx6"], T.nx6[:], T.kx[:, 0:24].indirect(T.ox6[:, 0:1]), -1.0, A.mult)
+    tp(["mmV"], ["xfV"], T.xk[:, 16:272], T.mm[:, 0:256])
+    tp(["mmS"], ["xfS"], T.xk[:, 272:656], T.mm[:, 256:640])
+    xs = ["xfV", "xfS"]
+    for e in range(3):
+        act(xs + ["nx6"], ["jk%d" % e, "sm%d" % e], T.jk[:, 640 * e:640 * e + 640], xf, AF.Sign, bias=T.nx6[:, e:e + 1], accum_out=T.sm[:, e:e + 1])
+    ts(xs + ["okg"], ["kg"], T.kg[:], xf.indirect(T.okg[:, 0:5]), -65536.0, A.is_gt, 1024.0, A.mult)
     for k in (0, 1):
-        ts(xf + ["x6"], ["cb%d" % k], T.cb[:, 640 * k:640 * k + 640], T.xf[:], T.x6[:, 3 + k:4 + k], A.is_gt)
-    for k in (0, 1):
-        scan(["cb%d" % k, "rs160"], ["cbs%d" % k], T.cbs[:, 640 * k:640 * k + 640], T.rs160[:], T.cb[:, 640 * k:640 * k + 640], 0.0, A.mult, A.add)
-    tt(["kg", "cst"], ["va2"], T.va2[:], T.kg[:], T.cst[:], A.add)
-    ts(["jt0"], ["jt"], T.jt[:, 0:5], T.jt[:, 5:10], 10000.0, A.subtract)
-    for k in (0, 1):
-        E("v", V.tensor_reduce, ["cbs%d" % k], ["sm%d" % (3 + k)], T.sm[:, 3 + k:4 + k], T.cbs[:, 640 * k + 159:640 * k + 640:160], AxisListType.X, A.add)
-    tt(["sm%d" % e for e in range(5)] + ["jt"], ["pm"], T.pm[:], T.sm[:], T.jt[:, 0:5], A.max)
-    ts(["pm"], ["pu"], T.pu[:, 0:3], T.pm[:, 0:3], 639.0, A.add, 0.5, A.mult)
-    copy(["pm"], ["pu"], T.pu[:, 3:5], T.pm[:, 3:5], add=True)
-    E("v", V.tensor_copy, ["pu", "va2"], ["w2"], T.w2[:, 0:960].indirect(T.pu[:, 0:5]), T.va2[:])
-    tp(["w2"], ["w2t"], T.w2t[:], T.w2[:, 0:512])
-    def ok_rows():
-        tp(["k2"], ["ro"], T.ro[:], T.k2[:])
-        D("y", "dok", T.ok[0:1, :], T.ro[0:16, 0:32], ["ro"], ["ok"], "par")
-        D("y", "dok", T.ok[1:2, :], T.ro[16:32, 0:32], ["ro"], ["ok"], "par")
-    later += [lambda k=k: tt(["w2t"], ["t3k"], T.t3[:, 16 * k:16 * k + 16], T.w2t[:, k:512:32], T.w2t[:, 16 + k:512:32], A.add, add=True) for k in (1, 2)]
-    later += [lambda a=a: copy(["t3k"], ["c6"], T.c6[:, 32 * a:32 * a + 32], T.t3[32 * a:32 * a + 32, 16:48], add=True) for a in range(4)]
-    later += [
-        lambda: tt(["c6"], ["a6"], T.a6[:], T.c6[:, 0:64], T.c6[:, 64:128], A.add),
-        lambda: tt(["a6"], ["c6b"], T.c6[:, 0:32], T.a6[:, 0:32], T.a6[:, 32:64], A.add),
-        lambda: ts(["c6b"], ["k2"], T.k2[:], T.c6[:, 0:32], 1.0, A.subtract),
-        ok_rows]
-    for a in range(4):
-        tt(["w2t"], ["c5"], T.c5[:, 16 * a:16 * a + 16], T.w2t[32 * a:32 * a + 32, 0:512:32], T.w2t[32 * a:32 * a + 32, 16:512:32], A.add, add=True)
-    gap(2)
-    tt(["c5"], ["a5"], T.a5[:], T.c5[:, 0:32], T.c5[:, 32:64], A.add)
-    gap()
-    for a in range(4):
-        tt(["a5"], ["sr"], T.sr[32 * a:32 * a + 32, 0:16], T.a5[:, 0:16], T.a5[:, 16:32], A.add, add=a > 0)
-    gap()
-    tp(["sr"], ["sx"], T.sx[:], T.sr[:])
-    gap()
+        ts(xs + ["nx6"], ["cb%d" % k], T.cb[:, 640 * k:640 * k + 640], xf, T.nx6[:, 3 + k:4 + k], A.add, 0.0, A.is_gt)
+        if k == 0: tt(["kg", "cst"], ["va2"], T.va2[:], T.kg[:], T.cst[:], A.min)
     for k in range(4):
-        copy(["sx"], ["sy"], T.sy[:, 16 * k:16 * k + 16], T.sx[:, 16 * (k // 2):16 * (k // 2) + 16], add=True)
-    gap()
+        scan(["cb%d" % (k // 2)], ["cbs%d" % k], T.cbs[:, 160 * k:160 * k + 160], T.cb[:, 320 * k:320 * k + 160], T.cb[:, 320 * k + 160:320 * k + 320], -160.0, A.add, A.add)
+    for k in (0, 1):
+        ts(["cbs%d" % (2 * k), "cbs%d" % (2 * k + 1)], ["pu"], T.pu[:, 3 + k:4 + k], T.cbs[:, 320 * k + 159:320 * k + 160], T.cbs[:, 320 * k + 319:320 * k + 320], A.add, 320.0, A.add, add=True)
+    ts(["sm0", "sm1", "sm2"], ["pu"], T.pu[:, 0:3], T.sm[:, 0:3], 639.0, A.add, 0.5, A.mult, add=True)
+    iota(xs, T.xk[32:64, 16:656], [[-2, 4], [1, 2], [0, 80]] if odd else [[-1, 8], [0, 80]], -odd)
+    E("v", V.tensor_copy, ["pu", "va2"], ["w2"], T.w2[:, 0:640].indirect(T.pu[:, 0:5]), T.va2[:])
+    tp(["w2"], ["w2t"], T.w2t[:], T.w2[:, 0:512])
+    for a in range(4):
+        tt(["w2t"], ["c5"], T.c5[:, a:64:4], T.w2t[32 * a:32 * a + 32, 0:512:32], T.w2t[32 * a:32 * a + 32, 16:512:32], A.add, add=True)
+    scan(["c5", "rz4"], ["cz"], T.cz[:, 0:64], T.rz4[:], T.c5[:], 0.0, A.mult, A.add)
+    for a in range(4):
+        tp(["cz"], ["sx"], T.sx[32 * a:32 * a + 32, :], T.cz[:, 3:128:4], add=True)
+    copy(["sx", "ody"], ["sy"], T.sy[:], T.sx[:, 0:32].indirect(T.ody[:, 0:4]))
     tp(["sy"], ["so"], T.so[:], T.sy[:])
-    gap()
-    copy(["so"], ["of2"], T.of2[:, 0:32:2], T.so[:, 0:16])
-    copy(["so"], ["of2"], T.of2[:, 1:32:2], T.so[:, 32:48], add=True)
+    copy(["so", "oo2"], ["of2"], T.of2[:], T.so[:, 0:64].indirect(T.oo2[:, 0:2]))
     wr["lca"], wr["lsa"] = [("rc", None)], [("rs", None)]
     land, lands = ["lca", "lco", "lcz"], ["lsa", "lso", "lsz"]
     for k in (0, 1):
@@ -380,22 +331,18 @@ def rank_program(g, core, T, topo):
         E("t", g.tensor.matmul_mx, land + lands + ["wc", "wz"], ["acc%d" % k], T.acc[:, 512 * k:512 * k + 320], T.wc[:], T.wz[:], T.lc[:, c:c + 320], T.ls[:, c:c + 320], True, True)
     for k in (0, 1):
         act(["acc%d" % k], ["yf%d" % k], T.yf[:, 16 + 320 * k:336 + 320 * k], T.acc[:, 512 * k:512 * k + 320])
-    ys = ["yfz", "yf0", "yf1", "of2"]
-    def codes(k):
-        E("v", V.tensor_copy, land + ["of2"], ["fc%d" % k], T.fc[:, 256 * k:256 * k + 256].bitcast(dt.uint32), T.lc[:, 0:656].bitcast(dt.uint32).indirect(T.of2[:, 16 * k:16 * k + 16]))
-        D("y", ["doc", "doc2"][k], T.oc[:, 1024 * k:1024 * k + 1024], T.fc[:, 256 * k:256 * k + 256].bitcast(dt.uint8), ["fc%d" % k], ["oc"], "par")
-    codes(0)
-    act(ys, ["yo0"], T.yo[:, 0:256], T.yf[:, 0:656].indirect(T.of2[:, 0:16]))
-    D("y", "dy", T.y[:, 0:256], T.yo[:, 0:256], ["yo0"], ["y"], "par")
-    codes(1)
+    for k, (a, b) in enumerate(CHUNKS):
+        o = T.of2[:, a // 16:b // 16]
+        E("v", V.tensor_copy, land + ["of2"], ["fc%d" % k], T.fc[:, a:b].bitcast(dt.uint32), T.lc[:, 0:656].bitcast(dt.uint32).indirect(o))
+        act(["yfz", "yf0", "yf1", "of2"], ["yo%d" % k], T.yo[:, a:b], T.yf[:, 0:656].indirect(o))
+        D("y", "doc%d" % k, T.oc[:, 4 * a:4 * b], T.fc[:, a:b].bitcast(dt.uint8), ["fc%d" % k], ["oc"])
+        D("y", "dy%d" % k, T.y[:, a:b], T.yo[:, a:b], ["yo%d" % k], ["y"])
     act(lands + ["of2"], ["fz"], T.fz[:], T.ls[:, 0:656].indirect(T.of2[:, 0:32]))
     for k in range(4):
-        D("s", "dos", T.osc[4 * k:4 * k + 4, :], T.fz[32 * k:32 * k + 4, :], ["fz"], ["osc"], "par")
+        D("s", "dos", T.osc[4 * k:4 * k + 4, :], T.fz[32 * k:32 * k + 4, :], ["fz"], ["osc"])
+    ts(xs + ["xk0", "of2"], ["ko"], T.ko[:], T.xk[:, 0:656].indirect(T.of2[:, 0:32]), -1.0, A.mult)
     for k in (0, 1):
-        c = 256 + 128 * k
-        copy(ys, ["yo%d" % (1 + k)], T.yo[:, c:c + 128], T.yf[:, 0:656].indirect(T.of2[:, 16 + 8 * k:24 + 8 * k]))
-        D("y", ["dy2", "dy3"][k], T.y[:, c:c + 128], T.yo[:, c:c + 128], ["yo%d" % (1 + k)], ["y"], "par")
-    gap(len(later))
+        D("y", "dok", T.ok[k:k + 1, :], T.ko[32 * k:32 * k + 1, :], ["ko"], ["ok"])
     for n in SEMAPHORES:
         if tot[n]:
             g.wait_ge(T.sem[n], tot[n])

@@ -3,20 +3,21 @@ from concourse.mybir import dt, AluOpType, AxisListType, ActivationFunctionType
 
 SCRATCH = {"mykd": ("dram", [128, 8], "int32"), "kd": ("dram", [7, 128, 8], "int32"), "acc": ("psum", [128, 1024], "float32")}
 SIZES = {
-    (128, "float32"): "ldf:32 zt:48 m0:512 xb:512 xg:512 mv:256 val:256 pvf:2 ps:32 ix:96 im:80 mh:40 ic:80 cst:80 i8:8 wi:1184 wt:672 qk:24 qi:32 "
-                      "xt:32 yy:64 ot:64 kx:24 mm:640 xk:656 nx6:16 sm:4 kg:80 va2:80 w2:640 w2t:512 sx:32 sy:64 so:64 yf:656 yo:512 ko:512",
-    (32, "float32"): "spn:16 spb:16 tr:16 d7:112 d7s:112 rs7:112 d96:20 c4:64 rk4:64 rz4:64 ks4:68 f1:16 nk:16 pl:64 pt:64 cc:64 cy:32 pq:16 c5:64 cz:128",
-    (128, "bfloat16"): "cm0:512 cm1:512 ct0:512 ct1:512 cs0:256 cs1:256 eq:512 et:512 es:272 zb:512 wb:512 jk:1920 cb:1280 cbs:640",
+    (128, "float32"): "ldf:32 zt:48 m0:512 xb:512 xg:256 mv:128 val:128 ps:32 ix:96 im:80 mh:40 ic:80 cst:80 i8:8 wi:1184 wt:672 hk:64 qk:24 qi:32 "
+                      "spb:16 xt:32 yy:64 ot:64 kx:24 xk:656 v6:16 pd:16 jf:8 jt:4 sm:4 w2:1664 w2t:512 sx:32 sy:64 so:64 yf:656 yo:512 ko:512",
+    (32, "float32"): "spn:16 tr:16 d7:112 d7s:112 rs7:112 d96:20 c4:64 rk4:64 rz4:64 ks4:68 f1:16 nk:16 pl:64 pt:64 cc:64 cy:32 pq:16 c5:64 cz:128",
+    (128, "bfloat16"): "pvh:6 v6b:16 cm:1024 ct:1024 eq:512 et:512 es:272 zb:512 wb:512 jk:1280 cb:1920",
+    (128, "float16"): "cs:544 cbs:960",
     (128, "int32"): "ti:64 piv:2 pi:8", (32, "int32"): "ld:32 spr:16",
-    (128, "uint16"): "xu:512 of1:32 mb:32 mo:40 oxg:32 omv:16 okg:6 ox6:2 ody:4 oof:4 oo2:2 pw:16 off:48 pu:6 of2:32",
+    (128, "uint16"): "xu:512 of1:32 mb:32 mo:40 oxg:16 omv:8 ox6:2 ody:4 oof:4 oo2:2 pw:8 off:48 pu:6 of2:32 mm:640 xf:640",
     (128, "float8_e4m3fn_x4"): "zc:128 kcs:512 qc:640 lc:656 fc:512 wc:128",
     (128, "uint8"): "zs:128 kss:512 qs:640 ls:672 fz:512 wz:128"}
 for (_p, _d), _l in SIZES.items():
     for _x in _l.split():
         SCRATCH[_x.split(":")[0]] = ("sbuf", [_p, int(_x.split(":")[1])], _d)
-SEMAPHORES = ["vs", "ss", "ts", "gs", "dk", "dt", "dsp", "dw", "dkc", "dz", "dpv", "dti", "dkx", "dlc", "doc0", "doc1", "dos", "dy0", "dy1", "dok",
+SEMAPHORES = ["vs", "ss", "ts", "gs", "dk", "dt", "dsp", "dw", "dkc", "dz", "dpv", "dti", "dkx", "dlc", "doc0", "doc1", "doc2", "dos", "dy0", "dy1", "dy2", "dok",
               "rk", "rx", "rc", "rs", "loc", "lk"]
-CHUNKS = ((0, 128), (128, 512))
+CHUNKS = ((0, 96), (96, 256), (256, 512))
 
 
 def rank_program(g, core, T, topo):
@@ -110,9 +111,9 @@ def rank_program(g, core, T, topo):
     D("s", "dsp", T.spr[0:1, :], T.sp[:], [], ["spr"])
 
     iota(["pi"], T.pi[:, 0:1], [[0, 1]], 0, 1)
-    iota(["imb"], T.ix[:, 0:32], [[1, 16], [0, 2]], 0)
-    iota(["ixg"], T.ix[:, 32:64], [[0, 2], [32, 8], [256, 2]], 0)
-    iota(["imv"], T.ix[:, 64:80], [[1, 8], [8, 2]], 0)
+    iota(["imb"], T.ix[:, 0:32], [[1, 8], [8, 2], [0, 2]], 0)
+    iota(["ixg"], T.ix[:, 32:48], [[32, 16]], 0)
+    iota(["imv"], T.ix[:, 64:72], [[1, 4], [8, 2]], 0)
     iota(["idz"], T.ix[:, 80:96], [[-256, 2], [-2, 8]], 0)
     if s > 0:
         fused([(T.cores[r], T.kd[s - r - 1], T.mykd[:]) for r in range(s)], "rk", 1, ["mykd"], "lk")
@@ -125,11 +126,12 @@ def rank_program(g, core, T, topo):
     copy(["pi%d" % k for k in range(6)], ["ps"], T.ps[:, 0:6], T.pi[:, 1:7])
     P = lambda k: T.ps[:, k:k + 1]
     copy(["imb"], ["mb"], T.mb[:], T.ix[:, 0:32])
-    ts(["ps"], ["ps6"], P(6), P(0), 0.0, A.is_equal, 32.0, A.mult)
+    ts(["ps"], ["ps6"], P(14), P(0), 0.0, A.is_equal, 32.0, A.mult)
+    ts(["ps"], ["ps6"], P(6), P(2), 2.0, A.is_ge, 4.0, A.mult, add=True)
     ts(["ps"], ["ps7"], P(7), P(0), -16.0, A.mult, P(1), A.subtract)
-    ts(["ps"], ["ps8"], P(8), P(3), 32.0, A.add)
-    ts(["ixg", "ps"], ["oxg"], T.oxg[:], T.ix[:, 32:64], P(3), A.add)
-    ts(["imv", "ps6"], ["omv"], T.omv[:], T.ix[:, 64:80], P(6), A.add)
+    ts(["ps"], ["ps8"], T.pvh[:, 4:5], P(3), 0.0, A.is_equal, 131072.0, A.mult)
+    ts(["ixg", "ps"], ["oxg"], T.oxg[:], T.ix[:, 32:48], P(3), A.add)
+    ts(["imv", "ps6", "ps"], ["omv"], T.omv[:], T.ix[:, 64:72], P(14), A.add, P(6), A.add)
     ts(["idz", "ps7"], ["ztc"], T.zt[:, 32:48], T.ix[:, 80:96], P(7), A.add)
     for a in range(4):
         copy(["ld"], ["ldf"], T.ldf[32 * a:32 * a + 32, :], T.ld[:], add=True)
@@ -150,12 +152,13 @@ def rank_program(g, core, T, topo):
                 fill(["piv"], T.piv[32 * a:32 * a + 32, h:h + 1], 65536, add=True)
                 fill(["ti"], T.ti[32 * a:32 * a + 32, 32 * h:32 * h + 32], -1, add=True)
         fill(["es0"], T.es[:, 0:1], 0.0)
-    act(["zt", "ztc", "omv"], ["mv"], T.mv[:], T.zt[:, 0:48].indirect(T.omv[:, 0:16]), scale=-1.0)
+        fill(["es0"], T.cs[:, 0:273:272], 0.0, add=True)
+    act(["zt", "ztc", "omv"], ["mv"], T.mv[:], T.zt[:, 0:48].indirect(T.omv[:, 0:8]), scale=-1.0)
     if NP:
-        act(xb + ["oxg"], ["xg"], T.xg[:, 0:256 * NP], T.xb[:, 0:512].indirect(T.oxg[:, 0:16 * NP]))
-    E("g", g.partition_broadcast, ["spn"], ["spb"], T.spb[:], T.spn[0:1, :], 32)
+        act(xb + ["oxg"], ["xg"], T.xg[:], T.xb[:, 0:512].indirect(T.oxg[:, 0:16]))
+    E("g", g.partition_broadcast, ["spn"], ["spb"], T.spb[:], T.spn[0:1, :], 128)
     for e in range(N - 1):
-        E("s", S.activation, ["zt", "spb"], ["d7"], T.d7[:, e:112:7], T.zt[0:32, 16:32], AF.Sign, bias=T.spb[:, e:e + 1], add=True)
+        E("s", S.activation, ["zt", "spb"], ["d7"], T.d7[:, e:112:7], T.zt[0:32, 16:32], AF.Sign, bias=T.spb[0:32, e:e + 1], add=True)
     iota(["ks4"], T.ks4[:], [[0, 68]], 0)
     if not NP:
         iota(["ks4"], T.ks4[:, 1:17], [[0, 16]], 1)
@@ -171,28 +174,35 @@ def rank_program(g, core, T, topo):
     iota(["im2"], T.im[:, 40:80], [[0, 4], [1, 5], [0, 2]], 0)
     iota(["im"], T.im[:, 0:40], [[6, 4], [1, 5], [0, 2]], 0)
     iota(["ic"], T.ic[:], [[32, 5], [1, 16]], 0)
+    iota(["jf"], T.jf[:, 0:5], [[128, 5]], 512, 1)
+    iota(["xkk"], T.xk[:, 16:656], [[-2, 4], [1, 2], [0, 80]] if odd else [[-1, 8], [0, 80]], -odd)
     iota(["xk0"], T.xk[:, 0:16], [[0, 16]], 1)
     iota(["yfz"], T.yf[:, 0:16], [[0, 16]], 0)
     iota(["rz4"], T.rz4[:], [[0, 16], [1, 4]], 0)
     iota(["cz"], T.cz[:], [[0, 128]], 0)
 
+    tp(["mv"], ["val"], T.val[:], T.mv[:])
+    ts(["ps"], ["ps10"], P(10), P(4), 32.0, A.mult, P(5), A.add)
+    ts(["ps"], ["ps11"], P(11), P(4), -31.0, A.mult, P(5), A.add)
+    ts(["ps"], ["ps18"], P(18), P(0), P(1), A.add, 3.0, A.is_ge)
+    ts(["ps"], ["ps9"], P(9), P(2), 6.0, A.mult, P(0), A.add)
+    ts(["ps"], ["ps12"], P(12), P(2), 160.0, A.mult, P(3), A.add)
+    ts(["ps9", "ps18"], ["ox6"], T.ox6[:, 0:1], P(9), P(18), A.add, 23.0, A.min)
+    ts(["ps12"], ["ps13"], P(13), P(12), P(0), A.subtract, 16.0, A.add)
+    def phi(k, sign, half):
+        if s < N - 1: ts(["spb"], ["phi"], P(k), T.spb[:, s:s + 1], -sign, A.mult, 0.5 * sign + half, A.add, add=True)
+        else: fill(["phi"], P(k), 65536.0 * sign + half, add=True)
     later += [
-        lambda: tp(["mv"], ["val"], T.val[:], T.mv[:]),
         lambda: scan(["d7", "rs7"], ["d7s"], T.d7s[:], T.rs7[:], T.d7[:], 0.0, A.mult, A.add),
         lambda: ts(["d7s"], ["d96"], T.d96[:, 0:16], T.d7s[:, 6:112:7], 40.0, A.mult, 280.0 + 16 * odd, A.add),
-        lambda: ts(["ps"], ["ps10"], P(10), P(4), 32.0, A.mult, P(5), A.add),
-        lambda: ts(["ps"], ["ps11"], P(11), P(4), -31.0, A.mult, P(5), A.add),
         lambda: ts(["i8", "ps"], ["ody"], T.ody[:], T.i8[:, 0:4], P(0), A.add),
         lambda: ts(["i8b", "ps10", "ps11"], ["oof"], T.oof[:], T.i8[:, 4:8], P(10 + odd), A.add, 32.0 * odd, A.add),
         lambda: ts(["im2", "ps"], ["mh"], T.mh[:], T.im[:, 40:80], P(1), A.add, 3.0, A.is_ge),
-        lambda: ts(["ps"], ["ps18"], P(18), P(0), P(1), A.add, 3.0, A.is_ge),
-        lambda: ts(["ps"], ["ps9"], P(9), P(2), 6.0, A.mult, P(0), A.add),
+        lambda: phi(20, 1.0, 0.0),
         lambda: tt(["im", "mh"], ["mo"], T.mo[:], T.im[:, 0:40], T.mh[:], A.add),
-        lambda: ts(["ps9", "ps18"], ["ox6"], T.ox6[:, 0:1], P(9), P(18), A.add, 23.0, A.min),
-        lambda: ts(["ps"], ["ps12"], P(12), P(2), 160.0, A.mult, P(3), A.add),
+        lambda: phi(21, 1.0, 0.5),
         lambda: ts(["i8b", "ps10"], ["oo2"], T.oo2[:], T.i8[:, 4:6], P(10), A.add),
-        lambda: ts(["ps12"], ["ps13"], P(13), P(12), P(0), A.subtract, 16.0, A.add),
-        lambda: ts(["ic", "ps12"], ["okg"], T.okg[:, 0:5], T.ic[:, 0:80:16], P(12), A.add),
+        lambda: phi(22, -1.0, 0.0),
         lambda: ts(["rz4"], ["rz4"], T.rz4[:], T.rz4[:], 1.0, A.min),
         lambda: E("v", V.quantize_mx, ["wb"], ["wc", "wz"], T.wc[:], T.wz[:], T.wb[:])]
 
@@ -210,24 +220,28 @@ def rank_program(g, core, T, topo):
     D("y", "dw", T.wb[:], T.w[:], [], ["wb"])
     D("y", "dz", T.lc[:, 0:1].bitcast(dt.uint8), T.zc[:, 0:1].bitcast(dt.uint8), ["zc"], ["lcz"])
     D("y", "dz", T.ls[:, 0:1], T.zs[:, 0:1], ["zs"], ["lsz"])
-    act(["wi"], ["w2"], T.w2[:], T.wi[:, 0:640], scale=0.0)
+    act(["wi"], ["w2"], T.w2[:, 0:512], T.wi[:, 0:512], scale=0.0)
+    act(["ic", "ps13"], ["cst"], T.cst[:], T.ic[:], AF.Identity, bias=P(13))
     kb = T.ks4[:, nq - 1:17 * nq:nq]
     kept = T.ks4[:, 2 * nq - 1:17 * nq:nq]
     if NP:
         n = 256 * NP
-        gap()
-        copy(["piv", "pva"], ["pvf"], T.pvf[:, 0:NP], T.piv[:, 0:NP])
+        copy(["piv", "pva"], ["pvh"], T.pvh[:, 0:NP], T.piv[:, 0:NP])
         for h in range(NP):
-            ts(["xu", "pvf", "ps8"], ["cm%d" % h], T["cm%d" % h][:], T.xu[:], T.pvf[:, h:h + 1], A.is_ge, P([3, 8][h]), A.mult)
-        for c in (0, 1):
-            for h in range(NP):
-                tp(["cm%d" % h], ["ct%d" % c], T["ct%d" % c][:, 256 * h:256 * h + 256], T["cm%d" % h][:, 256 * c:256 * c + 256], add=True)
-        for c in (0, 1):
-            scan(["ct%d" % c], ["cs%d" % c], T["cs%d" % c][:, 0:n // 2], T["ct%d" % c][:, 0:n:2], T["ct%d" % c][:, 1:n:2], 0.0, A.max, A.max)
-        for c in (0, 1):
-            copy(["cs%d" % c], ["of1"], T.of1[:, c:16 * NP:2], T["cs%d" % c][:, 15:n // 2:16], add=True)
-        gap()
-        tt(["ti", "tia", "of1", "xg"], ["eq"], T.eq[:, 0:n], T.ti[:, 0:32 * NP].indirect(T.of1[:, 0:16 * NP]), T.xg[:, 0:n], A.is_equal)
+            ts(["pvh", "ps8"], ["pvl%d" % h], T.pvh[:, 2 + h:3 + h], T.piv[:, h:h + 1], T.pvh[:, h:h + 1], A.subtract, T.pvh[:, 4:5], A.add)
+        for h in range(NP):
+            ts(["xu", "pvl%d" % h], ["cm%d" % h], T.cm[:, 512 * h:512 * h + 512], T.xu[:], T.pvh[:, h:h + 1], A.subtract, T.pvh[:, 2 + h:3 + h], A.is_ge)
+        for h in range(NP):
+            tp(["cm%d" % h], ["ct%d" % h], T.ct[:, 512 * h:512 * h + 512], T.cm[:, 512 * h:512 * h + 512])
+        for h in range(NP):
+            c = 272 * h
+            scan(["ct%d" % h], ["cs%d" % h], T.cs[:, c + 1:c + 257], T.ct[:, 512 * h:512 * h + 512:2], T.ct[:, 512 * h + 1:512 * h + 512:2], 0.0, A.add, A.add)
+        for h in range(NP):
+            c = 272 * h
+            tt(["cs%d" % h, "es0"], ["of%d" % h], T.of1[:, 16 * h:16 * h + 16], T.cs[:, c + 16:c + 257:16], T.cs[:, c:c + 256:16], A.subtract)
+        if NP == 1: gap()
+        for h in range(NP):
+            tt(["ti", "tia", "of%d" % h, "xg"], ["eq"], T.eq[:, 256 * h:256 * h + 256], T.ti[:, 32 * h:32 * h + 32].indirect(T.of1[:, 16 * h:16 * h + 16]), T.xg[:], A.is_equal, add=True)
         gap()
         tp(["eq"], ["et"], T.et[:, 0:n], T.eq[:, 0:n])
         gap()
@@ -255,14 +269,19 @@ def rank_program(g, core, T, topo):
     scan(["ks4", "d96", "cy"], ["pq"], T.pq[:], T.ks4[:, nq - 1:16 * nq:nq], T.d96[:, 0:16], T.cy[:, 16:17], A.add, A.max)
     gap()
     for a in range(4):
-        tt(["pq", "nk"], ["pw"], T.pw[32 * a:32 * a + 32, :], T.pq[:], T.nk[:], A.max, add=True)
+        c = 8 * (a // 2)
+        tt(["pq", "nk"], ["pw"], T.pw[32 * a:32 * a + 32, :], T.pq[:, c:c + 8], T.nk[:, c:c + 8], A.max, add=True)
     gap()
-    E("v", V.tensor_copy, ["pw", "val", "w2"], ["wi"], T.wi[:, 0:1184].indirect(T.pw[:, 0:16]), T.val[:])
+    E("v", V.tensor_copy, ["pw", "val", "w2"], ["wi"], T.wi[:, 0:1184].indirect(T.pw[:, 0:8]), T.val[:])
     gap()
     tp(["wi"], ["wt"], T.wt[:], T.wi[:, 0:672])
     gap()
-    tt(["wt"], ["qk"], T.qk[:, 0:21], T.wt[:, 1:672:32], T.wt[:, 17:672:32], A.max)
-    tt(["wt"], ["qi"], T.qi[:, 0:21], T.wt[:, 0:672:32], T.wt[:, 16:672:32], A.max)
+    tt(["wt"], ["hk"], T.hk[:, 0:21], T.wt[:, 1:672:32], T.wt[:, 17:672:32], A.max)
+    tt(["wt"], ["hi"], T.hk[:, 32:53], T.wt[:, 0:672:32], T.wt[:, 16:672:32], A.max)
+    for k in (0, 1):
+        tt(["hk"], ["qk"], T.qk[64 * k:64 * k + 64, 0:21], T.hk[0:64, 0:21], T.hk[64:128, 0:21], A.max, add=True)
+    for k in (0, 1):
+        tt(["hi"], ["qi"], T.qi[64 * k:64 * k + 64, 0:21], T.hk[0:64, 32:53], T.hk[64:128, 32:53], A.max, add=k > 0)
     peers = [(s + i) % N for i in range(1, N)]
     keys = lambda d: (T.kx[:, 3 * slot(s, d):3 * slot(s, d) + 3], T.qk[:, (5 * d + odd) // 2:(5 * d + odd) // 2 + 3])
     fused([(T.cores[d],) + keys(d) for d in peers], "rx", 2, ["qk"])
@@ -292,29 +311,31 @@ def rank_program(g, core, T, topo):
     D("y", "dlc", *codes_to(s), ["qc%d" % pairs[3]], ["lco"])
     D("y", "dlc", *scales_to(s), ["qs%d" % pairs[3]], ["lso"])
     gap(len(later))
-    act(["ic", "ps13"], ["cst"], T.cst[:], T.ic[:], AF.Identity, bias=P(13))
     tot["rx"] = 2 * (N - 1)
     wr["rx"] = [("rx", None)]
-    xf = T.xk[:, 16:656]
-    act(["rx", "kx", "mo"], ["mmS"], T.mm[:, 256:640], T.kx[:, 0:24].indirect(T.mo[:, 16:40]))
-    copy(["rx", "kx", "mo"], ["mmV"], T.mm[:, 0:256], T.kx[:, 0:24].indirect(T.mo[:, 0:16]))
-    ts(["rx", "kx", "ox6"], ["nx6"], T.nx6[:], T.kx[:, 0:24].indirect(T.ox6[:, 0:1]), -1.0, A.mult)
-    tp(["mmV"], ["xfV"], T.xk[:, 16:272], T.mm[:, 0:256])
-    tp(["mmS"], ["xfS"], T.xk[:, 272:656], T.mm[:, 256:640])
+    kxr = ["rx", "kx", "mo", "ox6", "phi"]
+    act(kxr, ["mmS"], T.mm[:, 192:640], T.kx[:, 0:24].indirect(T.mo[:, 12:40]), AF.Identity, bias=P(20))
+    ts(kxr, ["mmV"], T.mm[:, 0:192], T.kx[:, 0:24].indirect(T.mo[:, 0:12]), P(20), A.add)
+    ts(kxr, ["v6"], T.v6[:], T.kx[:, 0:24].indirect(T.ox6[:, 0:1]), P(21), A.add, 0.5, A.max)
+    tp(["mmV"], ["xfV"], T.xf[:, 0:192], T.mm[:, 0:192])
+    copy(["v6"], ["v6h"], T.v6b[:, 0:3], T.v6[:, 2:5])
+    ts(["v6"], ["pd"], T.pd[:, 0:5], T.v6[:, 0:5], 1.0, A.is_lt)
+    tt(["v6", "v6h"], ["v6l"], T.v6b[:, 8:11], T.v6[:, 2:5], T.v6b[:, 0:3], A.subtract)
+    tp(["mmS"], ["xfS"], T.xf[:, 192:640], T.mm[:, 192:640])
+    tt(["pd", "jf"], ["pd2"], T.pd[:, 8:13], T.pd[:, 0:5], T.jf[:, 0:5], A.mult)
     xs = ["xfV", "xfS"]
-    for e in range(3):
-        act(xs + ["nx6"], ["jk%d" % e, "sm%d" % e], T.jk[:, 640 * e:640 * e + 640], xf, AF.Sign, bias=T.nx6[:, e:e + 1], accum_out=T.sm[:, e:e + 1])
-    ts(xs + ["okg"], ["kg"], T.kg[:], xf.indirect(T.okg[:, 0:5]), -65536.0, A.is_gt, 1024.0, A.mult)
-    for k in (0, 1):
-        ts(xs + ["nx6"], ["cb%d" % k], T.cb[:, 640 * k:640 * k + 640], xf, T.nx6[:, 3 + k:4 + k], A.add, 0.0, A.is_gt)
-        if k == 0: tt(["kg", "cst"], ["va2"], T.va2[:], T.kg[:], T.cst[:], A.min)
-    for k in range(4):
-        scan(["cb%d" % (k // 2)], ["cbs%d" % k], T.cbs[:, 160 * k:160 * k + 160], T.cb[:, 320 * k:320 * k + 160], T.cb[:, 320 * k + 160:320 * k + 320], -160.0, A.add, A.add)
-    for k in (0, 1):
-        ts(["cbs%d" % (2 * k), "cbs%d" % (2 * k + 1)], ["pu"], T.pu[:, 3 + k:4 + k], T.cbs[:, 320 * k + 159:320 * k + 160], T.cbs[:, 320 * k + 319:320 * k + 320], A.add, 320.0, A.add, add=True)
-    ts(["sm0", "sm1", "sm2"], ["pu"], T.pu[:, 0:3], T.sm[:, 0:3], 639.0, A.add, 0.5, A.mult, add=True)
-    iota(xs, T.xk[32:64, 16:656], [[-2, 4], [1, 2], [0, 80]] if odd else [[-1, 8], [0, 80]], -odd)
-    E("v", V.tensor_copy, ["pu", "va2"], ["w2"], T.w2[:, 0:640].indirect(T.pu[:, 0:5]), T.va2[:])
+    for e in range(2):
+        act(xs + ["v6"], ["jk%d" % e, "sm%d" % e], T.jk[:, 640 * e:640 * e + 640], T.xf[:], AF.Sign, scale=-1.0, bias=T.v6[:, e:e + 1], accum_out=T.sm[:, e:e + 1])
+    act(xs + ["phi"], ["xkk"], T.xk[0:32, 16:656], T.xf[0:32, :], AF.Identity, bias=T.ps[0:32, 22:23])
+    for k in range(3):
+        ts(xs + ["v6l"], ["cb%d" % k], T.cb[:, 640 * k:640 * k + 640], T.xf[:], T.v6b[:, k:k + 1], A.subtract, T.v6b[:, 8 + k:9 + k], A.is_gt)
+    ts(["pd2"], ["jt"], T.jt[:, 0:2], T.pd[:, 8:10], 320.0, A.add)
+    for k in range(3):
+        scan(["cb%d" % k], ["cbs"], T.cbs[:, 320 * k:320 * k + 320], T.cb[:, 640 * k:640 * k + 320], T.cb[:, 640 * k + 320:640 * k + 640], 0.0, A.add, A.add, add=True)
+    for e in range(2):
+        ts(["sm%d" % e, "jt"], ["pu"], T.pu[:, e:e + 1], T.sm[:, e:e + 1], -0.5, A.mult, T.jt[:, e:e + 1], A.add, add=True)
+    tt(["cbs", "pd2"], ["pu"], T.pu[:, 2:5], T.cbs[:, 319:960:320], T.pd[:, 10:13], A.add, add=True)
+    E("v", V.tensor_copy, ["pu", "cst"], ["w2"], T.w2[:, 0:1664].indirect(T.pu[:, 0:5]), T.cst[:])
     tp(["w2"], ["w2t"], T.w2t[:], T.w2[:, 0:512])
     for a in range(4):
         tt(["w2t"], ["c5"], T.c5[:, a:64:4], T.w2t[32 * a:32 * a + 32, 0:512:32], T.w2t[32 * a:32 * a + 32, 16:512:32], A.add, add=True)
@@ -338,11 +359,10 @@ def rank_program(g, core, T, topo):
         D("y", "doc%d" % k, T.oc[:, 4 * a:4 * b], T.fc[:, a:b].bitcast(dt.uint8), ["fc%d" % k], ["oc"])
         D("y", "dy%d" % k, T.y[:, a:b], T.yo[:, a:b], ["yo%d" % k], ["y"])
     act(lands + ["of2"], ["fz"], T.fz[:], T.ls[:, 0:656].indirect(T.of2[:, 0:32]))
+    ts(["xkk", "xk0", "of2"], ["ko"], T.ko[:], T.xk[:, 0:656].indirect(T.of2[:, 0:32]), -1.0, A.mult)
+    D("y", "dok", T.ok[:], T.ko[0:64:32, :], ["ko"], ["ok"])
     for k in range(4):
         D("s", "dos", T.osc[4 * k:4 * k + 4, :], T.fz[32 * k:32 * k + 4, :], ["fz"], ["osc"])
-    ts(xs + ["xk0", "of2"], ["ko"], T.ko[:], T.xk[:, 0:656].indirect(T.of2[:, 0:32]), -1.0, A.mult)
-    for k in (0, 1):
-        D("y", "dok", T.ok[k:k + 1, :], T.ko[32 * k:32 * k + 1, :], ["ko"], ["ok"])
     for n in SEMAPHORES:
         if tot[n]:
             g.wait_ge(T.sem[n], tot[n])

@@ -3,21 +3,21 @@ from concourse.mybir import dt, AluOpType, AxisListType, ActivationFunctionType
 
 SCRATCH = {"mykd": ("dram", [128, 8], "int32"), "kd": ("dram", [7, 128, 8], "int32"), "acc": ("psum", [128, 1024], "float32")}
 SIZES = {
-    (128, "float32"): "ldf:32 zt:48 m0:512 xb:512 xg:256 mv:128 val:128 ps:32 ix:96 im:80 mh:40 ic:80 cst:80 i8:8 wi:1184 wt:672 hk:64 qk:24 qi:32 "
-                      "spb:16 xt:32 yy:64 ot:64 kx:24 xk:656 v6:16 pd:16 jf:8 jt:4 sm:4 w2:1664 w2t:512 sx:32 sy:64 so:64 yf:656 yo:512 ko:512",
-    (32, "float32"): "spn:16 tr:16 d7:112 d7s:112 rs7:112 d96:20 c4:64 rk4:64 rz4:64 ks4:68 f1:16 nk:16 pl:64 pt:64 cc:64 cy:32 pq:16 c5:64 cz:128",
-    (128, "bfloat16"): "pvh:6 v6b:16 cm:1024 ct:1024 eq:512 et:512 es:272 zb:512 wb:512 jk:1280 cb:1920",
+    (128, "float32"): "mv:128 val:128 ps:32 ix:96 im:80 mh:40 ic:80 i8:8 wi:1184 wt:672 hk:64 qk:24 qi:32 "
+                      "spb:16 xt:32 yy:64 ot:64 kx:24 xk:656 v6:16 pd:16 jf:8 jt:4 sm:4 sx:32 sy:64 so:64 yf:656 yo:512 ko:512",
+    (32, "float32"): "spn:16 tr:16 d7:112 d7s:112 rs7:112 d96:20 c4:64 rk4:64 ks4:68 f1:16 nk:16 pl:64 pt:64 cc:64 cy:32 pq:16 rz4:128 c5:128 cz:256",
+    (128, "bfloat16"): "pvh:6 pva:16 pvs:16 v6b:16 cm:1024 ct:1024 eq:512 et:512 es:272 zb:512 wb:512 jk:1280 cb:1920 w2:1664 w2t:512 cst:80",
     (128, "float16"): "cs:544 cbs:960",
-    (128, "int32"): "ti:64 piv:2 pi:8", (32, "int32"): "ld:32 spr:16",
-    (128, "uint16"): "xu:512 of1:32 mb:32 mo:40 oxg:16 omv:8 ox6:2 ody:4 oof:4 oo2:2 pw:8 off:48 pu:6 of2:32 mm:640 xf:640",
+    (128, "int32"): "ti:64 pi:8 zt:48", (32, "int32"): "ld:32 spr:16",
+    (128, "uint16"): "opv:2 m0:512 xu:512 mg:256 xg:256 of1:32 mb:32 mo:40 omg:16 omv:8 ox6:2 ody:4 oof:4 oo2:2 pw:8 off:48 pu:6 of2:32 mm:640 xf:640",
     (128, "float8_e4m3fn_x4"): "zc:128 kcs:512 qc:640 lc:656 fc:512 wc:128",
     (128, "uint8"): "zs:128 kss:512 qs:640 ls:672 fz:512 wz:128"}
 for (_p, _d), _l in SIZES.items():
     for _x in _l.split():
         SCRATCH[_x.split(":")[0]] = ("sbuf", [_p, int(_x.split(":")[1])], _d)
-SEMAPHORES = ["vs", "ss", "ts", "gs", "dk", "dt", "dsp", "dw", "dkc", "dz", "dpv", "dti", "dkx", "dlc", "doc0", "doc1", "doc2", "dos", "dy0", "dy1", "dy2", "dok",
+SEMAPHORES = ["vs", "ss", "ts", "gs", "dk", "dt", "dsp", "dw", "dkc", "dz", "rp", "dti", "dkx", "dlc", "doc0", "doc1", "doc2", "dos", "dy0", "dy1", "dy2", "dok",
               "rk", "rx", "rc", "rs", "loc", "lk"]
-CHUNKS = ((0, 96), (96, 256), (256, 512))
+CHUNKS = ((0, 96), (96, 352), (352, 512))
 
 
 def rank_program(g, core, T, topo):
@@ -74,7 +74,8 @@ def rank_program(g, core, T, topo):
     def tp(r, w, out, in_, add=False): E("v", V.transpose, r, w, out, in_, add=add)
     def scan(r, w, out, a, b, init, o0, o1, add=False): E("v", V.tensor_tensor_scan, r, w, out, a, b, init, o0, o1, add=add)
     def fill(w, ap, c, add=False): E("v", V.memset, [], w, ap, c, add=add)
-    def act(r, w, out, in_, fn=AF.Copy, **kw): E("s", S.activation, r, w, out, in_, fn, **kw)
+    def act(r, w, out, in_, fn=AF.Copy, add=False, **kw): E("s", S.activation, r, w, out, in_, fn, add=add, **kw)
+    def lin(r, w, out, in_, scale, bias, add=False): act(r, w, out, in_, AF.Identity, add, scale=scale, bias=bias)
     def iota(w, ap, pat, base, mult=0):
         E("g", g.iota, [], w, ap, pat, base, mult, allow_small_or_imprecise_dtypes=True)
 
@@ -101,6 +102,7 @@ def rank_program(g, core, T, topo):
     nq = lists[0] if lists else 1
     odd = s % 2
     slot = lambda src, dst: src ^ (dst % 2)
+    P = lambda k: T.ps[:, k:k + 1]
 
     if s > 0:
         for k in (0, 1):
@@ -112,53 +114,58 @@ def rank_program(g, core, T, topo):
 
     iota(["pi"], T.pi[:, 0:1], [[0, 1]], 0, 1)
     iota(["imb"], T.ix[:, 0:32], [[1, 8], [8, 2], [0, 2]], 0)
-    iota(["ixg"], T.ix[:, 32:48], [[32, 16]], 0)
+    iota(["img"], T.ix[:, 32:48], [[1, 16]], 16)
     iota(["imv"], T.ix[:, 64:72], [[1, 4], [8, 2]], 0)
     iota(["idz"], T.ix[:, 80:96], [[-256, 2], [-2, 8]], 0)
     if s > 0:
         fused([(T.cores[r], T.kd[s - r - 1], T.mykd[:]) for r in range(s)], "rk", 1, ["mykd"], "lk")
-    sent = tot["lk"]
 
-    fill(["zb"], T.zb[:], 0.0)
-    for k, (sh, m) in enumerate(((0, 15), (4, 1), (5, 3), (0, 31), (0, 1), (1, 7))):
-        ts(["pi"], ["pi%d" % k], T.pi[:, 1 + k:2 + k], T.pi[:, 0:1], sh, A.logical_shift_right, m, A.bitwise_and)
-    E("v", V.quantize_mx, ["zb"], ["zc", "zs"], T.zc[:], T.zs[:], T.zb[:])
-    copy(["pi%d" % k for k in range(6)], ["ps"], T.ps[:, 0:6], T.pi[:, 1:7])
-    P = lambda k: T.ps[:, k:k + 1]
-    copy(["imb"], ["mb"], T.mb[:], T.ix[:, 0:32])
-    ts(["ps"], ["ps6"], P(14), P(0), 0.0, A.is_equal, 32.0, A.mult)
-    ts(["ps"], ["ps6"], P(6), P(2), 2.0, A.is_ge, 4.0, A.mult, add=True)
-    ts(["ps"], ["ps7"], P(7), P(0), -16.0, A.mult, P(1), A.subtract)
-    ts(["ps"], ["ps8"], T.pvh[:, 4:5], P(3), 0.0, A.is_equal, 131072.0, A.mult)
-    ts(["ixg", "ps"], ["oxg"], T.oxg[:], T.ix[:, 32:48], P(3), A.add)
-    ts(["imv", "ps6", "ps"], ["omv"], T.omv[:], T.ix[:, 64:72], P(14), A.add, P(6), A.add)
-    ts(["idz", "ps7"], ["ztc"], T.zt[:, 32:48], T.ix[:, 80:96], P(7), A.add)
-    for a in range(4):
-        copy(["ld"], ["ldf"], T.ldf[32 * a:32 * a + 32, :], T.ld[:], add=True)
-    ts(["spr"], ["spn"], T.spn[0:1, :], T.spr[0:1, :], -1.0, A.mult, 0.5, A.add)
-    tp(["ldf"], ["zt"], T.zt[:, 0:32], T.ldf[:])
+    for h, n in enumerate(lists):
+        for a in range(n, 4):
+            fill(["ti"], T.ti[32 * a:32 * a + 32, 32 * h:32 * h + 32], -1, add=True)
     fill(["rs7"], T.rs7[:], 1.0)
-    act(["zt", "mb"], ["m0b"], T.m0[:, 256:512], T.zt[:, 0:32].indirect(T.mb[:, 16:32]))
-    copy(["zt", "mb"], ["m0a"], T.m0[:, 0:256], T.zt[:, 0:32].indirect(T.mb[:, 0:16]))
+    for k, (sh, m) in enumerate(((0, 15), (4, 1), (5, 3), (0, 31), (0, 1), (1, 7), (1, 1))):
+        ts(["pi"], ["pi%d" % k], T.pi[:, 1 + k:2 + k], T.pi[:, 0:1], sh, A.logical_shift_right, m, A.bitwise_and)
     fill(["rs7"], T.rs7[:, 0:112:7], 0.0)
-    tp(["m0a"], ["xba"], T.xb[:, 0:256], T.m0[:, 0:256])
-    tp(["m0b"], ["xbb"], T.xb[:, 256:512], T.m0[:, 256:512])
-    xb = ["xba", "xbb"]
+    fill(["es0"], T.es[:, 0:1], 0.0)
+    copy(["pi%d" % k for k in range(7)], ["ps"], T.ps[:, 0:7], T.pi[:, 1:8])
+    fill(["es0"], T.cs[:, 0:273:272], 0.0, add=True)
+    fill(["zb"], T.zb[:], 0.0)
+    act(["imb"], ["mb"], T.mb[:], T.ix[:, 0:32])
+    act(["img"], ["omg"], T.omg[:], T.ix[:, 32:48])
+    ts(["ps"], ["ps8"], T.pvh[:, 4:5], P(3), 0.0, A.is_equal, 131072.0, A.mult)
+    ts(["ps"], ["ps14"], P(14), P(0), 0.0, A.is_equal, 32.0, A.mult)
+    ts(["ps"], ["ps15"], P(15), P(2), 2.0, A.is_ge, 4.0, A.mult)
+    ts(["ps"], ["ps7"], P(7), P(0), -16.0, A.mult, P(1), A.subtract)
     if NP:
-        copy(["xba"], ["xu"], T.xu[:, 0:256], T.xb[:, 0:256], add=True)
-        copy(["xbb"], ["xu"], T.xu[:, 256:512], T.xb[:, 256:512], add=True)
-        for h, n in enumerate(lists):
-            for a in range(n, 4):
-                fill(["piv"], T.piv[32 * a:32 * a + 32, h:h + 1], 65536, add=True)
-                fill(["ti"], T.ti[32 * a:32 * a + 32, 32 * h:32 * h + 32], -1, add=True)
-        fill(["es0"], T.es[:, 0:1], 0.0)
-        fill(["es0"], T.cs[:, 0:273:272], 0.0, add=True)
+        ts(["ps"], ["ps16"], P(16), P(2), lists[0] - 1.0, A.min, 4.0, A.mult)
+        ts(["ps"], ["ps17"], P(17), P(2), float(sum(lists[1:])), A.is_lt, P(6), A.mult)
+    ts(["imv", "ps14", "ps15"], ["omv"], T.omv[:], T.ix[:, 64:72], P(14), A.add, P(15), A.add)
+    ts(["idz", "ps7"], ["ztc"], T.zt[:, 32:48], T.ix[:, 80:96], P(7), A.add)
+    if NP:
+        lin(["ps16"], ["ps19"], P(19), P(4), 1.0, P(16))
+        lin(["ps17", "ps19"], ["opv"], T.opv[:, 0:1], P(17), 2.0, P(19))
+    for a in range(4):
+        tp(["ld"], ["zt"], T.zt[32 * a:32 * a + 32, 0:32], T.ld[:], add=True)
+    ts(["spr"], ["spn"], T.spn[0:1, :], T.spr[0:1, :], -1.0, A.mult, 0.5, A.add)
+    if NP:
+        act(["zt", "mb"], ["m0b"], T.m0[:, 256:512], T.zt[:, 0:32].indirect(T.mb[:, 16:32]))
+    if s > 0:
+        copy(["zt"], ["pvh"], T.pvh[:, 0:1], T.zt[:, 16:17])
+        ts(["pvh", "ps8"], ["pvl"], T.pvh[:, 1:2], T.zt[:, 16:17], T.pvh[:, 0:1], A.subtract, T.pvh[:, 4:5], A.add)
+        at = lambda i: 4 * (i % 4) + 2 * (i // 4)
+        fused([(T.cores[r], T.pva[:, at(s - r - 1):at(s - r - 1) + 2], T.pvh[:, 0:2]) for r in range(s)], "rp", 2, ["pvl"], "lk")
+    sent = tot["lk"]
+    if NP:
+        copy(["zt", "mb"], ["m0a"], T.m0[:, 0:256], T.zt[:, 0:32].indirect(T.mb[:, 0:16]))
+        act(["zt", "omg"], ["mg"], T.mg[:], T.zt[:, 0:32].indirect(T.omg[:, 0:16]))
+        tp(["m0b"], ["xu"], T.xu[:, 256:512], T.m0[:, 256:512], add=True)
+        tp(["m0a"], ["xu"], T.xu[:, 0:256], T.m0[:, 0:256], add=True)
+        tp(["mg"], ["xg"], T.xg[:], T.mg[:])
     act(["zt", "ztc", "omv"], ["mv"], T.mv[:], T.zt[:, 0:48].indirect(T.omv[:, 0:8]), scale=-1.0)
-    if NP:
-        act(xb + ["oxg"], ["xg"], T.xg[:], T.xb[:, 0:512].indirect(T.oxg[:, 0:16]))
     E("g", g.partition_broadcast, ["spn"], ["spb"], T.spb[:], T.spn[0:1, :], 128)
     for e in range(N - 1):
-        E("s", S.activation, ["zt", "spb"], ["d7"], T.d7[:, e:112:7], T.zt[0:32, 16:32], AF.Sign, bias=T.spb[0:32, e:e + 1], add=True)
+        act(["zt", "spb"], ["d7"], T.d7[:, e:112:7], T.zt[0:32, 16:32], AF.Sign, True, bias=T.spb[0:32, e:e + 1])
     iota(["ks4"], T.ks4[:], [[0, 68]], 0)
     if not NP:
         iota(["ks4"], T.ks4[:, 1:17], [[0, 16]], 1)
@@ -169,48 +176,63 @@ def rank_program(g, core, T, topo):
     iota(["tr"], T.tr[:], [[1, 16]], 672, 16)
     iota(["wi"], T.wi[:, 0:672], [[-1, 672]], -(66000 + 672 * s))
     iota(["qi"], T.qi[:], [[0, 32]], 0)
-    iota(["i8"], T.i8[:, 0:4], [[0, 2], [16, 2]][::-1], 0)
+    iota(["i8"], T.i8[:, 0:4], [[16, 2], [0, 2]], 0)
     iota(["i8b"], T.i8[:, 4:8], [[8, 4]], 0)
     iota(["im2"], T.im[:, 40:80], [[0, 4], [1, 5], [0, 2]], 0)
     iota(["im"], T.im[:, 0:40], [[6, 4], [1, 5], [0, 2]], 0)
     iota(["ic"], T.ic[:], [[32, 5], [1, 16]], 0)
     iota(["jf"], T.jf[:, 0:5], [[128, 5]], 512, 1)
-    iota(["xkk"], T.xk[:, 16:656], [[-2, 4], [1, 2], [0, 80]] if odd else [[-1, 8], [0, 80]], -odd)
+    iota(["rz4"], T.rz4[:], [[0, 16], [1, 8]], 0)
+    iota(["cz"], T.cz[:, 135:256:8], [[0, 16]], 0)
     iota(["xk0"], T.xk[:, 0:16], [[0, 16]], 1)
     iota(["yfz"], T.yf[:, 0:16], [[0, 16]], 0)
-    iota(["rz4"], T.rz4[:], [[0, 16], [1, 4]], 0)
-    iota(["cz"], T.cz[:], [[0, 128]], 0)
+    iota(["xkk"], T.xk[:, 16:656], [[-2, 4], [1, 2], [0, 80]] if odd else [[-1, 8], [0, 80]], -odd)
 
-    tp(["mv"], ["val"], T.val[:], T.mv[:])
-    ts(["ps"], ["ps10"], P(10), P(4), 32.0, A.mult, P(5), A.add)
-    ts(["ps"], ["ps11"], P(11), P(4), -31.0, A.mult, P(5), A.add)
-    ts(["ps"], ["ps18"], P(18), P(0), P(1), A.add, 3.0, A.is_ge)
-    ts(["ps"], ["ps9"], P(9), P(2), 6.0, A.mult, P(0), A.add)
-    ts(["ps"], ["ps12"], P(12), P(2), 160.0, A.mult, P(3), A.add)
-    ts(["ps9", "ps18"], ["ox6"], T.ox6[:, 0:1], P(9), P(18), A.add, 23.0, A.min)
-    ts(["ps12"], ["ps13"], P(13), P(12), P(0), A.subtract, 16.0, A.add)
-    def phi(k, sign, half):
-        if s < N - 1: ts(["spb"], ["phi"], P(k), T.spb[:, s:s + 1], -sign, A.mult, 0.5 * sign + half, A.add, add=True)
-        else: fill(["phi"], P(k), 65536.0 * sign + half, add=True)
+    lin(["ps"], ["ps9"], P(9), P(2), 6.0, P(0))
+    lin(["ps"], ["ps10"], P(10), P(4), 32.0, P(5))
+    lin(["ps"], ["ps11"], P(11), P(4), -31.0, P(5))
+    lin(["ps"], ["ps12"], P(12), P(1), 16.0, 16.0)
+    lin(["ps14"], ["ps24"], P(24), P(14), 1.0 / 32, 0.0)
+    for k, sign, half in ((20, 1.0, 0.0), (21, 1.0, 0.5), (22, -1.0, 0.0)):
+        if s < N - 1: lin(["spb"], ["phi"], P(k), T.spb[:, s:s + 1], -sign, 0.5 * sign + half, True)
+        else: lin(["ps"], ["phi"], P(k), P(0), 0.0, 65536.0 * sign + half, True)
+    lin(["ps12"], ["ps13"], P(13), P(2), 160.0, P(12))
+    if nq > 1:
+        act(["rk4"], ["rk4"], T.rk4[:, 0:16 * nq], T.rk4[:, 0:16 * nq], AF.Relu)
+
+    def first_slots():
+        scan(["d7", "rs7"], ["d7s"], T.d7s[:], T.rs7[:], T.d7[:], 0.0, A.mult, A.add)
+        lin(["d7s"], ["d96"], T.d96[:, 0:16], T.d7s[:, 6:112:7], 40.0, 280.0 + 16 * odd)
+        act(["wi"], ["w2"], T.w2[:, 0:512], T.wi[:, 0:512], scale=0.0)
+        lin(["i8", "ps"], ["ody"], T.ody[:], T.i8[:, 0:4], 1.0, P(0))
+        lin(["i8b", "ps10"], ["oo2"], T.oo2[:], T.i8[:, 4:6], 1.0, P(10))
+        lin(["ps11"], ["ps23"], P(23), P(10 + odd), 1.0, 32.0 * odd)
+        lin(["i8b", "ps23"], ["oof"], T.oof[:], T.i8[:, 4:8], 1.0, P(23))
+        act(["rz4"], ["rz4"], T.rz4[:], T.rz4[:], AF.Sign)
+
+    def zeros():
+        E("v", V.quantize_mx, ["zb"], ["zc", "zs"], T.zc[:], T.zs[:], T.zb[:])
+        D("y", "dz", T.lc[:, 0:1].bitcast(dt.uint8), T.zc[:, 0:1].bitcast(dt.uint8), ["zc"], ["lcz"])
+        D("y", "dz", T.ls[:, 0:1], T.zs[:, 0:1], ["zs"], ["lsz"])
+
+    def columns():
+        ts(["ps13"], ["ps25"], P(25), P(0), 8.0, A.is_equal, P(13), A.mult)
+        lin(["ic", "ps24", "ps25"], ["cst"], T.cst[:], T.ic[:], P(24), P(25))
+
     later += [
-        lambda: scan(["d7", "rs7"], ["d7s"], T.d7s[:], T.rs7[:], T.d7[:], 0.0, A.mult, A.add),
-        lambda: ts(["d7s"], ["d96"], T.d96[:, 0:16], T.d7s[:, 6:112:7], 40.0, A.mult, 280.0 + 16 * odd, A.add),
-        lambda: ts(["i8", "ps"], ["ody"], T.ody[:], T.i8[:, 0:4], P(0), A.add),
-        lambda: ts(["i8b", "ps10", "ps11"], ["oof"], T.oof[:], T.i8[:, 4:8], P(10 + odd), A.add, 32.0 * odd, A.add),
+        first_slots,
+        lambda: tp(["mv"], ["val"], T.val[:], T.mv[:]),
+        zeros,
+        columns,
+        lambda: ts(["ps"], ["ps18"], P(18), P(0), P(1), A.add, 3.0, A.is_ge),
         lambda: ts(["im2", "ps"], ["mh"], T.mh[:], T.im[:, 40:80], P(1), A.add, 3.0, A.is_ge),
-        lambda: phi(20, 1.0, 0.0),
+        lambda: ts(["ps9", "ps18"], ["ox6"], T.ox6[:, 0:1], P(9), P(18), A.add, 23.0, A.min),
         lambda: tt(["im", "mh"], ["mo"], T.mo[:], T.im[:, 0:40], T.mh[:], A.add),
-        lambda: phi(21, 1.0, 0.5),
-        lambda: ts(["i8b", "ps10"], ["oo2"], T.oo2[:], T.i8[:, 4:6], P(10), A.add),
-        lambda: phi(22, -1.0, 0.0),
-        lambda: ts(["rz4"], ["rz4"], T.rz4[:], T.rz4[:], 1.0, A.min),
         lambda: E("v", V.quantize_mx, ["wb"], ["wc", "wz"], T.wc[:], T.wz[:], T.wb[:])]
 
     if NP:
         tot["rk"] = higher
         wr["rk"] = [("rk", None)]
-        for h, n in enumerate(lists):
-            D("y", "dpv", T.piv[0:32 * n, h:h + 1], T.kd[4 * h:4 * h + n, 0:4, :], ["rk", "piv"], ["pva"])
         for h, n in enumerate(lists):
             D("y", "dti", T.ti[0:32 * n, 32 * h:32 * h + 32], T.kd[4 * h:4 * h + n], ["rk", "ti"], ["tia"])
     if sent:
@@ -218,19 +240,16 @@ def rank_program(g, core, T, topo):
     D("y", "dkc", T.kcs[:].bitcast(dt.uint8), T.kc[:], [], ["kcs"])
     D("y", "dkc", T.kss[:], T.ks[:], [], ["kss"])
     D("y", "dw", T.wb[:], T.w[:], [], ["wb"])
-    D("y", "dz", T.lc[:, 0:1].bitcast(dt.uint8), T.zc[:, 0:1].bitcast(dt.uint8), ["zc"], ["lcz"])
-    D("y", "dz", T.ls[:, 0:1], T.zs[:, 0:1], ["zs"], ["lsz"])
-    act(["wi"], ["w2"], T.w2[:, 0:512], T.wi[:, 0:512], scale=0.0)
-    act(["ic", "ps13"], ["cst"], T.cst[:], T.ic[:], AF.Identity, bias=P(13))
     kb = T.ks4[:, nq - 1:17 * nq:nq]
     kept = T.ks4[:, 2 * nq - 1:17 * nq:nq]
     if NP:
         n = 256 * NP
-        copy(["piv", "pva"], ["pvh"], T.pvh[:, 0:NP], T.piv[:, 0:NP])
+        tot["rp"] = 2 * higher
+        wr["rp"] = [("rp", None)]
+        copy(["rp", "opv"], ["pvs"], T.pvs[:], T.pva[:, 0:16].indirect(T.opv[:, 0:1]))
+        gap()
         for h in range(NP):
-            ts(["pvh", "ps8"], ["pvl%d" % h], T.pvh[:, 2 + h:3 + h], T.piv[:, h:h + 1], T.pvh[:, h:h + 1], A.subtract, T.pvh[:, 4:5], A.add)
-        for h in range(NP):
-            ts(["xu", "pvl%d" % h], ["cm%d" % h], T.cm[:, 512 * h:512 * h + 512], T.xu[:], T.pvh[:, h:h + 1], A.subtract, T.pvh[:, 2 + h:3 + h], A.is_ge)
+            ts(["xu", "pvs"], ["cm%d" % h], T.cm[:, 512 * h:512 * h + 512], T.xu[:], T.pvs[:, 2 * h:2 * h + 1], A.subtract, T.pvs[:, 2 * h + 1:2 * h + 2], A.is_ge)
         for h in range(NP):
             tp(["cm%d" % h], ["ct%d" % h], T.ct[:, 512 * h:512 * h + 512], T.cm[:, 512 * h:512 * h + 512])
         for h in range(NP):
@@ -239,7 +258,6 @@ def rank_program(g, core, T, topo):
         for h in range(NP):
             c = 272 * h
             tt(["cs%d" % h, "es0"], ["of%d" % h], T.of1[:, 16 * h:16 * h + 16], T.cs[:, c + 16:c + 257:16], T.cs[:, c:c + 256:16], A.subtract)
-        if NP == 1: gap()
         for h in range(NP):
             tt(["ti", "tia", "of%d" % h, "xg"], ["eq"], T.eq[:, 256 * h:256 * h + 256], T.ti[:, 32 * h:32 * h + 32].indirect(T.of1[:, 16 * h:16 * h + 16]), T.xg[:], A.is_equal, add=True)
         gap()
@@ -247,7 +265,7 @@ def rank_program(g, core, T, topo):
         gap()
         if NP == 2: w = 16; scan(["et"], ["es"], T.es[:, 1:257], T.et[:, 0:256], T.et[:, 256:512], 0.0, A.add, A.add)
         else: w = 8; scan(["et"], ["es"], T.es[:, 1:129], T.et[:, 0:256:2], T.et[:, 1:256:2], 0.0, A.add, A.add)
-        if nq > 1: ts(["rk4"], ["rk4"], T.rk4[:, 0:16 * nq], T.rk4[:, 0:16 * nq], 0.0, A.max)
+        gap()
         for a in range(nq):
             out, tok = (T.c4[:, a:16 * nq:nq], "c4") if nq > 1 else (kept, "ks4")
             tt(["es", "es0"], [tok], out, T.es[32 * a:32 * a + 32, w:16 * w + 1:w], T.es[32 * a:32 * a + 32, 0:16 * w:w], A.is_equal, add=nq > 1)
@@ -271,11 +289,8 @@ def rank_program(g, core, T, topo):
     for a in range(4):
         c = 8 * (a // 2)
         tt(["pq", "nk"], ["pw"], T.pw[32 * a:32 * a + 32, :], T.pq[:, c:c + 8], T.nk[:, c:c + 8], A.max, add=True)
-    gap()
     E("v", V.tensor_copy, ["pw", "val", "w2"], ["wi"], T.wi[:, 0:1184].indirect(T.pw[:, 0:8]), T.val[:])
-    gap()
     tp(["wi"], ["wt"], T.wt[:], T.wi[:, 0:672])
-    gap()
     tt(["wt"], ["hk"], T.hk[:, 0:21], T.wt[:, 1:672:32], T.wt[:, 17:672:32], A.max)
     tt(["wt"], ["hi"], T.hk[:, 32:53], T.wt[:, 0:672:32], T.wt[:, 16:672:32], A.max)
     for k in (0, 1):
@@ -286,7 +301,6 @@ def rank_program(g, core, T, topo):
     keys = lambda d: (T.kx[:, 3 * slot(s, d):3 * slot(s, d) + 3], T.qk[:, (5 * d + odd) // 2:(5 * d + odd) // 2 + 3])
     fused([(T.cores[d],) + keys(d) for d in peers], "rx", 2, ["qk"])
     D("y", "dkx", *keys(s), ["qk"], ["kx"])
-    gap()
     tp(["qi"], ["xt"], T.xt[:], T.qi[:])
     gap()
     copy(["xt", "ody"], ["yy"], T.yy[:], T.xt[:, 0:32].indirect(T.ody[:, 0:4]))
@@ -295,21 +309,21 @@ def rank_program(g, core, T, topo):
     gap()
     copy(["ot", "oof"], ["off"], T.off[:], T.ot[:, 0:64].indirect(T.oof[:, 0:3]))
     gap()
-    pairs = [(s // 2 + i) % 4 for i in (1, 2, 3, 4)]
-    for u in pairs:
-        E("v", V.tensor_copy, ["off", "kcs"], ["qc%d" % u], T.qc[:, 160 * u:160 * u + 160].bitcast(dt.uint32), T.kcs[:, 0:512].bitcast(dt.uint32).indirect(T.off[:, 10 * u:10 * u + 10]))
-        act(["off", "kss"], ["qs%d" % u], T.qs[:, 160 * u:160 * u + 160], T.kss[:, 0:512].indirect(T.off[:, 10 * u:10 * u + 10]))
+    halves = [1 - s // 4, s // 4]
+    for u in halves:
+        E("v", V.tensor_copy, ["off", "kcs"], ["qc%d" % u], T.qc[:, 320 * u:320 * u + 320].bitcast(dt.uint32), T.kcs[:, 0:512].bitcast(dt.uint32).indirect(T.off[:, 20 * u:20 * u + 20]))
+        act(["off", "kss"], ["qs%d" % u], T.qs[:, 320 * u:320 * u + 320], T.kss[:, 0:512].indirect(T.off[:, 20 * u:20 * u + 20]))
     codes_to = lambda d: (T.lc[:, 16 + 80 * slot(s, d):96 + 80 * slot(s, d)].bitcast(dt.uint8), T.qc[:, 80 * d:80 * d + 80].bitcast(dt.uint8))
     scales_to = lambda d: (T.ls[:, 16 + 80 * slot(s, d):96 + 80 * slot(s, d)], T.qs[:, 80 * d:80 * d + 80])
-    for us in (pairs[:1], pairs[1:3], pairs[3:]):
-        part = [d for u in us for d in (2 * u, 2 * u + 1) if d != s]
-        e = len(topo.engines(core, T.cores[part[0]])) // len(part)
-        fused([(T.cores[d],) + codes_to(d) for d in part], "rc", e, ["qc%d" % u for u in us])
-        fused([(T.cores[d],) + scales_to(d) for d in part], "rs", e, ["qs%d" % u for u in us])
+    for u in halves:
+        part = [d for d in range(4 * u, 4 * u + 4) if d != s]
+        e = len(topo.engines(core, T.cores[part[0]])) // 4
+        fused([(T.cores[d],) + codes_to(d) for d in part], "rc", e, ["qc%d" % u])
+        fused([(T.cores[d],) + scales_to(d) for d in part], "rs", e, ["qs%d" % u])
         tot["rc"] += e * len(part)
         tot["rs"] += e * len(part)
-    D("y", "dlc", *codes_to(s), ["qc%d" % pairs[3]], ["lco"])
-    D("y", "dlc", *scales_to(s), ["qs%d" % pairs[3]], ["lso"])
+    D("y", "dlc", *codes_to(s), ["qc%d" % halves[1]], ["lco"])
+    D("y", "dlc", *scales_to(s), ["qs%d" % halves[1]], ["lso"])
     gap(len(later))
     tot["rx"] = 2 * (N - 1)
     wr["rx"] = [("rx", None)]
@@ -338,10 +352,10 @@ def rank_program(g, core, T, topo):
     E("v", V.tensor_copy, ["pu", "cst"], ["w2"], T.w2[:, 0:1664].indirect(T.pu[:, 0:5]), T.cst[:])
     tp(["w2"], ["w2t"], T.w2t[:], T.w2[:, 0:512])
     for a in range(4):
-        tt(["w2t"], ["c5"], T.c5[:, a:64:4], T.w2t[32 * a:32 * a + 32, 0:512:32], T.w2t[32 * a:32 * a + 32, 16:512:32], A.add, add=True)
-    scan(["c5", "rz4"], ["cz"], T.cz[:, 0:64], T.rz4[:], T.c5[:], 0.0, A.mult, A.add)
+        tt(["w2t"], ["c5"], T.c5[:, a:128:4], T.w2t[32 * a:32 * a + 32, 0:512:16], T.w2t[32 * a:32 * a + 32, 8:512:16], A.add, add=True)
+    scan(["c5", "rz4"], ["cz"], T.cz[:, 0:128], T.rz4[:], T.c5[:], 0.0, A.mult, A.add)
     for a in range(4):
-        tp(["cz"], ["sx"], T.sx[32 * a:32 * a + 32, :], T.cz[:, 3:128:4], add=True)
+        tp(["cz"], ["sx"], T.sx[32 * a:32 * a + 32, :], T.cz[:, 7:256:8], add=True)
     copy(["sx", "ody"], ["sy"], T.sy[:], T.sx[:, 0:32].indirect(T.ody[:, 0:4]))
     tp(["sy"], ["so"], T.so[:], T.sy[:])
     copy(["so", "oo2"], ["of2"], T.of2[:], T.so[:, 0:64].indirect(T.oo2[:, 0:2]))
@@ -355,14 +369,15 @@ def rank_program(g, core, T, topo):
     for k, (a, b) in enumerate(CHUNKS):
         o = T.of2[:, a // 16:b // 16]
         E("v", V.tensor_copy, land + ["of2"], ["fc%d" % k], T.fc[:, a:b].bitcast(dt.uint32), T.lc[:, 0:656].bitcast(dt.uint32).indirect(o))
-        act(["yfz", "yf0", "yf1", "of2"], ["yo%d" % k], T.yo[:, a:b], T.yf[:, 0:656].indirect(o))
         D("y", "doc%d" % k, T.oc[:, 4 * a:4 * b], T.fc[:, a:b].bitcast(dt.uint8), ["fc%d" % k], ["oc"])
-        D("y", "dy%d" % k, T.y[:, a:b], T.yo[:, a:b], ["yo%d" % k], ["y"])
-    act(lands + ["of2"], ["fz"], T.fz[:], T.ls[:, 0:656].indirect(T.of2[:, 0:32]))
+        if b == 512:
+            act(lands + ["of2"], ["fz"], T.fz[:], T.ls[:, 0:656].indirect(T.of2[:, 0:32]))
+            for j in range(4):
+                D("y", "dos", T.osc[4 * j:4 * j + 4, :], T.fz[32 * j:32 * j + 4, :], ["fz"], ["osc"])
+        act(["yfz", "yf0", "yf1", "of2"], ["yo%d" % k], T.yo[:, a:b], T.yf[:, 0:656].indirect(o))
+        D("s" if b == 512 else "y", "dy%d" % k, T.y[:, a:b], T.yo[:, a:b], ["yo%d" % k], ["y"])
     ts(["xkk", "xk0", "of2"], ["ko"], T.ko[:], T.xk[:, 0:656].indirect(T.of2[:, 0:32]), -1.0, A.mult)
     D("y", "dok", T.ok[:], T.ko[0:64:32, :], ["ko"], ["ok"])
-    for k in range(4):
-        D("s", "dos", T.osc[4 * k:4 * k + 4, :], T.fz[32 * k:32 * k + 4, :], ["fz"], ["osc"])
     for n in SEMAPHORES:
         if tot[n]:
             g.wait_ge(T.sem[n], tot[n])

@@ -1,22 +1,23 @@
 from concourse.bass import DstId, RemoteDMATransfer
 from concourse.mybir import dt, AluOpType, AxisListType, ActivationFunctionType
 
-SCRATCH = {"mykd": ("dram", [128, 8], "int32"), "kd": ("dram", [7, 128, 8], "int32"), "acc": ("psum", [128, 1024], "float32")}
+SCRATCH = {"mykd": ("dram", [128, 8], "int32"), "kd": ("dram", [7, 128, 8], "int32"), "acc": ("psum", [128, 1536], "float32")}
 SIZES = {
-    (128, "float32"): "mv:128 val:128 ps:32 ix:96 im:80 mh:40 ic:80 i8:8 wi:1184 wt:672 hk:64 qk:24 qi:32 "
-                      "spb:16 xt:32 yy:64 ot:64 kx:24 xk:656 v6:16 pd:16 jf:8 jt:4 sm:4 sx:32 sy:64 so:64 yf:656 yo:512 ko:512",
-    (32, "float32"): "spn:16 tr:16 d7:112 d7s:112 rs7:112 d96:20 c4:64 rk4:64 ks4:68 f1:16 nk:16 pl:64 pt:64 cc:64 cy:32 pq:16 rz4:128 c5:128 cz:256",
-    (128, "bfloat16"): "pvh:6 pva:16 pvs:16 v6b:16 cm:1024 ct:1024 eq:512 et:512 es:272 zb:512 wb:512 jk:1280 cb:1920 w2:1664 w2t:512 cst:80",
-    (128, "float16"): "cs:544 cbs:960",
-    (128, "int32"): "ti:64 pi:8 zt:48", (32, "int32"): "ld:32 spr:16",
-    (128, "uint16"): "opv:2 m0:512 xu:512 mg:256 xg:256 of1:32 mb:32 mo:40 omg:16 omv:8 ox6:2 ody:4 oof:4 oo2:2 pw:8 off:48 pu:6 of2:32 mm:640 xf:640",
+    (128, "float32"): "mv:128 val:128 ps:32 ix:96 im:40 mh:20 ic:80 i8:8 wi:1184 wt:672 hk:64 qk:24 qi:32 "
+                      "spb:16 xt:32 yy:64 ot:64 kx:32 xk:656 v6:16 pd:16 jf:16 sm:8 sx:32 sy:64 so:64 yf:656 yo:512 ko:512",
+    (32, "bfloat16"): "d7:112 d7s:112 rs7:112",
+    (32, "float32"): "spn:16 tr:16 d96:20 c4:64 rk4:64 ks4:68 f1:16 nk:16 pl:64 pt:64 cc:64 cy:32 pq:16 rz4:128 c5:128 cz:256",
+    (128, "bfloat16"): "pvs:32 v6b:24 cm:1024 ct:1024 eq:512 et:512 es:272 zb:512 wb:512 jk:1280 cb:1920 w2:1664 w2t:512 cst:80",
+    (128, "float16"): "cs:544",
+    (128, "int32"): "ti:64 pi:8 zt:48 pv:4 pva:16", (32, "int32"): "ld:32 spr:16",
+    (128, "uint16"): "opv:4 m0:512 xu:512 mg:256 xg:256 of1:32 mb:32 mo:20 omg:16 omv:8 ox6:2 ody:4 oof:4 oo2:2 pw:8 off:48 pu:964 of2:32 mm:640 xf:640",
     (128, "float8_e4m3fn_x4"): "zc:128 kcs:512 qc:640 lc:656 fc:512 wc:128",
     (128, "uint8"): "zs:128 kss:512 qs:640 ls:672 fz:512 wz:128"}
 for (_p, _d), _l in SIZES.items():
     for _x in _l.split():
         SCRATCH[_x.split(":")[0]] = ("sbuf", [_p, int(_x.split(":")[1])], _d)
-SEMAPHORES = ["vs", "ss", "ts", "gs", "dk", "dt", "dsp", "dw", "dkc", "dz", "rp", "dti", "dkx", "dlc", "doc0", "doc1", "doc2", "dos", "dy0", "dy1", "dy2", "dok",
-              "rk", "rx", "rc", "rs", "loc", "lk"]
+SEMAPHORES = ["vs", "ss", "ts", "gs", "dk", "dt", "dsp", "dw", "dkc", "dz", "dti0", "dti1", "dpv", "drc", "drs", "doc0", "doc1", "doc2", "dos", "dy0", "dy1", "dy2", "dok",
+              "rk0", "rk1", "rp0", "rp1", "rx0", "rx1", "rx2", "rc", "rs0", "rs1", "rs2", "loc", "lk"]
 CHUNKS = ((0, 96), (96, 352), (352, 512))
 
 
@@ -90,11 +91,11 @@ def rank_program(g, core, T, topo):
         tr = []
         for i, (c, dst, src) in enumerate(pairs):
             rid, pid, _ = topo.addr(c)
-            e = topo.engines(core, c)[per * i:per * (i + 1)]
+            e = topo.engines(core, c)[sum(per[:i]):sum(per[:i + 1])]
             tr.append(RemoteDMATransfer(dst_ids=[DstId(rid=rid, pnc=pid)], dma_engine_mask=sum(1 << k for k in e),
-                                        remote_sem=T.sem[sem], src=src, dst=dst))
+                                        remote_sem=T.sem[sem[i] if isinstance(sem, list) else sem], src=src, dst=dst))
         g.remote_dma_fused(tr, local_sem=T.sem[loc])
-        tot[loc] += per * len(pairs)
+        tot[loc] += sum(per)
 
     higher = N - 1 - s
     lists = [n for n in (min(higher, 4), higher - 4) if n > 0]
@@ -103,10 +104,15 @@ def rank_program(g, core, T, topo):
     odd = s % 2
     slot = lambda src, dst: src ^ (dst % 2)
     P = lambda k: T.ps[:, k:k + 1]
+    pass_of = lambda src, dst: (src - dst - 1) // 4
+    e_piv = lambda src, dst: 2 if dst else 4
+    wave = lambda r: min(r // 2, 2)
 
     if s > 0:
         for k in (0, 1):
             D("ys"[k], "dk", T.mykd[64 * k:64 * k + 64, :], T.ky[:], [], ["mykd"])
+        for a in range(4):
+            D("ys"[a % 2], "dpv", T.pv[32 * a:32 * a + 32, 0:1], T.ky[0:1, :], [], ["pv"])
     for k in (0, 1):
         D("ys"[k], "dt", T.ld[8 * k:8 * k + 8, :], T.ky[:, 16 * k:16 * k + 16], [], ["ld"])
     D("y", "dt", T.ld[16:32, :], T.ky[:], [], ["ld"])
@@ -114,54 +120,51 @@ def rank_program(g, core, T, topo):
 
     iota(["pi"], T.pi[:, 0:1], [[0, 1]], 0, 1)
     iota(["imb"], T.ix[:, 0:32], [[1, 8], [8, 2], [0, 2]], 0)
-    iota(["img"], T.ix[:, 32:48], [[1, 16]], 16)
-    iota(["imv"], T.ix[:, 64:72], [[1, 4], [8, 2]], 0)
-    iota(["idz"], T.ix[:, 80:96], [[-256, 2], [-2, 8]], 0)
-    if s > 0:
-        fused([(T.cores[r], T.kd[s - r - 1], T.mykd[:]) for r in range(s)], "rk", 1, ["mykd"], "lk")
-
     for h, n in enumerate(lists):
         for a in range(n, 4):
             fill(["ti"], T.ti[32 * a:32 * a + 32, 32 * h:32 * h + 32], -1, add=True)
     fill(["rs7"], T.rs7[:], 1.0)
-    for k, (sh, m) in enumerate(((0, 15), (4, 1), (5, 3), (0, 31), (0, 1), (1, 7), (1, 1))):
+    for k, (sh, m) in enumerate(((0, 15), (4, 1), (5, 3), (0, 31), (0, 1), (1, 7))):
         ts(["pi"], ["pi%d" % k], T.pi[:, 1 + k:2 + k], T.pi[:, 0:1], sh, A.logical_shift_right, m, A.bitwise_and)
     fill(["rs7"], T.rs7[:, 0:112:7], 0.0)
     fill(["es0"], T.es[:, 0:1], 0.0)
-    copy(["pi%d" % k for k in range(7)], ["ps"], T.ps[:, 0:7], T.pi[:, 1:8])
+    copy(["pi%d" % k for k in range(6)], ["ps"], T.ps[:, 0:6], T.pi[:, 1:7])
     fill(["es0"], T.cs[:, 0:273:272], 0.0, add=True)
-    fill(["zb"], T.zb[:], 0.0)
     act(["imb"], ["mb"], T.mb[:], T.ix[:, 0:32])
-    act(["img"], ["omg"], T.omg[:], T.ix[:, 32:48])
-    ts(["ps"], ["ps8"], T.pvh[:, 4:5], P(3), 0.0, A.is_equal, 131072.0, A.mult)
-    ts(["ps"], ["ps14"], P(14), P(0), 0.0, A.is_equal, 32.0, A.mult)
-    ts(["ps"], ["ps15"], P(15), P(2), 2.0, A.is_ge, 4.0, A.mult)
-    ts(["ps"], ["ps7"], P(7), P(0), -16.0, A.mult, P(1), A.subtract)
-    if NP:
-        ts(["ps"], ["ps16"], P(16), P(2), lists[0] - 1.0, A.min, 4.0, A.mult)
-        ts(["ps"], ["ps17"], P(17), P(2), float(sum(lists[1:])), A.is_lt, P(6), A.mult)
-    ts(["imv", "ps14", "ps15"], ["omv"], T.omv[:], T.ix[:, 64:72], P(14), A.add, P(15), A.add)
-    ts(["idz", "ps7"], ["ztc"], T.zt[:, 32:48], T.ix[:, 80:96], P(7), A.add)
-    if NP:
-        lin(["ps16"], ["ps19"], P(19), P(4), 1.0, P(16))
-        lin(["ps17", "ps19"], ["opv"], T.opv[:, 0:1], P(17), 2.0, P(19))
+    if s > 0:
+        for k, m in enumerate((0xFF00, 0xFF)):
+            ts(["pv"], ["pvh"], T.pv[:, 2 + k:3 + k], T.pv[:, 0:1], m, A.bitwise_and, add=True)
+        fused([(T.cores[r], T.kd[s - r - 1], T.mykd[:]) for r in range(s)], ["rk%d" % pass_of(s, r) for r in range(s)], [1] * s, ["mykd"], "lk")
+        fused([(T.cores[r], T.pva[:, 2 * (s - r - 1):2 * (s - r)], T.pv[:, 2:4]) for r in range(s)], ["rp%d" % pass_of(s, r) for r in range(s)], [e_piv(s, r) for r in range(s)], ["pvh"], "lk")
+    sent = tot["lk"]
+    iota(["img"], T.ix[:, 32:48], [[1, 16]], 16)
+    iota(["imv"], T.ix[:, 64:72], [[1, 4], [8, 2]], 0)
+    iota(["idz"], T.ix[:, 80:96], [[-256, 2], [-2, 8]], 0)
     for a in range(4):
         tp(["ld"], ["zt"], T.zt[32 * a:32 * a + 32, 0:32], T.ld[:], add=True)
     ts(["spr"], ["spn"], T.spn[0:1, :], T.spr[0:1, :], -1.0, A.mult, 0.5, A.add)
+    for h, n in enumerate(lists):
+        ts(["ps"], ["ps16"], P(16 + h), P(2), n - 1.0, A.min, 2.0, A.mult, add=True)
     if NP:
         act(["zt", "mb"], ["m0b"], T.m0[:, 256:512], T.zt[:, 0:32].indirect(T.mb[:, 16:32]))
-    if s > 0:
-        copy(["zt"], ["pvh"], T.pvh[:, 0:1], T.zt[:, 16:17])
-        ts(["pvh", "ps8"], ["pvl"], T.pvh[:, 1:2], T.zt[:, 16:17], T.pvh[:, 0:1], A.subtract, T.pvh[:, 4:5], A.add)
-        at = lambda i: 4 * (i % 4) + 2 * (i // 4)
-        fused([(T.cores[r], T.pva[:, at(s - r - 1):at(s - r - 1) + 2], T.pvh[:, 0:2]) for r in range(s)], "rp", 2, ["pvl"], "lk")
-    sent = tot["lk"]
-    if NP:
         copy(["zt", "mb"], ["m0a"], T.m0[:, 0:256], T.zt[:, 0:32].indirect(T.mb[:, 0:16]))
-        act(["zt", "omg"], ["mg"], T.mg[:], T.zt[:, 0:32].indirect(T.omg[:, 0:16]))
-        tp(["m0b"], ["xu"], T.xu[:, 256:512], T.m0[:, 256:512], add=True)
+    for h in range(NP):
+        lin(["ps16"], ["opv"], T.opv[:, 2 * h:2 * h + 1], P(4), 1.0, P(16 + h), True)
+    ts(["ps"], ["ps8"], P(8), P(3), 0.0, A.is_equal, 131072.0, A.mult)
+    ts(["ps"], ["ps14"], P(14), P(0), 0.0, A.is_equal, 32.0, A.mult)
+    if NP:
         tp(["m0a"], ["xu"], T.xu[:, 0:256], T.m0[:, 0:256], add=True)
-        tp(["mg"], ["xg"], T.xg[:], T.mg[:])
+        tp(["m0b"], ["xu"], T.xu[:, 256:512], T.m0[:, 256:512], add=True)
+    ts(["ps"], ["ps15"], P(15), P(2), 2.0, A.is_ge, 4.0, A.mult)
+    ts(["ps"], ["ps7"], P(7), P(0), -16.0, A.mult, P(1), A.subtract)
+    ts(["ps"], ["ps26"], P(26), P(0), 4.0, A.min)
+    fill(["zb"], T.zb[:], 0.0)
+    if NP:
+        act(["img"], ["omg"], T.omg[:], T.ix[:, 32:48])
+        act(["zt", "omg"], ["mg"], T.mg[:], T.zt[:, 0:32].indirect(T.omg[:, 0:16]))
+    lin(["ps14", "ps15"], ["ps6"], P(6), P(14), 1.0, P(15))
+    lin(["idz", "ps7"], ["ztc"], T.zt[:, 32:48], T.ix[:, 80:96], 1.0, P(7))
+    lin(["imv", "ps6"], ["omv"], T.omv[:], T.ix[:, 64:72], 1.0, P(6))
     act(["zt", "ztc", "omv"], ["mv"], T.mv[:], T.zt[:, 0:48].indirect(T.omv[:, 0:8]), scale=-1.0)
     E("g", g.partition_broadcast, ["spn"], ["spb"], T.spb[:], T.spn[0:1, :], 128)
     for e in range(N - 1):
@@ -178,17 +181,19 @@ def rank_program(g, core, T, topo):
     iota(["qi"], T.qi[:], [[0, 32]], 0)
     iota(["i8"], T.i8[:, 0:4], [[16, 2], [0, 2]], 0)
     iota(["i8b"], T.i8[:, 4:8], [[8, 4]], 0)
-    iota(["im2"], T.im[:, 40:80], [[0, 4], [1, 5], [0, 2]], 0)
-    iota(["im"], T.im[:, 0:40], [[6, 4], [1, 5], [0, 2]], 0)
+    iota(["im2"], T.im[:, 20:40], [[0, 2], [1, 5], [0, 2]], 0)
+    iota(["im"], T.im[:, 0:20], [[8, 2], [1, 5], [0, 2]], 1)
     iota(["ic"], T.ic[:], [[32, 5], [1, 16]], 0)
-    iota(["jf"], T.jf[:, 0:5], [[128, 5]], 512, 1)
+    iota(["ijf"], T.jf[:, 8:13], [[128, 5]], 512)
     iota(["rz4"], T.rz4[:], [[0, 16], [1, 8]], 0)
     iota(["cz"], T.cz[:, 135:256:8], [[0, 16]], 0)
     iota(["xk0"], T.xk[:, 0:16], [[0, 16]], 1)
     iota(["yfz"], T.yf[:, 0:16], [[0, 16]], 0)
     iota(["xkk"], T.xk[:, 16:656], [[-2, 4], [1, 2], [0, 80]] if odd else [[-1, 8], [0, 80]], -odd)
 
-    lin(["ps"], ["ps9"], P(9), P(2), 6.0, P(0))
+    lin(["ps26"], ["ps9"], P(9), P(2), 8.0, P(26))
+    lin(["ps"], ["ps27"], P(27), P(1), 1.0, -2.5)
+    lin(["ps"], ["ps28"], P(28), P(0), 8.0, 0.0)
     lin(["ps"], ["ps10"], P(10), P(4), 32.0, P(5))
     lin(["ps"], ["ps11"], P(11), P(4), -31.0, P(5))
     lin(["ps"], ["ps12"], P(12), P(1), 16.0, 16.0)
@@ -208,61 +213,55 @@ def rank_program(g, core, T, topo):
         lin(["i8b", "ps10"], ["oo2"], T.oo2[:], T.i8[:, 4:6], 1.0, P(10))
         lin(["ps11"], ["ps23"], P(23), P(10 + odd), 1.0, 32.0 * odd)
         lin(["i8b", "ps23"], ["oof"], T.oof[:], T.i8[:, 4:8], 1.0, P(23))
+        act(["im2", "ps27"], ["mh"], T.mh[:], T.im[:, 20:40], AF.Sign, bias=P(27))
+        lin(["ijf", "ps28"], ["jf"], T.jf[:, 0:5], T.jf[:, 8:13], 1.0, P(28))
         act(["rz4"], ["rz4"], T.rz4[:], T.rz4[:], AF.Sign)
-
-    def zeros():
-        E("v", V.quantize_mx, ["zb"], ["zc", "zs"], T.zc[:], T.zs[:], T.zb[:])
-        D("y", "dz", T.lc[:, 0:1].bitcast(dt.uint8), T.zc[:, 0:1].bitcast(dt.uint8), ["zc"], ["lcz"])
-        D("y", "dz", T.ls[:, 0:1], T.zs[:, 0:1], ["zs"], ["lsz"])
 
     def columns():
         ts(["ps13"], ["ps25"], P(25), P(0), 8.0, A.is_equal, P(13), A.mult)
         lin(["ic", "ps24", "ps25"], ["cst"], T.cst[:], T.ic[:], P(24), P(25))
 
+    E("v", V.quantize_mx, ["zb"], ["zc", "zs"], T.zc[:], T.zs[:], T.zb[:])
+    if NP: later.append(lambda: tp(["mg"], ["xg"], T.xg[:], T.mg[:]))
     later += [
         first_slots,
         lambda: tp(["mv"], ["val"], T.val[:], T.mv[:]),
-        zeros,
-        columns,
         lambda: ts(["ps"], ["ps18"], P(18), P(0), P(1), A.add, 3.0, A.is_ge),
-        lambda: ts(["im2", "ps"], ["mh"], T.mh[:], T.im[:, 40:80], P(1), A.add, 3.0, A.is_ge),
-        lambda: ts(["ps9", "ps18"], ["ox6"], T.ox6[:, 0:1], P(9), P(18), A.add, 23.0, A.min),
-        lambda: tt(["im", "mh"], ["mo"], T.mo[:], T.im[:, 0:40], T.mh[:], A.add),
-        lambda: E("v", V.quantize_mx, ["wb"], ["wc", "wz"], T.wc[:], T.wz[:], T.wb[:])]
+        columns,
+        lambda: ts(["ps9", "ps18"], ["ox6"], T.ox6[:, 0:1], P(18), 2.0, A.mult, P(9), A.add)]
 
     if NP:
-        tot["rk"] = higher
-        wr["rk"] = [("rk", None)]
         for h, n in enumerate(lists):
-            D("y", "dti", T.ti[0:32 * n, 32 * h:32 * h + 32], T.kd[4 * h:4 * h + n], ["rk", "ti"], ["tia"])
+            tot["rk%d" % h] = n
+            wr["rk%d" % h] = [("rk%d" % h, None)]
+            D("y", "dti%d" % h, T.ti[0:32 * n, 32 * h:32 * h + 32], T.kd[4 * h:4 * h + n], ["rk%d" % h, "ti"], ["tia%d" % h])
     if sent:
         g.sync.wait_ge(T.sem.lk, sent)
     D("y", "dkc", T.kcs[:].bitcast(dt.uint8), T.kc[:], [], ["kcs"])
     D("y", "dkc", T.kss[:], T.ks[:], [], ["kss"])
     D("y", "dw", T.wb[:], T.w[:], [], ["wb"])
+    D("y", "dz", T.lc[:, 0:16].bitcast(dt.uint8), T.zc[:, 0:16].bitcast(dt.uint8), ["zc"], ["lcz"])
+    D("y", "dz", T.ls[:, 0:16], T.zs[:, 0:16], ["zs"], ["lsz"])
     kb = T.ks4[:, nq - 1:17 * nq:nq]
     kept = T.ks4[:, 2 * nq - 1:17 * nq:nq]
     if NP:
         n = 256 * NP
-        tot["rp"] = 2 * higher
-        wr["rp"] = [("rp", None)]
-        copy(["rp", "opv"], ["pvs"], T.pvs[:], T.pva[:, 0:16].indirect(T.opv[:, 0:1]))
-        gap()
-        for h in range(NP):
-            ts(["xu", "pvs"], ["cm%d" % h], T.cm[:, 512 * h:512 * h + 512], T.xu[:], T.pvs[:, 2 * h:2 * h + 1], A.subtract, T.pvs[:, 2 * h + 1:2 * h + 2], A.is_ge)
-        for h in range(NP):
-            tp(["cm%d" % h], ["ct%d" % h], T.ct[:, 512 * h:512 * h + 512], T.cm[:, 512 * h:512 * h + 512])
-        for h in range(NP):
-            c = 272 * h
-            scan(["ct%d" % h], ["cs%d" % h], T.cs[:, c + 1:c + 257], T.ct[:, 512 * h:512 * h + 512:2], T.ct[:, 512 * h + 1:512 * h + 512:2], 0.0, A.add, A.add)
-        for h in range(NP):
-            c = 272 * h
-            tt(["cs%d" % h, "es0"], ["of%d" % h], T.of1[:, 16 * h:16 * h + 16], T.cs[:, c + 16:c + 257:16], T.cs[:, c:c + 256:16], A.subtract)
-        for h in range(NP):
-            tt(["ti", "tia", "of%d" % h, "xg"], ["eq"], T.eq[:, 256 * h:256 * h + 256], T.ti[:, 32 * h:32 * h + 32].indirect(T.of1[:, 16 * h:16 * h + 16]), T.xg[:], A.is_equal, add=True)
-        gap()
-        tp(["eq"], ["et"], T.et[:, 0:n], T.eq[:, 0:n])
-        gap()
+        def search(h):
+            H, c, b = "%d" % h, 272 * h, 512 * h
+            tot["rp" + H] = sum(e_piv(r, s) for r in range(s + 1 + 4 * h, min(s + 5 + 4 * h, N)))
+            wr["rp" + H] = [("rp" + H, None)]
+            return [
+                lambda: ts(["rp" + H, "opv", "ps8"], ["pvs" + H], T.pvs[:, 16 * h:16 * h + 16], T.pva[:, 8 * h:8 * h + 8].indirect(T.opv[:, 2 * h:2 * h + 1]), P(8), A.add),
+                lambda: ts(["xu", "pvs" + H], ["cm" + H], T.cm[:, b:b + 512], T.xu[:], T.pvs[:, 16 * h:16 * h + 1], A.subtract, T.pvs[:, 16 * h + 1:16 * h + 2], A.is_ge),
+                lambda: tp(["cm" + H], ["ct" + H], T.ct[:, b:b + 512], T.cm[:, b:b + 512]),
+                lambda: scan(["ct" + H], ["cs" + H], T.cs[:, c + 1:c + 257], T.ct[:, b:b + 512:2], T.ct[:, b + 1:b + 512:2], 0.0, A.add, A.add),
+                lambda: tt(["cs" + H, "es0"], ["of" + H], T.of1[:, 16 * h:16 * h + 16], T.cs[:, c + 16:c + 257:16], T.cs[:, c:c + 256:16], A.subtract),
+                lambda: tt(["ti", "tia" + H, "of" + H, "xg"], ["eq" + H], T.eq[:, 256 * h:256 * h + 256], T.ti[:, 32 * h:32 * h + 32].indirect(T.of1[:, 16 * h:16 * h + 16]), T.xg[:], A.is_equal),
+                lambda: tp(["eq" + H], ["et"], T.et[:, 256 * h:256 * h + 256], T.eq[:, 256 * h:256 * h + 256], add=True)]
+        steps = [search(h) for h in range(NP)]
+        for k in range(7):
+            for p in steps: p[k]()
+            if k in (0, 5, 6): gap()
         if NP == 2: w = 16; scan(["et"], ["es"], T.es[:, 1:257], T.et[:, 0:256], T.et[:, 256:512], 0.0, A.add, A.add)
         else: w = 8; scan(["et"], ["es"], T.es[:, 1:129], T.et[:, 0:256:2], T.et[:, 1:256:2], 0.0, A.add, A.add)
         gap()
@@ -283,7 +282,7 @@ def rank_program(g, core, T, topo):
     scan(["pt"], ["cc"], T.cc[:, 1:33], T.pt[:, 0:32], T.pt[:, 32:64], 0.0, A.add, A.max)
     gap()
     tp(["cc"], ["cy"], T.cy[:], T.cc[:, 0:32])
-    gap()
+    tt(["im", "mh"], ["mo"], T.mo[:], T.im[:, 0:20], T.mh[:], A.add)
     scan(["ks4", "d96", "cy"], ["pq"], T.pq[:], T.ks4[:, nq - 1:16 * nq:nq], T.d96[:, 0:16], T.cy[:, 16:17], A.add, A.max)
     gap()
     for a in range(4):
@@ -298,11 +297,11 @@ def rank_program(g, core, T, topo):
     for k in (0, 1):
         tt(["hi"], ["qi"], T.qi[64 * k:64 * k + 64, 0:21], T.hk[0:64, 32:53], T.hk[64:128, 32:53], A.max, add=k > 0)
     peers = [(s + i) % N for i in range(1, N)]
-    keys = lambda d: (T.kx[:, 3 * slot(s, d):3 * slot(s, d) + 3], T.qk[:, (5 * d + odd) // 2:(5 * d + odd) // 2 + 3])
-    fused([(T.cores[d],) + keys(d) for d in peers], "rx", 2, ["qk"])
-    D("y", "dkx", *keys(s), ["qk"], ["kx"])
+    keys = lambda d: (T.kx[:, 4 * slot(s, d):4 * slot(s, d) + 3], T.qk[:, (5 * d + odd) // 2:(5 * d + odd) // 2 + 3])
+    fused([(T.cores[d],) + keys(d) for d in peers], "rx%d" % wave(s), [2] * len(peers), ["qk"])
+    act(["qk"], ["kx%d" % wave(s)], *keys(s))
     tp(["qi"], ["xt"], T.xt[:], T.qi[:])
-    gap()
+    E("v", V.quantize_mx, ["wb"], ["wc", "wz"], T.wc[:], T.wz[:], T.wb[:])
     copy(["xt", "ody"], ["yy"], T.yy[:], T.xt[:, 0:32].indirect(T.ody[:, 0:4]))
     gap()
     tp(["yy"], ["ot"], T.ot[:], T.yy[:])
@@ -310,46 +309,62 @@ def rank_program(g, core, T, topo):
     copy(["ot", "oof"], ["off"], T.off[:], T.ot[:, 0:64].indirect(T.oof[:, 0:3]))
     gap()
     halves = [1 - s // 4, s // 4]
-    for u in halves:
-        E("v", V.tensor_copy, ["off", "kcs"], ["qc%d" % u], T.qc[:, 320 * u:320 * u + 320].bitcast(dt.uint32), T.kcs[:, 0:512].bitcast(dt.uint32).indirect(T.off[:, 20 * u:20 * u + 20]))
-        act(["off", "kss"], ["qs%d" % u], T.qs[:, 320 * u:320 * u + 320], T.kss[:, 0:512].indirect(T.off[:, 20 * u:20 * u + 20]))
     codes_to = lambda d: (T.lc[:, 16 + 80 * slot(s, d):96 + 80 * slot(s, d)].bitcast(dt.uint8), T.qc[:, 80 * d:80 * d + 80].bitcast(dt.uint8))
     scales_to = lambda d: (T.ls[:, 16 + 80 * slot(s, d):96 + 80 * slot(s, d)], T.qs[:, 80 * d:80 * d + 80])
-    for u in halves:
-        part = [d for d in range(4 * u, 4 * u + 4) if d != s]
-        e = len(topo.engines(core, T.cores[part[0]])) // 4
-        fused([(T.cores[d],) + codes_to(d) for d in part], "rc", e, ["qc%d" % u])
-        fused([(T.cores[d],) + scales_to(d) for d in part], "rs", e, ["qs%d" % u])
-        tot["rc"] += e * len(part)
-        tot["rs"] += e * len(part)
-    D("y", "dlc", *codes_to(s), ["qc%d" % halves[1]], ["lco"])
-    D("y", "dlc", *scales_to(s), ["qs%d" % halves[1]], ["lso"])
+
+    def send(a, b, to, sem, toks):
+        part = [d for d in range(a, b) if d != s]
+        e = len(topo.engines(core, T.cores[part[0]])) // (b - a)
+        fused([(T.cores[d],) + to(d) for d in part], sem, [e] * len(part), toks)
+        if a <= s < b: D("y", "d" + sem[:2], *to(s), toks, ["o" + sem[:2]])
+
+    def codes(a, b):
+        E("v", V.tensor_copy, ["off", "kcs"], ["qc%d" % a], T.qc[:, 80 * a:80 * b].bitcast(dt.uint32), T.kcs[:, 0:512].bitcast(dt.uint32).indirect(T.off[:, 5 * a:5 * b]))
+
+    def scales(a, b, sem):
+        act(["off", "kss"], ["qs%d" % a], T.qs[:, 80 * a:80 * b], T.kss[:, 0:512].indirect(T.off[:, 5 * a:5 * b]))
+        send(a, b, scales_to, sem, ["qs%d" % a])
+
+    far, near, me, nb = 4 * halves[0], 4 * halves[1], s - odd, (s - odd) ^ 2
+    codes(far, far + 4)
+    send(far, far + 4, codes_to, "rc", ["qc%d" % far])
+    scales(me, me + 2, "rs0")
+    codes(me, me + 2)
+    codes(nb, nb + 2)
+    send(near, near + 4, codes_to, "rc", ["qc%d" % me, "qc%d" % nb])
+
+    if NP < 2: scales(far, far + 4, "rs2")
     gap(len(later))
-    tot["rx"] = 2 * (N - 1)
-    wr["rx"] = [("rx", None)]
-    kxr = ["rx", "kx", "mo", "ox6", "phi"]
-    act(kxr, ["mmS"], T.mm[:, 192:640], T.kx[:, 0:24].indirect(T.mo[:, 12:40]), AF.Identity, bias=P(20))
-    ts(kxr, ["mmV"], T.mm[:, 0:192], T.kx[:, 0:24].indirect(T.mo[:, 0:12]), P(20), A.add)
-    ts(kxr, ["v6"], T.v6[:], T.kx[:, 0:24].indirect(T.ox6[:, 0:1]), P(21), A.add, 0.5, A.max)
-    tp(["mmV"], ["xfV"], T.xf[:, 0:192], T.mm[:, 0:192])
-    copy(["v6"], ["v6h"], T.v6b[:, 0:3], T.v6[:, 2:5])
+    for u in range(3):
+        tot["rx%d" % u] = sum(2 for r in range(N) if r != s and wave(r) == u)
+        wr["kx%d" % u] = wr.get("kx%d" % u, []) + [("rx%d" % u, None)]
+    kxr, kxs = ["mo", "ox6", "phi"], ["kx0", "kx1", "kx2"]
+    act(kxr + ["kx2"], ["mm2"], T.mm[:, 320:640], T.kx[:, 16:32].indirect(T.mo[:, 0:20]), AF.Identity, bias=P(20))
+    act(kxr + ["kx1"], ["mm1"], T.mm[:, 160:320], T.kx[:, 8:16].indirect(T.mo[:, 0:10]), AF.Identity, bias=P(20))
+    act(kxr + ["kx0"], ["mm0"], T.mm[:, 0:160], T.kx[:, 0:8].indirect(T.mo[:, 0:10]), AF.Identity, bias=P(20))
+    for out, tok in ((T.v6, "v6"), (T.v6b, "v6h")):
+        ts(kxr + kxs, [tok], out[:, 0:16], T.kx[:, 0:32].indirect(T.ox6[:, 0:1]), P(21), A.add, 0.5, A.max)
+    tp(["mm2"], ["xf2"], T.xf[:, 320:640], T.mm[:, 320:640])
     ts(["v6"], ["pd"], T.pd[:, 0:5], T.v6[:, 0:5], 1.0, A.is_lt)
-    tt(["v6", "v6h"], ["v6l"], T.v6b[:, 8:11], T.v6[:, 2:5], T.v6b[:, 0:3], A.subtract)
-    tp(["mmS"], ["xfS"], T.xf[:, 192:640], T.mm[:, 192:640])
-    tt(["pd", "jf"], ["pd2"], T.pd[:, 8:13], T.pd[:, 0:5], T.jf[:, 0:5], A.mult)
-    xs = ["xfV", "xfS"]
-    for e in range(2):
-        act(xs + ["v6"], ["jk%d" % e, "sm%d" % e], T.jk[:, 640 * e:640 * e + 640], T.xf[:], AF.Sign, scale=-1.0, bias=T.v6[:, e:e + 1], accum_out=T.sm[:, e:e + 1])
+    tt(["v6", "v6h"], ["v6l"], T.v6b[:, 16:19], T.v6[:, 0:3], T.v6b[:, 0:3], A.subtract)
+    tp(["mm1"], ["xf1"], T.xf[:, 160:320], T.mm[:, 160:320])
+    tp(["mm0"], ["xf0"], T.xf[:, 0:160], T.mm[:, 0:160])
+    tt(["pd", "jf"], ["pd2"], T.v6b[:, 20:23], T.pd[:, 0:3], T.jf[:, 0:3], A.mult)
+    xs = ["xf0", "xf1", "xf2"]
+    for e in (3, 4):
+        act(xs + ["v6"], ["jk%d" % e, "sm%d" % e], T.jk[:, 640 * e - 1920:640 * e - 1280], T.xf[:], AF.Sign, scale=-1.0, bias=T.v6[:, e:e + 1], accum_out=T.sm[:, e:e + 1])
+    if NP == 2: scales(far, far + 4, "rs2")
+    scales(nb, nb + 2, "rs1")
     act(xs + ["phi"], ["xkk"], T.xk[0:32, 16:656], T.xf[0:32, :], AF.Identity, bias=T.ps[0:32, 22:23])
     for k in range(3):
-        ts(xs + ["v6l"], ["cb%d" % k], T.cb[:, 640 * k:640 * k + 640], T.xf[:], T.v6b[:, k:k + 1], A.subtract, T.v6b[:, 8 + k:9 + k], A.is_gt)
-    ts(["pd2"], ["jt"], T.jt[:, 0:2], T.pd[:, 8:10], 320.0, A.add)
+        ts(xs + ["v6l"], ["cb%d" % k], T.cb[:, 640 * k:640 * k + 640], T.xf[:], T.v6b[:, k:k + 1], A.subtract, T.v6b[:, 16 + k:17 + k], A.is_gt)
+    for e in (3, 4):
+        ts(["pd", "jf"], ["jt"], T.pd[:, 8 + e:9 + e], T.pd[:, e:e + 1], T.jf[:, e:e + 1], A.mult, 320.0, A.add, add=True)
     for k in range(3):
-        scan(["cb%d" % k], ["cbs"], T.cbs[:, 320 * k:320 * k + 320], T.cb[:, 640 * k:640 * k + 320], T.cb[:, 640 * k + 320:640 * k + 640], 0.0, A.add, A.add, add=True)
-    for e in range(2):
-        ts(["sm%d" % e, "jt"], ["pu"], T.pu[:, e:e + 1], T.sm[:, e:e + 1], -0.5, A.mult, T.jt[:, e:e + 1], A.add, add=True)
-    tt(["cbs", "pd2"], ["pu"], T.pu[:, 2:5], T.cbs[:, 319:960:320], T.pd[:, 10:13], A.add, add=True)
-    E("v", V.tensor_copy, ["pu", "cst"], ["w2"], T.w2[:, 0:1664].indirect(T.pu[:, 0:5]), T.cst[:])
+        scan(["cb%d" % k, "pd2"], ["pu"], T.pu[:, 1 + k:959 + k:3], T.cb[:, 640 * k:640 * k + 320], T.cb[:, 640 * k + 320:640 * k + 640], T.v6b[:, 20 + k:21 + k], A.add, A.add, add=True)
+        if k:
+            ts(["sm%d" % (2 + k), "jt"], ["pu"], T.pu[:, 960 + k:961 + k], T.sm[:, 2 + k:3 + k], -0.5, A.mult, T.pd[:, 10 + k:11 + k], A.add, add=True)
+    E("v", V.tensor_copy, ["pu", "cst"], ["w2"], T.w2[:, 0:1664].indirect(T.pu[:, 958:963]), T.cst[:])
     tp(["w2"], ["w2t"], T.w2t[:], T.w2[:, 0:512])
     for a in range(4):
         tt(["w2t"], ["c5"], T.c5[:, a:128:4], T.w2t[32 * a:32 * a + 32, 0:512:16], T.w2t[32 * a:32 * a + 32, 8:512:16], A.add, add=True)
@@ -359,13 +374,16 @@ def rank_program(g, core, T, topo):
     copy(["sx", "ody"], ["sy"], T.sy[:], T.sx[:, 0:32].indirect(T.ody[:, 0:4]))
     tp(["sy"], ["so"], T.so[:], T.sy[:])
     copy(["so", "oo2"], ["of2"], T.of2[:], T.so[:, 0:64].indirect(T.oo2[:, 0:2]))
-    wr["lca"], wr["lsa"] = [("rc", None)], [("rs", None)]
-    land, lands = ["lca", "lco", "lcz"], ["lsa", "lso", "lsz"]
-    for k in (0, 1):
-        c = 16 + 320 * k
-        E("t", g.tensor.matmul_mx, land + lands + ["wc", "wz"], ["acc%d" % k], T.acc[:, 512 * k:512 * k + 320], T.wc[:], T.wz[:], T.lc[:, c:c + 320], T.ls[:, c:c + 320], True, True)
-    for k in (0, 1):
-        act(["acc%d" % k], ["yf%d" % k], T.yf[:, 16 + 320 * k:336 + 320 * k], T.acc[:, 512 * k:512 * k + 320])
+    tot["rc"] = 4 * (N - 1)
+    wr["lca"] = [("rc", None)]
+    land, lands = ["lca", "orc", "lcz"], ["ls0", "ls1", "ls2", "ors", "lsz"]
+    for k in (0, 2, 1):
+        r, n = ((me, 160), (nb, 160), (far, 320))[k]
+        tot["rs%d" % k] = 16 if k else 8
+        wr["ls%d" % k] = [("rs%d" % k, None)]
+        c = 16 + 80 * r
+        E("t", g.tensor.matmul_mx, land + ["ls%d" % k, "ors", "wc", "wz"], ["acc%d" % k], T.acc[:, 512 * k:512 * k + n], T.wc[:], T.wz[:], T.lc[:, c:c + n], T.ls[:, c:c + n], True, True)
+        act(["acc%d" % k], ["yf%d" % k], T.yf[:, c:c + n], T.acc[:, 512 * k:512 * k + n])
     for k, (a, b) in enumerate(CHUNKS):
         o = T.of2[:, a // 16:b // 16]
         E("v", V.tensor_copy, land + ["of2"], ["fc%d" % k], T.fc[:, a:b].bitcast(dt.uint32), T.lc[:, 0:656].bitcast(dt.uint32).indirect(o))
@@ -374,7 +392,7 @@ def rank_program(g, core, T, topo):
             act(lands + ["of2"], ["fz"], T.fz[:], T.ls[:, 0:656].indirect(T.of2[:, 0:32]))
             for j in range(4):
                 D("y", "dos", T.osc[4 * j:4 * j + 4, :], T.fz[32 * j:32 * j + 4, :], ["fz"], ["osc"])
-        act(["yfz", "yf0", "yf1", "of2"], ["yo%d" % k], T.yo[:, a:b], T.yf[:, 0:656].indirect(o))
+        act(["yfz", "yf0", "yf1", "yf2", "of2"], ["yo%d" % k], T.yo[:, a:b], T.yf[:, 0:656].indirect(o))
         D("s" if b == 512 else "y", "dy%d" % k, T.y[:, a:b], T.yo[:, a:b], ["yo%d" % k], ["y"])
     ts(["xkk", "xk0", "of2"], ["ko"], T.ko[:], T.xk[:, 0:656].indirect(T.of2[:, 0:32]), -1.0, A.mult)
     D("y", "dok", T.ok[:], T.ko[0:64:32, :], ["ko"], ["ok"])

@@ -1,23 +1,24 @@
 from concourse.bass import DstId, RemoteDMATransfer
 from concourse.mybir import dt, AluOpType, AxisListType, ActivationFunctionType
 
-SCRATCH = {"mykd": ("dram", [128, 8], "int32"), "kd": ("dram", [7, 128, 8], "int32"), "acc": ("psum", [128, 1536], "float32")}
+SCRATCH = {"mykd": ("dram", [128, 8], "int32"), "kd": ("dram", [7, 128, 8], "int32"), "acc": ("psum", [128, 2048], "float32")}
 SIZES = {
-    (128, "float32"): "mv:128 val:128 ps:32 ix:96 im:40 mh:20 ic:80 i8:8 wi:1184 wt:672 hk:64 qk:24 qi:32 "
+    (128, "float32"): "vf:16 ps:32 ix:96 im:40 mh:20 ic:80 i8:4 qk:24 "
                       "spb:16 xt:32 yy:64 ot:64 kx:32 xk:656 v6:16 pd:16 jf:16 sm:8 sx:32 sy:64 so:64 yf:656 yo:512 ko:512",
-    (32, "bfloat16"): "d7:112 d7s:112 rs7:112",
-    (32, "float32"): "spn:16 tr:16 d96:20 c4:64 rk4:64 ks4:68 f1:16 nk:16 pl:64 pt:64 cc:64 cy:32 pq:16 rz4:128 c5:128 cz:256",
-    (128, "bfloat16"): "pvs:32 v6b:24 cm:1024 ct:1024 eq:512 et:512 es:272 zb:512 wb:512 jk:1280 cb:1920 w2:1664 w2t:512 cst:80",
+    (64, "bfloat16"): "d7:112 d7s:112 rs7:112 es:528", (32, "float32"): "spn:16 c4:20",
+    (64, "float32"): "tr:16 d96:20 ks4:20 f1:16 nk:20 dd:48 pl:64 pt:64 cc:64 cy:32 hk:88 qi:128 nj:16 c5:64 cz:128",
+    (128, "bfloat16"): "zw:64 mv:128 val:128 wi:2368 wt:672 pvs:16 v6b:24 cm:1024 ct:1024 eq:512 et:512 zb:512 wb:512 jk:1280 cb:1920 w2:1664 w2t:512 cst:80",
     (128, "float16"): "cs:544",
-    (128, "int32"): "ti:64 pi:8 zt:48 pv:4 pva:16", (32, "int32"): "ld:32 spr:16",
-    (128, "uint16"): "opv:4 m0:512 xu:512 mg:256 xg:256 of1:32 mb:32 mo:20 omg:16 omv:8 ox6:2 ody:4 oof:4 oo2:2 pw:8 off:48 pu:964 of2:32 mm:640 xf:640",
+    (128, "int32"): "ti:64 pi:8 zt:32 pv:4 pva:16", (32, "int32"): "ld:32 spr:16",
+    (128, "uint16"): "opv:4 m0:512 xu:512 mg:256 xg:256 of1:32 mb:32 mo:20 omg:16 omv:8 ox6:2 ody:4 pw:24 off:40 pu:964 of2:32 mm:640 xf:640",
     (128, "float8_e4m3fn_x4"): "zc:128 kcs:512 qc:640 lc:656 fc:512 wc:128",
     (128, "uint8"): "zs:128 kss:512 qs:640 ls:672 fz:512 wz:128"}
 for (_p, _d), _l in SIZES.items():
     for _x in _l.split():
         SCRATCH[_x.split(":")[0]] = ("sbuf", [_p, int(_x.split(":")[1])], _d)
-SEMAPHORES = ["vs", "ss", "ts", "gs", "dk", "dt", "dsp", "dw", "dkc", "dz", "dti0", "dti1", "dpv", "drc", "drs", "doc0", "doc1", "doc2", "dos", "dy0", "dy1", "dy2", "dok",
-              "rk0", "rk1", "rp0", "rp1", "rx0", "rx1", "rx2", "rc", "rs0", "rs1", "rs2", "loc", "lk"]
+SEMAPHORES = ["gs", "dk", "dt", "dsp", "dpv", "lk", "rk", "rp", "dti0", "dti1", "dw", "dkc", "dz", "rx0", "rx1", "rx2", "drc", "drs", "rc", "rs0", "rs1", "rs2",
+              "loc", "ts", "vs", "ss", "doc0", "dy0", "doc1", "dy1", "doc2", "dos", "dok", "dy2"]
+E_TABLE, E_FIRST = 4, 8
 CHUNKS = ((0, 96), (96, 352), (352, 512))
 
 
@@ -36,13 +37,14 @@ def rank_program(g, core, T, topo):
     def need(q, r, w, add=False):
         deps = [(d, 0) for t in r for d in wr.get(t, [])]
         deps += [(d, 1) for t in w for d in wr.get(t, []) + rd.get(t, [])]
+        most = {}
         for (sem, n), order in deps:
-            if order and add and own.get(q) == sem:
-                continue
-            n = tot[sem] if n is None else n
-            if seen[q].get(sem, 0) < n:
-                q_of[q].wait_ge(T.sem[sem], n)
-                seen[q][sem] = n
+            if not (order and add and own.get(q) == sem):
+                most[sem] = max(most.get(sem, 0), tot[sem] if n is None else n)
+        for sem in sorted(most, key=lambda x: x == own.get(q)):
+            if seen[q].get(sem, 0) < most[sem]:
+                q_of[q].wait_ge(T.sem[sem], most[sem])
+                seen[q][sem] = most[sem]
 
     def note(me, r, w, add=False):
         for t in r:
@@ -86,26 +88,31 @@ def rank_program(g, core, T, topo):
         for _ in range(min(n, len(later))):
             later.pop(0)()
 
-    def fused(pairs, sem, per, r, loc="loc"):
+    def fused(pairs, sem, per, r):
         need("g", r, [])
         tr = []
         for i, (c, dst, src) in enumerate(pairs):
             rid, pid, _ = topo.addr(c)
             e = topo.engines(core, c)[sum(per[:i]):sum(per[:i + 1])]
             tr.append(RemoteDMATransfer(dst_ids=[DstId(rid=rid, pnc=pid)], dma_engine_mask=sum(1 << k for k in e),
-                                        remote_sem=T.sem[sem[i] if isinstance(sem, list) else sem], src=src, dst=dst))
-        g.remote_dma_fused(tr, local_sem=T.sem[loc])
-        tot[loc] += sum(per)
+                                        remote_sem=T.sem[sem], src=src, dst=dst))
+        g.remote_dma_fused(tr, local_sem=T.sem.loc)
+        tot["loc"] += sum(per)
+
+    def to_lower(dst, src, sem, per, r):
+        need("g", r, [])
+        ids = [DstId(rid=topo.addr(c)[0], pnc=topo.addr(c)[1]) for c in T.cores[:s]]
+        mask = sum(1 << k for k in topo.engines(core, T.cores[0])[:per])
+        g.remote_dma_fused([RemoteDMATransfer(dst_ids=ids, dma_engine_mask=mask, remote_sem=T.sem[sem], srcs=[src],
+                                              dsts=[dst(s - d - 1) for d in range(s)])], local_sem=T.sem.lk)
+        tot["lk"] += per
 
     higher = N - 1 - s
     lists = [n for n in (min(higher, 4), higher - 4) if n > 0]
     NP = len(lists)
-    nq = lists[0] if lists else 1
     odd = s % 2
     slot = lambda src, dst: src ^ (dst % 2)
     P = lambda k: T.ps[:, k:k + 1]
-    pass_of = lambda src, dst: (src - dst - 1) // 4
-    e_piv = lambda src, dst: 2 if dst else 4
     wave = lambda r: min(r // 2, 2)
 
     if s > 0:
@@ -120,73 +127,76 @@ def rank_program(g, core, T, topo):
 
     iota(["pi"], T.pi[:, 0:1], [[0, 1]], 0, 1)
     iota(["imb"], T.ix[:, 0:32], [[1, 8], [8, 2], [0, 2]], 0)
+    iota(["img"], T.ix[:, 32:48], [[1, 16]], 16)
+    iota(["imv"], T.ix[:, 64:72], [[1, 4], [8, 2]], 0)
     for h, n in enumerate(lists):
         for a in range(n, 4):
             fill(["ti"], T.ti[32 * a:32 * a + 32, 32 * h:32 * h + 32], -1, add=True)
     fill(["rs7"], T.rs7[:], 1.0)
-    for k, (sh, m) in enumerate(((0, 15), (4, 1), (5, 3), (0, 31), (0, 1), (1, 7))):
+    for k, (sh, m) in enumerate(((0, 15), (4, 1), (5, 3), (0, 31), (0, 1), (2, 1), (3, 1))):
         ts(["pi"], ["pi%d" % k], T.pi[:, 1 + k:2 + k], T.pi[:, 0:1], sh, A.logical_shift_right, m, A.bitwise_and)
     fill(["rs7"], T.rs7[:, 0:112:7], 0.0)
     fill(["es0"], T.es[:, 0:1], 0.0)
-    copy(["pi%d" % k for k in range(6)], ["ps"], T.ps[:, 0:6], T.pi[:, 1:7])
+    copy(["pi%d" % k for k in range(7)], ["ps"], T.ps[:, 0:7], T.pi[:, 1:8])
     fill(["es0"], T.cs[:, 0:273:272], 0.0, add=True)
+    fill(["zb"], T.zb[:], 0.0)
     act(["imb"], ["mb"], T.mb[:], T.ix[:, 0:32])
+    ts(["ps"], ["ps16"], P(16), P(0), 2.0, A.is_ge, 4.0, A.mult)
+    ts(["ps"], ["ps8"], P(8), P(3), 0.0, A.is_equal, 131072.0, A.mult)
+    ts(["ps"], ["ps15"], P(15), P(2), 2.0, A.is_ge, 4.0, A.mult)
+    ts(["ps"], ["ps7"], P(7), P(0), 16.0, A.mult, P(1), A.add)
+    if NP:
+        ts(["ps16"], ["ps17"], P(17), P(16), P(2), A.add, higher - 1.0, A.min)
+        lin(["ps17"], ["opv"], T.opv[:, 0:1], P(17), 2.0, P(4))
     if s > 0:
         for k, m in enumerate((0xFF00, 0xFF)):
             ts(["pv"], ["pvh"], T.pv[:, 2 + k:3 + k], T.pv[:, 0:1], m, A.bitwise_and, add=True)
-        fused([(T.cores[r], T.kd[s - r - 1], T.mykd[:]) for r in range(s)], ["rk%d" % pass_of(s, r) for r in range(s)], [1] * s, ["mykd"], "lk")
-        fused([(T.cores[r], T.pva[:, 2 * (s - r - 1):2 * (s - r)], T.pv[:, 2:4]) for r in range(s)], ["rp%d" % pass_of(s, r) for r in range(s)], [e_piv(s, r) for r in range(s)], ["pvh"], "lk")
+        to_lower(lambda i: T.kd[i], T.mykd[:], "rk", E_TABLE, ["mykd"])
+        to_lower(lambda i: T.pva[:, 2 * i:2 * i + 2], T.pv[:, 2:4], "rp", E_FIRST, ["pvh"])
     sent = tot["lk"]
-    iota(["img"], T.ix[:, 32:48], [[1, 16]], 16)
-    iota(["imv"], T.ix[:, 64:72], [[1, 4], [8, 2]], 0)
-    iota(["idz"], T.ix[:, 80:96], [[-256, 2], [-2, 8]], 0)
+    iota(["idz"], T.ix[:, 80:96], [[0, 2], [2, 8]], 0)
+    iota(["zw3"], T.zw[:, 48:64], [[256, 2], [0, 8]], 0)
     for a in range(4):
         tp(["ld"], ["zt"], T.zt[32 * a:32 * a + 32, 0:32], T.ld[:], add=True)
     ts(["spr"], ["spn"], T.spn[0:1, :], T.spr[0:1, :], -1.0, A.mult, 0.5, A.add)
-    for h, n in enumerate(lists):
-        ts(["ps"], ["ps16"], P(16 + h), P(2), n - 1.0, A.min, 2.0, A.mult, add=True)
+    E("v", V.quantize_mx, ["zb"], ["zc", "zs"], T.zc[:], T.zs[:], T.zb[:])
     if NP:
         act(["zt", "mb"], ["m0b"], T.m0[:, 256:512], T.zt[:, 0:32].indirect(T.mb[:, 16:32]))
         copy(["zt", "mb"], ["m0a"], T.m0[:, 0:256], T.zt[:, 0:32].indirect(T.mb[:, 0:16]))
-    for h in range(NP):
-        lin(["ps16"], ["opv"], T.opv[:, 2 * h:2 * h + 1], P(4), 1.0, P(16 + h), True)
-    ts(["ps"], ["ps8"], P(8), P(3), 0.0, A.is_equal, 131072.0, A.mult)
-    ts(["ps"], ["ps14"], P(14), P(0), 0.0, A.is_equal, 32.0, A.mult)
+    for out, tok in ((T.vf, "vf"), (T.zw, "zw0")):
+        ts(["zt"], [tok], out[:, 0:16], T.zt[:, 0:16], -1.0, A.mult, 65536.0, A.add)
     if NP:
         tp(["m0a"], ["xu"], T.xu[:, 0:256], T.m0[:, 0:256], add=True)
         tp(["m0b"], ["xu"], T.xu[:, 256:512], T.m0[:, 256:512], add=True)
-    ts(["ps"], ["ps15"], P(15), P(2), 2.0, A.is_ge, 4.0, A.mult)
-    ts(["ps"], ["ps7"], P(7), P(0), -16.0, A.mult, P(1), A.subtract)
+    tt(["vf", "zw0"], ["zw1"], T.zw[:, 16:32], T.vf[:], T.zw[:, 0:16], A.subtract)
     ts(["ps"], ["ps26"], P(26), P(0), 4.0, A.min)
-    fill(["zb"], T.zb[:], 0.0)
+    ts(["ps"], ["ps24"], P(24), P(0), 0.0, A.is_equal)
     if NP:
         act(["img"], ["omg"], T.omg[:], T.ix[:, 32:48])
         act(["zt", "omg"], ["mg"], T.mg[:], T.zt[:, 0:32].indirect(T.omg[:, 0:16]))
-    lin(["ps14", "ps15"], ["ps6"], P(6), P(14), 1.0, P(15))
-    lin(["idz", "ps7"], ["ztc"], T.zt[:, 32:48], T.ix[:, 80:96], 1.0, P(7))
-    lin(["imv", "ps6"], ["omv"], T.omv[:], T.ix[:, 64:72], 1.0, P(6))
-    act(["zt", "ztc", "omv"], ["mv"], T.mv[:], T.zt[:, 0:48].indirect(T.omv[:, 0:8]), scale=-1.0)
+    lin(["ps15"], ["ps10"], P(10), P(5), 32.0, P(15))
+    lin(["idz", "ps7"], ["zw2"], T.zw[:, 32:48], T.ix[:, 80:96], 1.0, P(7))
+    lin(["ps10"], ["ps11"], P(11), P(6), 16.0, P(10))
+    lin(["imv", "ps11"], ["omv"], T.omv[:], T.ix[:, 64:72], 1.0, P(11))
+    act(["zw0", "zw1", "zw2", "zw3", "omv"], ["mv"], T.mv[:], T.zw[:, 0:64].indirect(T.omv[:, 0:8]))
     E("g", g.partition_broadcast, ["spn"], ["spb"], T.spb[:], T.spn[0:1, :], 128)
     for e in range(N - 1):
-        act(["zt", "spb"], ["d7"], T.d7[:, e:112:7], T.zt[0:32, 16:32], AF.Sign, True, bias=T.spb[0:32, e:e + 1])
-    iota(["ks4"], T.ks4[:], [[0, 68]], 0)
+        act(["zt", "spb"], ["d7"], T.d7[:, e:112:7], T.zt[0:64, 16:32], AF.Sign, True, bias=T.spb[0:64, e:e + 1])
+    iota(["ks4"], T.ks4[:, 0:1], [[0, 1]], 0)
     if not NP:
         iota(["ks4"], T.ks4[:, 1:17], [[0, 16]], 1)
-    if nq > 1:
-        iota(["rk4"], T.rk4[:, 0:16 * nq], [[0, 16], [-1, nq]], 1)
-    for n, c in (("d96", 20), ("pl", 64), ("cc", 64)):
-        iota([n], T[n][:], [[0, c]], 0)
+    for n, ap, c in (("d96", T.d96[:], 20), ("plz", T.pl[:], 64), ("cc", T.cc[:, 0:1], 1), ("nkz", T.nk[:, 0:1], 1)):
+        iota([n], ap, [[0, c]], 0)
     iota(["tr"], T.tr[:], [[1, 16]], 672, 16)
-    iota(["wi"], T.wi[:, 0:672], [[-1, 672]], -(66000 + 672 * s))
-    iota(["qi"], T.qi[:], [[0, 32]], 0)
+    iota(["wi"], T.wi[:, 0:672], [[0, 672]], 0)
+    iota(["hk"], T.hk[:, 3:4], [[0, 1]], 0)
+    iota(["qi"], T.qi[:, 3:128:4], [[0, 32]], 0)
     iota(["i8"], T.i8[:, 0:4], [[16, 2], [0, 2]], 0)
-    iota(["i8b"], T.i8[:, 4:8], [[8, 4]], 0)
     iota(["im2"], T.im[:, 20:40], [[0, 2], [1, 5], [0, 2]], 0)
     iota(["im"], T.im[:, 0:20], [[8, 2], [1, 5], [0, 2]], 1)
     iota(["ic"], T.ic[:], [[32, 5], [1, 16]], 0)
     iota(["ijf"], T.jf[:, 8:13], [[128, 5]], 512)
-    iota(["rz4"], T.rz4[:], [[0, 16], [1, 8]], 0)
-    iota(["cz"], T.cz[:, 135:256:8], [[0, 16]], 0)
+    iota(["cz"], T.cz[:, 3:128:4], [[0, 32]], 0)
     iota(["xk0"], T.xk[:, 0:16], [[0, 16]], 1)
     iota(["yfz"], T.yf[:, 0:16], [[0, 16]], 0)
     iota(["xkk"], T.xk[:, 16:656], [[-2, 4], [1, 2], [0, 80]] if odd else [[-1, 8], [0, 80]], -odd)
@@ -194,47 +204,39 @@ def rank_program(g, core, T, topo):
     lin(["ps26"], ["ps9"], P(9), P(2), 8.0, P(26))
     lin(["ps"], ["ps27"], P(27), P(1), 1.0, -2.5)
     lin(["ps"], ["ps28"], P(28), P(0), 8.0, 0.0)
-    lin(["ps"], ["ps10"], P(10), P(4), 32.0, P(5))
-    lin(["ps"], ["ps11"], P(11), P(4), -31.0, P(5))
     lin(["ps"], ["ps12"], P(12), P(1), 16.0, 16.0)
-    lin(["ps14"], ["ps24"], P(24), P(14), 1.0 / 32, 0.0)
-    for k, sign, half in ((20, 1.0, 0.0), (21, 1.0, 0.5), (22, -1.0, 0.0)):
+    for k, sign, half in ((20, 1.0, -65536.0), (21, 1.0, -65535.5), (22, -1.0, 0.0)):
         if s < N - 1: lin(["spb"], ["phi"], P(k), T.spb[:, s:s + 1], -sign, 0.5 * sign + half, True)
         else: lin(["ps"], ["phi"], P(k), P(0), 0.0, 65536.0 * sign + half, True)
     lin(["ps12"], ["ps13"], P(13), P(2), 160.0, P(12))
-    if nq > 1:
-        act(["rk4"], ["rk4"], T.rk4[:, 0:16 * nq], T.rk4[:, 0:16 * nq], AF.Relu)
 
     def first_slots():
         scan(["d7", "rs7"], ["d7s"], T.d7s[:], T.rs7[:], T.d7[:], 0.0, A.mult, A.add)
         lin(["d7s"], ["d96"], T.d96[:, 0:16], T.d7s[:, 6:112:7], 40.0, 280.0 + 16 * odd)
         act(["wi"], ["w2"], T.w2[:, 0:512], T.wi[:, 0:512], scale=0.0)
-        lin(["i8", "ps"], ["ody"], T.ody[:], T.i8[:, 0:4], 1.0, P(0))
-        lin(["i8b", "ps10"], ["oo2"], T.oo2[:], T.i8[:, 4:6], 1.0, P(10))
-        lin(["ps11"], ["ps23"], P(23), P(10 + odd), 1.0, 32.0 * odd)
-        lin(["i8b", "ps23"], ["oof"], T.oof[:], T.i8[:, 4:8], 1.0, P(23))
+
+    def constants():
         act(["im2", "ps27"], ["mh"], T.mh[:], T.im[:, 20:40], AF.Sign, bias=P(27))
+        lin(["i8", "ps"], ["ody"], T.ody[:], T.i8[:, 0:4], 1.0, P(0))
         lin(["ijf", "ps28"], ["jf"], T.jf[:, 0:5], T.jf[:, 8:13], 1.0, P(28))
-        act(["rz4"], ["rz4"], T.rz4[:], T.rz4[:], AF.Sign)
 
     def columns():
         ts(["ps13"], ["ps25"], P(25), P(0), 8.0, A.is_equal, P(13), A.mult)
         lin(["ic", "ps24", "ps25"], ["cst"], T.cst[:], T.ic[:], P(24), P(25))
 
-    E("v", V.quantize_mx, ["zb"], ["zc", "zs"], T.zc[:], T.zs[:], T.zb[:])
     if NP: later.append(lambda: tp(["mg"], ["xg"], T.xg[:], T.mg[:]))
     later += [
         first_slots,
         lambda: tp(["mv"], ["val"], T.val[:], T.mv[:]),
         lambda: ts(["ps"], ["ps18"], P(18), P(0), P(1), A.add, 3.0, A.is_ge),
-        columns,
-        lambda: ts(["ps9", "ps18"], ["ox6"], T.ox6[:, 0:1], P(18), 2.0, A.mult, P(9), A.add)]
+        lambda: ts(["ps9", "ps18"], ["ox6"], T.ox6[:, 0:1], P(18), 2.0, A.mult, P(9), A.add),
+        columns]
 
     if NP:
+        tot["rk"] = E_TABLE * higher
+        wr["rk"] = [("rk", None)]
         for h, n in enumerate(lists):
-            tot["rk%d" % h] = n
-            wr["rk%d" % h] = [("rk%d" % h, None)]
-            D("y", "dti%d" % h, T.ti[0:32 * n, 32 * h:32 * h + 32], T.kd[4 * h:4 * h + n], ["rk%d" % h, "ti"], ["tia%d" % h])
+            D("y", "dti%d" % h, T.ti[0:32 * n, 32 * h:32 * h + 32], T.kd[4 * h:4 * h + n], ["rk", "ti"], ["tia%d" % h])
     if sent:
         g.sync.wait_ge(T.sem.lk, sent)
     D("y", "dkc", T.kcs[:].bitcast(dt.uint8), T.kc[:], [], ["kcs"])
@@ -242,71 +244,74 @@ def rank_program(g, core, T, topo):
     D("y", "dw", T.wb[:], T.w[:], [], ["wb"])
     D("y", "dz", T.lc[:, 0:16].bitcast(dt.uint8), T.zc[:, 0:16].bitcast(dt.uint8), ["zc"], ["lcz"])
     D("y", "dz", T.ls[:, 0:16], T.zs[:, 0:16], ["zs"], ["lsz"])
-    kb = T.ks4[:, nq - 1:17 * nq:nq]
-    kept = T.ks4[:, 2 * nq - 1:17 * nq:nq]
+    kb, kept = T.ks4[:, 0:17], T.ks4[:, 1:17]
     if NP:
         n = 256 * NP
         def search(h):
             H, c, b = "%d" % h, 272 * h, 512 * h
-            tot["rp" + H] = sum(e_piv(r, s) for r in range(s + 1 + 4 * h, min(s + 5 + 4 * h, N)))
-            wr["rp" + H] = [("rp" + H, None)]
             return [
-                lambda: ts(["rp" + H, "opv", "ps8"], ["pvs" + H], T.pvs[:, 16 * h:16 * h + 16], T.pva[:, 8 * h:8 * h + 8].indirect(T.opv[:, 2 * h:2 * h + 1]), P(8), A.add),
-                lambda: ts(["xu", "pvs" + H], ["cm" + H], T.cm[:, b:b + 512], T.xu[:], T.pvs[:, 16 * h:16 * h + 1], A.subtract, T.pvs[:, 16 * h + 1:16 * h + 2], A.is_ge),
+                lambda: ts(["xu", "pvs"], ["cm" + H], T.cm[:, b:b + 512], T.xu[:], T.pvs[:, 2 * h:2 * h + 1], A.subtract, T.pvs[:, 2 * h + 1:2 * h + 2], A.is_ge),
                 lambda: tp(["cm" + H], ["ct" + H], T.ct[:, b:b + 512], T.cm[:, b:b + 512]),
                 lambda: scan(["ct" + H], ["cs" + H], T.cs[:, c + 1:c + 257], T.ct[:, b:b + 512:2], T.ct[:, b + 1:b + 512:2], 0.0, A.add, A.add),
                 lambda: tt(["cs" + H, "es0"], ["of" + H], T.of1[:, 16 * h:16 * h + 16], T.cs[:, c + 16:c + 257:16], T.cs[:, c:c + 256:16], A.subtract),
                 lambda: tt(["ti", "tia" + H, "of" + H, "xg"], ["eq" + H], T.eq[:, 256 * h:256 * h + 256], T.ti[:, 32 * h:32 * h + 32].indirect(T.of1[:, 16 * h:16 * h + 16]), T.xg[:], A.is_equal),
-                lambda: tp(["eq" + H], ["et"], T.et[:, 256 * h:256 * h + 256], T.eq[:, 256 * h:256 * h + 256], add=True)]
+                lambda: tp(["eq" + H], ["et"], T.et[:, h:n:NP], T.eq[:, 256 * h:256 * h + 256], add=True)]
         steps = [search(h) for h in range(NP)]
-        for k in range(7):
-            for p in steps: p[k]()
-            if k in (0, 5, 6): gap()
-        if NP == 2: w = 16; scan(["et"], ["es"], T.es[:, 1:257], T.et[:, 0:256], T.et[:, 256:512], 0.0, A.add, A.add)
-        else: w = 8; scan(["et"], ["es"], T.es[:, 1:129], T.et[:, 0:256:2], T.et[:, 1:256:2], 0.0, A.add, A.add)
+        tot["rp"] = E_FIRST * higher
+        wr["rp"] = [("rp", None)]
+        ts(["rp", "opv", "ps8"], ["pvs"], T.pvs[:], T.pva[:, 0:16].indirect(T.opv[:, 0:1]), P(8), A.add)
+        for k in range(6):
+            steps[0][k]()
+            if k == 3: gap()
+            if NP == 2: steps[1][k]()
+            if k >= 4: gap()
+        if higher > 2: scan(["et"], ["es"], T.es[:, 1:n + 1], T.et[0:64, 0:n], T.et[64:128, 0:n], 0.0, A.add, A.add)
+        else: n = 128; scan(["et"], ["es"], T.es[:, 1:n + 1], T.et[0:64, 0:256:2], T.et[0:64, 1:256:2], 0.0, A.add, A.add)
+        w = n // 16
+        if higher > 1:
+            tt(["es", "es0"], ["c4"], T.c4[:, 0:17], T.es[0:32, 0:n + 1:w], T.es[32:64, 0:n + 1:w], A.add)
+        now, before = (T.c4[:, 1:17], T.c4[:, 0:16]) if higher > 1 else (T.es[0:32, w:n + 1:w], T.es[0:32, 0:n:w])
+        for a in (0, 1):
+            tt(["c4", "es", "es0"], ["ks4"], T.ks4[32 * a:32 * a + 32, 1:17], now, before, A.is_equal, add=a > 0)
         gap()
-        for a in range(nq):
-            out, tok = (T.c4[:, a:16 * nq:nq], "c4") if nq > 1 else (kept, "ks4")
-            tt(["es", "es0"], [tok], out, T.es[32 * a:32 * a + 32, w:16 * w + 1:w], T.es[32 * a:32 * a + 32, 0:16 * w:w], A.is_equal, add=nq > 1)
-        gap()
-        if nq > 1:
-            scan(["c4", "rk4"], ["ks4"], T.ks4[:, nq:17 * nq], T.rk4[:, 0:16 * nq], T.c4[:, 0:16 * nq], 0.0, A.max, A.min)
-            gap()
     else:
         gap(3)
-    scan(["ks4", "d96"], ["pl"], T.pl[:, 32:49], kb, T.d96[:, 0:17], 0.0, A.add, A.max)
-    E("v", V.tensor_reduce, ["ks4"], ["pl"], T.pl[:, 16:17], kb, AxisListType.X, A.add, add=True)
-    ts(["ks4"], ["f1"], T.f1[:], kept, -4096.0, A.mult)
-    tp(["pl"], ["pt"], T.pt[:], T.pl[:])
-    tt(["f1", "tr"], ["nk"], T.nk[:], T.f1[:], T.tr[:], A.add)
+    scan(["ks4", "d96", "plz"], ["pl"], T.pl[:, 32:49], kb, T.d96[:, 0:17], 0.0, A.add, A.max)
+    act(["ks4", "plz"], ["pln"], T.nj[:], kept, accum_out=T.pl[:, 16:17])
+    constants()
+    ts(["ks4"], ["f1"], T.f1[:], kept, 0.0, A.is_equal)
+    tp(["pl", "pln"], ["pt"], T.pt[:], T.pl[:])
+    tt(["f1", "tr"], ["nk"], T.nk[:, 1:17], T.f1[:], T.tr[:], A.mult)
     scan(["pt"], ["cc"], T.cc[:, 1:33], T.pt[:, 0:32], T.pt[:, 32:64], 0.0, A.add, A.max)
-    gap()
+    tt(["ks4", "nk"], ["d0a"], T.dd[:, 0:16], T.ks4[:, 0:16], T.nk[:, 1:17], A.add)
+    tt(["d96", "nk"], ["d1"], T.dd[:, 32:48], T.d96[:, 0:16], T.nk[:, 1:17], A.add)
     tp(["cc"], ["cy"], T.cy[:], T.cc[:, 0:32])
-    tt(["im", "mh"], ["mo"], T.mo[:], T.im[:, 0:20], T.mh[:], A.add)
-    scan(["ks4", "d96", "cy"], ["pq"], T.pq[:], T.ks4[:, nq - 1:16 * nq:nq], T.d96[:, 0:16], T.cy[:, 16:17], A.add, A.max)
+    tt(["d0a", "nk", "nkz"], ["d0"], T.dd[:, 16:32], T.dd[:, 0:16], T.nk[:, 0:16], A.subtract)
+    for a in (0, 1):
+        scan(["d0", "d1", "cy"], ["pw"], T.pw[64 * a:64 * a + 64, 8 - 8 * a:24 - 8 * a], T.dd[:, 16:32], T.dd[:, 32:48], T.cy[:, 16:17], A.add, A.max, add=True)
     gap()
-    for a in range(4):
-        c = 8 * (a // 2)
-        tt(["pq", "nk"], ["pw"], T.pw[32 * a:32 * a + 32, :], T.pq[:, c:c + 8], T.nk[:, c:c + 8], A.max, add=True)
-    E("v", V.tensor_copy, ["pw", "val", "w2"], ["wi"], T.wi[:, 0:1184].indirect(T.pw[:, 0:8]), T.val[:])
-    tp(["wi"], ["wt"], T.wt[:], T.wi[:, 0:672])
-    tt(["wt"], ["hk"], T.hk[:, 0:21], T.wt[:, 1:672:32], T.wt[:, 17:672:32], A.max)
-    tt(["wt"], ["hi"], T.hk[:, 32:53], T.wt[:, 0:672:32], T.wt[:, 16:672:32], A.max)
+    E("v", V.tensor_copy, ["pw", "val", "w2"], ["wi"], T.wi[:, 0:2368].indirect(T.pw[:, 8:16]), T.val[:])
+    tt(["im", "mh"], ["mo"], T.mo[:], T.im[:, 0:20], T.mh[:], A.add)
+    nb32 = 20 + odd
+    tp(["wi"], ["wt"], T.wt[:, 0:32 * nb32], T.wi[:, 0:32 * nb32])
+    scan(["wt"], ["hk"], T.hk[:, 4:4 + 4 * nb32], T.wt[0:64, 0:32 * nb32:8], T.wt[64:128, 0:32 * nb32:8], 0.0, A.add, A.add)
     for k in (0, 1):
-        tt(["hk"], ["qk"], T.qk[64 * k:64 * k + 64, 0:21], T.hk[0:64, 0:21], T.hk[64:128, 0:21], A.max, add=True)
-    for k in (0, 1):
-        tt(["hi"], ["qi"], T.qi[64 * k:64 * k + 64, 0:21], T.hk[0:64, 32:53], T.hk[64:128, 32:53], A.max, add=k > 0)
+        tt(["hk"], ["qk"], T.qk[64 * k:64 * k + 64, 0:nb32], T.hk[:, 7:4 + 4 * nb32:4], T.hk[:, 3:4 * nb32:4], A.subtract, add=True)
+    scan(["wt"], ["qi"], T.qi[:, 4:4 + 4 * nb32], T.wt[0:64, 4:32 * nb32:8], T.wt[64:128, 4:32 * nb32:8], 0.0, A.add, A.add)
     peers = [(s + i) % N for i in range(1, N)]
     keys = lambda d: (T.kx[:, 4 * slot(s, d):4 * slot(s, d) + 3], T.qk[:, (5 * d + odd) // 2:(5 * d + odd) // 2 + 3])
     fused([(T.cores[d],) + keys(d) for d in peers], "rx%d" % wave(s), [2] * len(peers), ["qk"])
     act(["qk"], ["kx%d" % wave(s)], *keys(s))
-    tp(["qi"], ["xt"], T.xt[:], T.qi[:])
+    for k in (0, 1):
+        tp(["qi"], ["xt"], T.xt[64 * k:64 * k + 64, :], T.qi[:, 3:128:4], add=True)
     E("v", V.quantize_mx, ["wb"], ["wc", "wz"], T.wc[:], T.wz[:], T.wb[:])
     copy(["xt", "ody"], ["yy"], T.yy[:], T.xt[:, 0:32].indirect(T.ody[:, 0:4]))
     gap()
     tp(["yy"], ["ot"], T.ot[:], T.yy[:])
     gap()
-    copy(["ot", "oof"], ["off"], T.off[:], T.ot[:, 0:64].indirect(T.oof[:, 0:3]))
+    for e in (0, 1):
+        c = 32 * e + (odd > e)
+        tt(["ot"], ["off"], T.off[:, (e + odd) % 2:40:2], T.ot[:, c + 1:c + 21], T.ot[:, c:c + 20], A.subtract, add=True)
     gap()
     halves = [1 - s // 4, s // 4]
     codes_to = lambda d: (T.lc[:, 16 + 80 * slot(s, d):96 + 80 * slot(s, d)].bitcast(dt.uint8), T.qc[:, 80 * d:80 * d + 80].bitcast(dt.uint8))
@@ -318,82 +323,103 @@ def rank_program(g, core, T, topo):
         fused([(T.cores[d],) + to(d) for d in part], sem, [e] * len(part), toks)
         if a <= s < b: D("y", "d" + sem[:2], *to(s), toks, ["o" + sem[:2]])
 
+    far, near, me, nb = 4 * halves[0], 4 * halves[1], s - odd, (s - odd) ^ 2
+
     def codes(a, b):
         E("v", V.tensor_copy, ["off", "kcs"], ["qc%d" % a], T.qc[:, 80 * a:80 * b].bitcast(dt.uint32), T.kcs[:, 0:512].bitcast(dt.uint32).indirect(T.off[:, 5 * a:5 * b]))
+        send(a, b, codes_to, "rc", ["qc%d" % a])
 
     def scales(a, b, sem):
         act(["off", "kss"], ["qs%d" % a], T.qs[:, 80 * a:80 * b], T.kss[:, 0:512].indirect(T.off[:, 5 * a:5 * b]))
         send(a, b, scales_to, sem, ["qs%d" % a])
 
-    far, near, me, nb = 4 * halves[0], 4 * halves[1], s - odd, (s - odd) ^ 2
     codes(far, far + 4)
-    send(far, far + 4, codes_to, "rc", ["qc%d" % far])
-    scales(me, me + 2, "rs0")
     codes(me, me + 2)
-    codes(nb, nb + 2)
-    send(near, near + 4, codes_to, "rc", ["qc%d" % me, "qc%d" % nb])
-
-    if NP < 2: scales(far, far + 4, "rs2")
+    if NP < 2:
+        scales(me, me + 2, "rs0")
+        codes(nb, nb + 2)
+        scales(nb, nb + 2, "rs1")
     gap(len(later))
     for u in range(3):
         tot["rx%d" % u] = sum(2 for r in range(N) if r != s and wave(r) == u)
         wr["kx%d" % u] = wr.get("kx%d" % u, []) + [("rx%d" % u, None)]
     kxr, kxs = ["mo", "ox6", "phi"], ["kx0", "kx1", "kx2"]
     act(kxr + ["kx2"], ["mm2"], T.mm[:, 320:640], T.kx[:, 16:32].indirect(T.mo[:, 0:20]), AF.Identity, bias=P(20))
-    act(kxr + ["kx1"], ["mm1"], T.mm[:, 160:320], T.kx[:, 8:16].indirect(T.mo[:, 0:10]), AF.Identity, bias=P(20))
+    if NP == 2: scales(me, me + 2, "rs0")
+    if NP == 2: act(kxr + ["kx1"], ["mm1"], T.mm[:, 160:320], T.kx[:, 8:16].indirect(T.mo[:, 0:10]), AF.Identity, bias=P(20))
+    else: ts(kxr + ["kx1"], ["mm1"], T.mm[:, 160:320], T.kx[:, 8:16].indirect(T.mo[:, 0:10]), P(20), A.add)
     act(kxr + ["kx0"], ["mm0"], T.mm[:, 0:160], T.kx[:, 0:8].indirect(T.mo[:, 0:10]), AF.Identity, bias=P(20))
+    tp(["mm2"], ["xf2"], T.xf[:, 320:640], T.mm[:, 320:640])
+    if NP < 2: tp(["mm1"], ["xf1"], T.xf[:, 160:320], T.mm[:, 160:320])
     for out, tok in ((T.v6, "v6"), (T.v6b, "v6h")):
         ts(kxr + kxs, [tok], out[:, 0:16], T.kx[:, 0:32].indirect(T.ox6[:, 0:1]), P(21), A.add, 0.5, A.max)
-    tp(["mm2"], ["xf2"], T.xf[:, 320:640], T.mm[:, 320:640])
+    if NP == 2: tp(["mm1"], ["xf1"], T.xf[:, 160:320], T.mm[:, 160:320])
     ts(["v6"], ["pd"], T.pd[:, 0:5], T.v6[:, 0:5], 1.0, A.is_lt)
     tt(["v6", "v6h"], ["v6l"], T.v6b[:, 16:19], T.v6[:, 0:3], T.v6b[:, 0:3], A.subtract)
-    tp(["mm1"], ["xf1"], T.xf[:, 160:320], T.mm[:, 160:320])
     tp(["mm0"], ["xf0"], T.xf[:, 0:160], T.mm[:, 0:160])
-    tt(["pd", "jf"], ["pd2"], T.v6b[:, 20:23], T.pd[:, 0:3], T.jf[:, 0:3], A.mult)
     xs = ["xf0", "xf1", "xf2"]
-    for e in (3, 4):
-        act(xs + ["v6"], ["jk%d" % e, "sm%d" % e], T.jk[:, 640 * e - 1920:640 * e - 1280], T.xf[:], AF.Sign, scale=-1.0, bias=T.v6[:, e:e + 1], accum_out=T.sm[:, e:e + 1])
-    if NP == 2: scales(far, far + 4, "rs2")
-    scales(nb, nb + 2, "rs1")
-    act(xs + ["phi"], ["xkk"], T.xk[0:32, 16:656], T.xf[0:32, :], AF.Identity, bias=T.ps[0:32, 22:23])
-    for k in range(3):
-        ts(xs + ["v6l"], ["cb%d" % k], T.cb[:, 640 * k:640 * k + 640], T.xf[:], T.v6b[:, k:k + 1], A.subtract, T.v6b[:, 16 + k:17 + k], A.is_gt)
-    for e in (3, 4):
-        ts(["pd", "jf"], ["jt"], T.pd[:, 8 + e:9 + e], T.pd[:, e:e + 1], T.jf[:, e:e + 1], A.mult, 320.0, A.add, add=True)
+
+    def signs(e, a, b, col):
+        act(xs[a // 160:(b + 160) // 320 + 1] + ["v6"], ["jk%d" % col, "sm%d" % col], T.jk[:, 640 * e - 1920 + a:640 * e - 1920 + b], T.xf[:, a:b], AF.Sign,
+            scale=-1.0, bias=T.v6[:, e:e + 1], accum_out=T.sm[:, col:col + 1])
+
+    def larger(k, a, b):
+        ts(xs[a // 160:(b + 160) // 320 + 1] + ["v6l"], ["cb%d" % k], T.cb[:, 640 * k + a:640 * k + b], T.xf[:, a:b], T.v6b[:, k:k + 1], A.subtract, T.v6b[:, 16 + k:17 + k], A.is_gt, add=True)
+
+    signs(3, 160, 640, 2)
+    lin(["pd", "jf"], ["jt3"], T.pd[:, 11:12], T.pd[:, 3:4], T.jf[:, 3:4], 320.0)
+    lin(["pd", "jf"], ["jt4"], T.pd[:, 12:13], T.pd[:, 4:5], T.jf[:, 4:5], 320.0)
+    tt(["pd", "jf"], ["pd2"], T.v6b[:, 20:23], T.pd[:, 0:3], T.jf[:, 0:3], A.mult)
+    signs(3, 0, 160, 3)
+    lin(["sm2", "jt3"], ["jt2"], T.pd[:, 10:11], T.sm[:, 2:3], -0.5, T.pd[:, 11:12])
+    signs(4, 0, 640, 4)
+    for e, c in ((3, 2), (4, 4)):
+        lin(["sm%d" % e, "jt%d" % c], ["pu%d" % e], T.pu[:, 958 + e:959 + e], T.sm[:, e:e + 1], -0.5, T.pd[:, 8 + c:9 + c])
+    for k in range(3): larger(k, 160, 640)
+    for k in range(3): larger(k, 0, 160)
     for k in range(3):
         scan(["cb%d" % k, "pd2"], ["pu"], T.pu[:, 1 + k:959 + k:3], T.cb[:, 640 * k:640 * k + 320], T.cb[:, 640 * k + 320:640 * k + 640], T.v6b[:, 20 + k:21 + k], A.add, A.add, add=True)
-        if k:
-            ts(["sm%d" % (2 + k), "jt"], ["pu"], T.pu[:, 960 + k:961 + k], T.sm[:, 2 + k:3 + k], -0.5, A.mult, T.pd[:, 10 + k:11 + k], A.add, add=True)
-    E("v", V.tensor_copy, ["pu", "cst"], ["w2"], T.w2[:, 0:1664].indirect(T.pu[:, 958:963]), T.cst[:])
+    if NP == 2: codes(nb, nb + 2)
+    scales(far, far + 4, "rs2")
+    if NP == 2: scales(nb, nb + 2, "rs1")
+    act(xs + ["phi"], ["xkk"], T.xk[0:32, 16:656], T.xf[0:32, :], AF.Identity, bias=T.ps[0:32, 22:23])
+    E("v", V.tensor_copy, ["pu", "pu3", "pu4", "cst"], ["w2"], T.w2[:, 0:1664].indirect(T.pu[:, 958:963]), T.cst[:])
     tp(["w2"], ["w2t"], T.w2t[:], T.w2[:, 0:512])
-    for a in range(4):
-        tt(["w2t"], ["c5"], T.c5[:, a:128:4], T.w2t[32 * a:32 * a + 32, 0:512:16], T.w2t[32 * a:32 * a + 32, 8:512:16], A.add, add=True)
-    scan(["c5", "rz4"], ["cz"], T.cz[:, 0:128], T.rz4[:], T.c5[:], 0.0, A.mult, A.add)
-    for a in range(4):
-        tp(["cz"], ["sx"], T.sx[32 * a:32 * a + 32, :], T.cz[:, 7:256:8], add=True)
+    tt(["w2t"], ["c5"], T.c5[:], T.w2t[0:64, 0:512:8], T.w2t[64:128, 0:512:8], A.add)
+    for a in (0, 1):
+        scan(["c5"], ["cz"], T.cz[32 * a:32 * a + 32, 4:68], T.c5[0:32, :], T.c5[32:64, :], 0.0, A.add, A.add, add=a > 0)
+    for a in (0, 1):
+        tp(["cz"], ["sx"], T.sx[64 * a:64 * a + 64, :], T.cz[:, 3:128:4], add=True)
     copy(["sx", "ody"], ["sy"], T.sy[:], T.sx[:, 0:32].indirect(T.ody[:, 0:4]))
     tp(["sy"], ["so"], T.so[:], T.sy[:])
-    copy(["so", "oo2"], ["of2"], T.of2[:], T.so[:, 0:64].indirect(T.oo2[:, 0:2]))
-    tot["rc"] = 4 * (N - 1)
+    for e in (0, 1):
+        tt(["so"], ["of2"], T.of2[:, e:32:2], T.so[:, 32 * e + 1:32 * e + 17], T.so[:, 32 * e:32 * e + 16], A.subtract, add=True)
+    tot["rc"] = 8 + 16 + 16
     wr["lca"] = [("rc", None)]
     land, lands = ["lca", "orc", "lcz"], ["ls0", "ls1", "ls2", "ors", "lsz"]
-    for k in (0, 2, 1):
-        r, n = ((me, 160), (nb, 160), (far, 320))[k]
+    for k in range(3):
         tot["rs%d" % k] = 16 if k else 8
         wr["ls%d" % k] = [("rs%d" % k, None)]
-        c = 16 + 80 * r
-        E("t", g.tensor.matmul_mx, land + ["ls%d" % k, "ors", "wc", "wz"], ["acc%d" % k], T.acc[:, 512 * k:512 * k + n], T.wc[:], T.wz[:], T.lc[:, c:c + n], T.ls[:, c:c + n], True, True)
-        act(["acc%d" % k], ["yf%d" % k], T.yf[:, c:c + n], T.acc[:, 512 * k:512 * k + n])
-    for k, (a, b) in enumerate(CHUNKS):
-        o = T.of2[:, a // 16:b // 16]
-        E("v", V.tensor_copy, land + ["of2"], ["fc%d" % k], T.fc[:, a:b].bitcast(dt.uint32), T.lc[:, 0:656].bitcast(dt.uint32).indirect(o))
+    for k in ((0, 1, 2, 3) if far < near else (0, 2, 3, 1)):
+        c = 16 + 80 * (me, nb, far, far + 2)[k]
+        E("t", g.tensor.matmul_mx, land + ["ls%d" % min(k, 2), "ors", "wc", "wz"], ["acc%d" % k], T.acc[:, 512 * k:512 * k + 160], T.wc[:], T.wz[:], T.lc[:, c:c + 160], T.ls[:, c:c + 160], True, True)
+        act(["acc%d" % k], ["yf"], T.yf[:, c:c + 160], T.acc[:, 512 * k:512 * k + 160], add=True)
+    def codes_out(k, a, b):
+        E("v", V.tensor_copy, land + ["of2"], ["fc%d" % k], T.fc[:, a:b].bitcast(dt.uint32), T.lc[:, 0:656].bitcast(dt.uint32).indirect(T.of2[:, a // 16:b // 16]))
         D("y", "doc%d" % k, T.oc[:, 4 * a:4 * b], T.fc[:, a:b].bitcast(dt.uint8), ["fc%d" % k], ["oc"])
-        if b == 512:
-            act(lands + ["of2"], ["fz"], T.fz[:], T.ls[:, 0:656].indirect(T.of2[:, 0:32]))
-            for j in range(4):
-                D("y", "dos", T.osc[4 * j:4 * j + 4, :], T.fz[32 * j:32 * j + 4, :], ["fz"], ["osc"])
-        act(["yfz", "yf0", "yf1", "yf2", "of2"], ["yo%d" % k], T.yo[:, a:b], T.yf[:, 0:656].indirect(o))
-        D("s" if b == 512 else "y", "dy%d" % k, T.y[:, a:b], T.yo[:, a:b], ["yo%d" % k], ["y"])
+
+    def y_out(k, a, b, q):
+        act(["yfz", "yf", "of2"], ["yo%d" % k], T.yo[:, a:b], T.yf[:, 0:656].indirect(T.of2[:, a // 16:b // 16]))
+        D(q, "dy%d" % k, T.y[:, a:b], T.yo[:, a:b], ["yo%d" % k], ["y"])
+
+    codes_out(0, 0, 192)
+    y_out(1, 0, 448, "y")
+    codes_out(1, 192, 512)
+    act(lands + ["of2"], ["fz"], T.fz[:], T.ls[:, 0:656].indirect(T.of2[:, 0:32]))
+    act(["yfz", "yf", "of2"], ["yo2"], T.yo[:, 448:512], T.yf[:, 0:656].indirect(T.of2[:, 28:32]))
+    for j in range(4):
+        D("ys"[j % 2], "dos", T.osc[4 * j:4 * j + 4, :], T.fz[32 * j:32 * j + 4, :], ["fz"], ["osc"])
+    D("s", "dy2", T.y[:, 448:512], T.yo[:, 448:512], ["yo2"], ["y"])
     ts(["xkk", "xk0", "of2"], ["ko"], T.ko[:], T.xk[:, 0:656].indirect(T.of2[:, 0:32]), -1.0, A.mult)
     D("y", "dok", T.ok[:], T.ko[0:64:32, :], ["ko"], ["ok"])
     for n in SEMAPHORES:

@@ -3,23 +3,28 @@ from concourse.mybir import dt, AluOpType, AxisListType, ActivationFunctionType
 
 SCRATCH = {"mykd": ("dram", [128, 8], "int32"), "kd": ("dram", [7, 128, 8], "int32"), "acc": ("psum", [128, 2048], "float32")}
 SIZES = {
-    (128, "float32"): "vf:16 ps:32 ix:96 im:40 mh:20 ic:80 i8:4 qk:24 "
-                      "spb:16 xt:32 yy:64 ot:64 kx:32 xk:656 v6:16 pd:16 jf:16 sm:8 sx:32 sy:64 so:64 yf:656 yo:512 ko:512",
+    (128, "float32"): "vf:16 ps:48 ix:96 im:40 mh:20 ic:80 i8:16 qk:24 j3:80 "
+                      "spb:16 kx:32 xk:656 v6:32 pd:16 jf:24 sm:8 o2f:32 yf:656 yo:512 ko:128",
     (64, "bfloat16"): "d7:112 d7s:112 rs7:112 es:528", (32, "float32"): "spn:16 c4:20",
-    (64, "float32"): "tr:16 d96:20 ks4:20 f1:16 nk:20 dd:48 pl:64 pt:64 cc:64 cy:32 hk:88 qi:128 nj:16 c5:64 cz:128",
-    (128, "bfloat16"): "zw:64 mv:128 val:128 wi:2368 wt:672 pvs:16 v6b:24 cm:1024 ct:1024 eq:512 et:512 zb:512 wb:512 jk:1280 cb:1920 w2:1664 w2t:512 cst:80",
+    (64, "float32"): "tr:64 d96:20 ks4:20 f1:16 nk:20 dd:112 pl:24 pt:64 tri:32 hk:88 qi:84 nj:16 so:33 cz:132",
+    (128, "bfloat16"): "zw:64 mv:128 val:128 wi:2384 wt:1312 yy:80 sy:128 pvs:16 v6b:24 cm:1024 ct:1024 eq:512 et:512 zb:544 wb:512 jk:1280 cb:2080 w2:1744 w2t:1184 cst:80",
     (128, "float16"): "cs:544",
-    (128, "int32"): "ti:64 pi:8 zt:32 pv:4 pva:16", (32, "int32"): "ld:32 spr:16",
-    (128, "uint16"): "opv:4 m0:512 xu:512 mg:256 xg:256 of1:32 mb:32 mo:20 omg:16 omv:8 ox6:2 ody:4 pw:24 off:40 pu:964 of2:32 mm:640 xf:640",
+    (128, "int32"): "ti:80 pi:12 zt:32 pv:4 pva:128", (32, "int32"): "ld:32 spr:16",
+    (128, "uint16"): "oq:2 og:16 opv:4 m0:512 xu:512 mg:256 xg:256 of1:32 mb:32 mo:20 omg:16 omv:8 ox6:4 ogs:16 pw:56 off:40 pu:964 of2:32 mm:640 xf:640",
     (128, "float8_e4m3fn_x4"): "zc:128 kcs:512 qc:640 lc:656 fc:512 wc:128",
     (128, "uint8"): "zs:128 kss:512 qs:640 ls:672 fz:512 wz:128"}
 for (_p, _d), _l in SIZES.items():
     for _x in _l.split():
         SCRATCH[_x.split(":")[0]] = ("sbuf", [_p, int(_x.split(":")[1])], _d)
-SEMAPHORES = ["gs", "dk", "dt", "dsp", "dpv", "lk", "rk", "rp", "dti0", "dti1", "dw", "dkc", "dz", "rx0", "rx1", "rx2", "drc", "drs", "rc", "rs0", "rs1", "rs2",
-              "loc", "ts", "vs", "ss", "doc0", "dy0", "doc1", "dy1", "doc2", "dos", "dok", "dy2"]
+SEMAPHORES = ["gs", "dk", "dt", "dsp", "dpv", "lk", "rk", "rp", "dti0", "dti1", "dw", "dkc", "dz", "rx0", "rx1", "rx2", "drc", "drs", "rc0", "rs0", "rc1", "rs1", "rc2", "rs2",
+              "loc", "ts", "vs", "ss", "dout"]
 E_TABLE, E_FIRST = 4, 8
-CHUNKS = ((0, 96), (96, 352), (352, 512))
+ORDER = "m2 c0 m1 c1 c2 t2 s1 t1 m0 r h t0 x G A e0 p H J g4 K f4 e1 e2 l0 l1 l2 z0 z1 z2 s0 s2"
+EARLY = "c0 s1 c1 s2 c2 m2 s0 n1 t2 t1 m0 r h t0 x G A e0 p H J g4 K f4 e1 e2 l0 l1 l2 z0 z1 z2"
+LAST = (1, 2, 3, 0)
+TWO = 3
+DOWN = (("table", 0, 1), ("first", 0, TWO), ("first", TWO, 7), ("table", 1, 7))
+PIECES = ((0, 192), (192, 512))
 
 
 def rank_program(g, core, T, topo):
@@ -99,12 +104,13 @@ def rank_program(g, core, T, topo):
         g.remote_dma_fused(tr, local_sem=T.sem.loc)
         tot["loc"] += sum(per)
 
-    def to_lower(dst, src, sem, per, r):
+    def to_lower(dst, src, sem, per, r, ranks):
+        if not ranks: return
         need("g", r, [])
-        ids = [DstId(rid=topo.addr(c)[0], pnc=topo.addr(c)[1]) for c in T.cores[:s]]
+        ids = [DstId(rid=topo.addr(T.cores[d])[0], pnc=topo.addr(T.cores[d])[1]) for d in ranks]
         mask = sum(1 << k for k in topo.engines(core, T.cores[0])[:per])
         g.remote_dma_fused([RemoteDMATransfer(dst_ids=ids, dma_engine_mask=mask, remote_sem=T.sem[sem], srcs=[src],
-                                              dsts=[dst(s - d - 1) for d in range(s)])], local_sem=T.sem.lk)
+                                              dsts=[dst(s - d - 1) for d in ranks])], local_sem=T.sem.lk)
         tot["lk"] += per
 
     higher = N - 1 - s
@@ -119,7 +125,7 @@ def rank_program(g, core, T, topo):
         for k in (0, 1):
             D("ys"[k], "dk", T.mykd[64 * k:64 * k + 64, :], T.ky[:], [], ["mykd"])
         for a in range(4):
-            D("ys"[a % 2], "dpv", T.pv[32 * a:32 * a + 32, 0:1], T.ky[0:1, :], [], ["pv"])
+            D("ys"[a % 2], "dpv", T.pv[32 * a:32 * a + 32, 2:3], T.ky[0:1, :], [], ["pv"])
     for k in (0, 1):
         D("ys"[k], "dt", T.ld[8 * k:8 * k + 8, :], T.ky[:, 16 * k:16 * k + 16], [], ["ld"])
     D("y", "dt", T.ld[16:32, :], T.ky[:], [], ["ld"])
@@ -129,37 +135,38 @@ def rank_program(g, core, T, topo):
     iota(["imb"], T.ix[:, 0:32], [[1, 8], [8, 2], [0, 2]], 0)
     iota(["img"], T.ix[:, 32:48], [[1, 16]], 16)
     iota(["imv"], T.ix[:, 64:72], [[1, 4], [8, 2]], 0)
-    for h, n in enumerate(lists):
-        for a in range(n, 4):
-            fill(["ti"], T.ti[32 * a:32 * a + 32, 32 * h:32 * h + 32], -1, add=True)
+    if NP:
+        fill(["ti"], T.ti[:], -1)
+        if NP == 2:
+            for k in (4, 5): fill(["pv0"], T.pva[:, 32 * lists[1] + k:128:32], 0, add=True)
+        elif higher < 4:
+            fill(["pv0"], T.pva[:, 32 * higher:128], 0)
     fill(["rs7"], T.rs7[:], 1.0)
-    for k, (sh, m) in enumerate(((0, 15), (4, 1), (5, 3), (0, 31), (0, 1), (2, 1), (3, 1))):
+    for k, (sh, m) in enumerate(((0, 15), (4, 1), (5, 3), (4, 4), (0, 97 + 4 * (NP == 2)), (2, 1), (3, 1), (1, 24), (0, 3))):
         ts(["pi"], ["pi%d" % k], T.pi[:, 1 + k:2 + k], T.pi[:, 0:1], sh, A.logical_shift_right, m, A.bitwise_and)
     fill(["rs7"], T.rs7[:, 0:112:7], 0.0)
     fill(["es0"], T.es[:, 0:1], 0.0)
-    copy(["pi%d" % k for k in range(7)], ["ps"], T.ps[:, 0:7], T.pi[:, 1:8])
+    copy(["pi%d" % k for k in range(9)], ["ps"], T.ps[:, 0:9], T.pi[:, 1:10])
     fill(["es0"], T.cs[:, 0:273:272], 0.0, add=True)
-    fill(["zb"], T.zb[:], 0.0)
+    fill(["zb"], T.zb[:, 0:256], 0.0)
     act(["imb"], ["mb"], T.mb[:], T.ix[:, 0:32])
-    ts(["ps"], ["ps16"], P(16), P(0), 2.0, A.is_ge, 4.0, A.mult)
-    ts(["ps"], ["ps8"], P(8), P(3), 0.0, A.is_equal, 131072.0, A.mult)
-    ts(["ps"], ["ps15"], P(15), P(2), 2.0, A.is_ge, 4.0, A.mult)
-    ts(["ps"], ["ps7"], P(7), P(0), 16.0, A.mult, P(1), A.add)
-    if NP:
-        ts(["ps16"], ["ps17"], P(17), P(16), P(2), A.add, higher - 1.0, A.min)
-        lin(["ps17"], ["opv"], T.opv[:, 0:1], P(17), 2.0, P(4))
+    act(["img"], ["omg"], T.omg[:], T.ix[:, 32:48])
+    act(["pi4"], ["opv"], T.opv[:, 0:1], T.pi[:, 5:6])
     if s > 0:
         for k, m in enumerate((0xFF00, 0xFF)):
-            ts(["pv"], ["pvh"], T.pv[:, 2 + k:3 + k], T.pv[:, 0:1], m, A.bitwise_and, add=True)
-        to_lower(lambda i: T.kd[i], T.mykd[:], "rk", E_TABLE, ["mykd"])
-        to_lower(lambda i: T.pva[:, 2 * i:2 * i + 2], T.pv[:, 2:4], "rp", E_FIRST, ["pvh"])
+            ts(["pv"], ["pvh"], T.pv[:, k:k + 1], T.pv[:, 2:3], m, A.bitwise_and, add=True)
+        for what, a, b in DOWN:
+            if what == "table": to_lower(lambda i: T.kd[i], T.mykd[:], "rk", E_TABLE, ["mykd"], range(s)[a:b])
+            else: to_lower(lambda i: T.pva[:, 32 * (i % 4) + 4 * (i // 4):32 * (i % 4) + 4 * (i // 4) + 2], T.pv[:, 0:2], "rp", E_FIRST, ["pvh"], range(s)[a:b])
     sent = tot["lk"]
-    iota(["idz"], T.ix[:, 80:96], [[0, 2], [2, 8]], 0)
+    iota(["idz"], T.ix[:, 80:96], [[256, 2], [2, 8]], -255)
     iota(["zw3"], T.zw[:, 48:64], [[256, 2], [0, 8]], 0)
+    lin(["ps"], ["ps10"], P(10), P(5), 32.0, P(3))
+    lin(["ps"], ["ps14"], P(14), P(0), 16.0, P(1))
+    lin(["ps"], ["p85"], T.v6b[:, 23:24], P(5), 85.0, 0.0)
     for a in range(4):
         tp(["ld"], ["zt"], T.zt[32 * a:32 * a + 32, 0:32], T.ld[:], add=True)
     ts(["spr"], ["spn"], T.spn[0:1, :], T.spr[0:1, :], -1.0, A.mult, 0.5, A.add)
-    E("v", V.quantize_mx, ["zb"], ["zc", "zs"], T.zc[:], T.zs[:], T.zb[:])
     if NP:
         act(["zt", "mb"], ["m0b"], T.m0[:, 256:512], T.zt[:, 0:32].indirect(T.mb[:, 16:32]))
         copy(["zt", "mb"], ["m0a"], T.m0[:, 0:256], T.zt[:, 0:32].indirect(T.mb[:, 0:16]))
@@ -169,102 +176,131 @@ def rank_program(g, core, T, topo):
         tp(["m0a"], ["xu"], T.xu[:, 0:256], T.m0[:, 0:256], add=True)
         tp(["m0b"], ["xu"], T.xu[:, 256:512], T.m0[:, 256:512], add=True)
     tt(["vf", "zw0"], ["zw1"], T.zw[:, 16:32], T.vf[:], T.zw[:, 0:16], A.subtract)
-    ts(["ps"], ["ps26"], P(26), P(0), 4.0, A.min)
-    ts(["ps"], ["ps24"], P(24), P(0), 0.0, A.is_equal)
-    if NP:
-        act(["img"], ["omg"], T.omg[:], T.ix[:, 32:48])
-        act(["zt", "omg"], ["mg"], T.mg[:], T.zt[:, 0:32].indirect(T.omg[:, 0:16]))
-    lin(["ps15"], ["ps10"], P(10), P(5), 32.0, P(15))
-    lin(["idz", "ps7"], ["zw2"], T.zw[:, 32:48], T.ix[:, 80:96], 1.0, P(7))
     lin(["ps10"], ["ps11"], P(11), P(6), 16.0, P(10))
+    if NP: act(["zt", "omg"], ["mg"], T.mg[:], T.zt[:, 0:32].indirect(T.omg[:, 0:16]))
     lin(["imv", "ps11"], ["omv"], T.omv[:], T.ix[:, 64:72], 1.0, P(11))
+    if NP:
+        tot["rp"] = E_FIRST * higher
+        wr["rp"] = [("rp", None)]
+    lin(["idz", "ps14"], ["zw2"], T.zw[:, 32:48], T.ix[:, 80:96], 1.0, P(14))
     act(["zw0", "zw1", "zw2", "zw3", "omv"], ["mv"], T.mv[:], T.zw[:, 0:64].indirect(T.omv[:, 0:8]))
+    def first_fills():
+        iota(["ks4"], T.ks4[:, 0:1], [[0, 1]], 0)
+        if not NP:
+            iota(["ks4"], T.ks4[:, 1:17], [[0, 16]], 1)
+        for n, ap, c in (("d96", T.d96[:], 20), ("nkz", T.nk[:, 0:1], 1)):
+            iota([n], ap, [[0, c]], 0)
+        iota(["tri0"], T.tri[:], [[1, 32]], 0, -1)
+
+    if s == 0: first_fills()
     E("g", g.partition_broadcast, ["spn"], ["spb"], T.spb[:], T.spn[0:1, :], 128)
     for e in range(N - 1):
         act(["zt", "spb"], ["d7"], T.d7[:, e:112:7], T.zt[0:64, 16:32], AF.Sign, True, bias=T.spb[0:64, e:e + 1])
-    iota(["ks4"], T.ks4[:, 0:1], [[0, 1]], 0)
-    if not NP:
-        iota(["ks4"], T.ks4[:, 1:17], [[0, 16]], 1)
-    for n, ap, c in (("d96", T.d96[:], 20), ("plz", T.pl[:], 64), ("cc", T.cc[:, 0:1], 1), ("nkz", T.nk[:, 0:1], 1)):
-        iota([n], ap, [[0, c]], 0)
-    iota(["tr"], T.tr[:], [[1, 16]], 672, 16)
-    iota(["wi"], T.wi[:, 0:672], [[0, 672]], 0)
-    iota(["hk"], T.hk[:, 3:4], [[0, 1]], 0)
-    iota(["qi"], T.qi[:, 3:128:4], [[0, 32]], 0)
-    iota(["i8"], T.i8[:, 0:4], [[16, 2], [0, 2]], 0)
+    if s > 0: first_fills()
+    iota(["tr"], T.tr[:, 0:17], [[1, 17]], 672, 16)
+    iota(["trc"], T.tr[:, 32:33], [[0, 1]], 672, 16)
+    iota(["trd"], T.tr[:, 33:48], [[0, 15]], 1)
+    if NP:
+        tot["rk"] = E_TABLE * higher
+        wr["rk"] = [("rk", None)]
+    iota(["zb2"], T.zb[:, 256:544], [[0, 288]], 0)
+    iota(["i5"], T.i8[:, 10:15], [[128, 5]], -700)
+    iota(["i8"], T.i8[:, 0:8], [[64, 8]], 0)
     iota(["im2"], T.im[:, 20:40], [[0, 2], [1, 5], [0, 2]], 0)
-    iota(["im"], T.im[:, 0:20], [[8, 2], [1, 5], [0, 2]], 1)
-    iota(["ic"], T.ic[:], [[32, 5], [1, 16]], 0)
     iota(["ijf"], T.jf[:, 8:13], [[128, 5]], 512)
-    iota(["cz"], T.cz[:, 3:128:4], [[0, 32]], 0)
+    iota(["ic"], T.ic[:], [[32, 5], [1, 16]], 0)
+    iota(["im"], T.im[:, 0:20], [[8, 2], [1, 5], [0, 2]], 1)
+    iota(["hk"], T.hk[:, 3:4], [[0, 1]], 0)
+    iota(["qi"], T.qi[:, 3:4], [[0, 1]], 0)
+    iota(["cz"], T.cz[:, 3:4], [[0, 1]], 0)
     iota(["xk0"], T.xk[:, 0:16], [[0, 16]], 1)
     iota(["yfz"], T.yf[:, 0:16], [[0, 16]], 0)
     iota(["xkk"], T.xk[:, 16:656], [[-2, 4], [1, 2], [0, 80]] if odd else [[-1, 8], [0, 80]], -odd)
 
-    lin(["ps26"], ["ps9"], P(9), P(2), 8.0, P(26))
-    lin(["ps"], ["ps27"], P(27), P(1), 1.0, -2.5)
-    lin(["ps"], ["ps28"], P(28), P(0), 8.0, 0.0)
-    lin(["ps"], ["ps12"], P(12), P(1), 16.0, 16.0)
-    for k, sign, half in ((20, 1.0, -65536.0), (21, 1.0, -65535.5), (22, -1.0, 0.0)):
-        if s < N - 1: lin(["spb"], ["phi"], P(k), T.spb[:, s:s + 1], -sign, 0.5 * sign + half, True)
-        else: lin(["ps"], ["phi"], P(k), P(0), 0.0, 65536.0 * sign + half, True)
-    lin(["ps12"], ["ps13"], P(13), P(2), 160.0, P(12))
+    def numbers():
+        for k, src, fn, scale, bias in ((27, 1, AF.Identity, 1.0, -2.5), (28, 0, AF.Identity, 8.0, 0.0), (19, 6, AF.Identity, -8.0, P(0)), (16, 5, AF.Identity, -1.0, P(1)),
+                                        (29, 0, AF.Relu, -1.0, 4.0), (9, 8, AF.Relu, -1.0, 1.0), (17, 2, AF.Identity, 8.0, 5.0), (12, 1, AF.Identity, 16.0, 16.0),
+                                        (23, 0, AF.Identity, 4.0, 676.0), (41, 2, AF.Identity, -32.0, 0.0)):
+            act(["ps"], ["ps%d" % k], P(k), P(src), fn, scale=scale, bias=bias)
+        for k, n, add in ((20, 128, -65536.0), (21, 128, -65535.5), (22, 64, 0.0)):
+            if s < N - 1: lin(["spb"], ["phi"], T.ps[0:n, k:k + 1], T.spb[0:n, s:s + 1], -1.0, 0.5 + add, True)
+            else: lin(["ps"], ["phi"], T.ps[0:n, k:k + 1], T.ps[0:n, 0:1], 0.0, 65536.0 + add, True)
+        lin(["ps"], ["phi"], T.ps[64:128, 22:23], T.ps[64:128, 0:1], 0.0, 0.0, True)
+        for a, b in ((0, 256), (256, 672)) * (NP // 2):
+            lin(["p85", "zb", "zb2"][:2 + a // 256], ["wi"], T.wi[:, a:b], T.zb[:, 0:b - a], 1.0, T.v6b[:, 23:24], True)
 
     def first_slots():
         scan(["d7", "rs7"], ["d7s"], T.d7s[:], T.rs7[:], T.d7[:], 0.0, A.mult, A.add)
-        lin(["d7s"], ["d96"], T.d96[:, 0:16], T.d7s[:, 6:112:7], 40.0, 280.0 + 16 * odd)
-        act(["wi"], ["w2"], T.w2[:, 0:512], T.wi[:, 0:512], scale=0.0)
+        lin(["d7s"], ["d96"], T.d96[:, 0:16], T.d7s[:, 6:112:7], 40.0, 296.0)
 
     def constants():
         act(["im2", "ps27"], ["mh"], T.mh[:], T.im[:, 20:40], AF.Sign, bias=P(27))
-        lin(["i8", "ps"], ["ody"], T.ody[:], T.i8[:, 0:4], 1.0, P(0))
-        lin(["ijf", "ps28"], ["jf"], T.jf[:, 0:5], T.jf[:, 8:13], 1.0, P(28))
+        lin(["ps23"], ["ps31"], P(31), P(8), 4.0, P(23))
+        act(["ps"], ["ps35"], P(35), P(8), AF.Sign, bias=-1.5)
+        lin(["ps"], ["ps36"], P(36), P(1), 1.0, -0.5)
+        act(["ps27"], ["ps18"], P(18), P(0), AF.Sign, bias=P(27))
+        lin(["ps31"], ["ps33"], P(33), P(1), -16.0, P(31))
+        lin(["ps9"], ["ps32"], P(32), P(9), P(5), 0.0)
+        act(["ps35", "ps36"], ["ps37"], P(37), P(35), AF.Square, scale=-0.5, bias=P(36))
+        lin(["ps33", "ps12"], ["ps38"], P(38), P(33), 2.0, P(12))
+        lin(["ps29", "ps17"], ["ps26"], P(26), P(29), -1.0, P(17))
+        lin(["ps32"], ["ps15"], P(15), P(32), P(6), 0.0)
+        lin(["ps38", "ps35"], ["ps39"], P(39), P(35), -8.0, P(38))
+        lin(["ps12"], ["ps13"], P(13), P(2), 160.0, P(12))
+        lin(["ps18", "ps26"], ["ox6"], T.ox6[:, 0:1], P(18), 1.0, P(26))
+        lin(["ps39", "ps37"], ["ps40"], P(40), P(37), -656.0, P(39))
+        lin(["ps15", "ps32"], ["ps24"], P(24), P(15), -1.0, P(32))
+        lin(["ps13", "ps15"], ["ps25"], P(25), P(13), P(15), 0.0)
+        lin(["i5", "ps40"], ["ogt"], T.ogs[:, 10:15], T.i8[:, 10:15], 1.0, P(40))
+        act(["zb", "zb2"], ["w2"], T.w2[:, 0:544], T.zb[:])
 
     def columns():
-        ts(["ps13"], ["ps25"], P(25), P(0), 8.0, A.is_equal, P(13), A.mult)
+        act(["ps16"], ["ps30"], P(30), P(16), AF.Square)
+        lin(["ijf", "ps28"], ["jf"], T.jf[:, 0:5], T.jf[:, 8:13], 1.0, P(28))
+        lin(["ps19"], ["oq"], T.oq[:, 0:1], P(19), 1.0, P(7))
+        lin(["ps30", "ps33"], ["ps34"], P(34), P(30), -656.0, P(33))
+        lin(["xk0", "phi"], ["xk0"], T.xk[:, 0:16], T.xk[:, 0:16], 1.0, P(22))
         lin(["ic", "ps24", "ps25"], ["cst"], T.cst[:], T.ic[:], P(24), P(25))
+        lin(["i8", "ps34"], ["ogs"], T.ogs[:, 0:8], T.i8[:, 0:8], 1.0, P(34))
 
-    if NP: later.append(lambda: tp(["mg"], ["xg"], T.xg[:], T.mg[:]))
-    later += [
-        first_slots,
-        lambda: tp(["mv"], ["val"], T.val[:], T.mv[:]),
-        lambda: ts(["ps"], ["ps18"], P(18), P(0), P(1), A.add, 3.0, A.is_ge),
-        lambda: ts(["ps9", "ps18"], ["ox6"], T.ox6[:, 0:1], P(18), 2.0, A.mult, P(9), A.add),
-        columns]
+    lanes = lambda: tp(["mg"], ["xg"], T.xg[:], T.mg[:])
+    values = lambda: tp(["mv"], ["val"], T.val[:], T.mv[:])
+    aside = lambda: tt(["d96", "tr"], ["dtr"], T.tr[:, 48:64], T.d96[:, 0:16], T.tr[:, 0:16], A.add)
+    if NP == 1: lanes()
+    for a, b in ((0, 256), (256, 512), (512, 672)) * (NP < 2):
+        ts(["p85", "zb"], ["wi"], T.wi[:, a:b], T.zb[:, 0:b - a], T.v6b[:, 23:24], A.add, add=True)
+    later += [values, first_slots, aside, lambda: ts(["tri0", "ps41"], ["tri"], T.tri[:], T.tri[:], T.ps[0:64, 41:42], A.is_gt)]
 
     if NP:
-        tot["rk"] = E_TABLE * higher
-        wr["rk"] = [("rk", None)]
         for h, n in enumerate(lists):
-            D("y", "dti%d" % h, T.ti[0:32 * n, 32 * h:32 * h + 32], T.kd[4 * h:4 * h + n], ["rk", "ti"], ["tia%d" % h])
+            D("y", "dti%d" % h, T.ti[0:32 * n, 40 * h + 1:40 * h + 33], T.kd[4 * h:4 * h + n], ["rk", "ti"], ["tia%d" % h])
     if sent:
         g.sync.wait_ge(T.sem.lk, sent)
     D("y", "dkc", T.kcs[:].bitcast(dt.uint8), T.kc[:], [], ["kcs"])
     D("y", "dkc", T.kss[:], T.ks[:], [], ["kss"])
     D("y", "dw", T.wb[:], T.w[:], [], ["wb"])
-    D("y", "dz", T.lc[:, 0:16].bitcast(dt.uint8), T.zc[:, 0:16].bitcast(dt.uint8), ["zc"], ["lcz"])
-    D("y", "dz", T.ls[:, 0:16], T.zs[:, 0:16], ["zs"], ["lsz"])
     kb, kept = T.ks4[:, 0:17], T.ks4[:, 1:17]
     if NP:
         n = 256 * NP
-        def search(h):
-            H, c, b = "%d" % h, 272 * h, 512 * h
+        def search(u):
+            H, c, b, h, x = "%d" % u, 272 * u, n * u, u * (NP - 1), 256 * u * (2 - NP)
             return [
-                lambda: ts(["xu", "pvs"], ["cm" + H], T.cm[:, b:b + 512], T.xu[:], T.pvs[:, 2 * h:2 * h + 1], A.subtract, T.pvs[:, 2 * h + 1:2 * h + 2], A.is_ge),
-                lambda: tp(["cm" + H], ["ct" + H], T.ct[:, b:b + 512], T.cm[:, b:b + 512]),
-                lambda: scan(["ct" + H], ["cs" + H], T.cs[:, c + 1:c + 257], T.ct[:, b:b + 512:2], T.ct[:, b + 1:b + 512:2], 0.0, A.add, A.add),
-                lambda: tt(["cs" + H, "es0"], ["of" + H], T.of1[:, 16 * h:16 * h + 16], T.cs[:, c + 16:c + 257:16], T.cs[:, c:c + 256:16], A.subtract),
-                lambda: tt(["ti", "tia" + H, "of" + H, "xg"], ["eq" + H], T.eq[:, 256 * h:256 * h + 256], T.ti[:, 32 * h:32 * h + 32].indirect(T.of1[:, 16 * h:16 * h + 16]), T.xg[:], A.is_equal),
-                lambda: tp(["eq" + H], ["et"], T.et[:, h:n:NP], T.eq[:, 256 * h:256 * h + 256], add=True)]
-        steps = [search(h) for h in range(NP)]
-        tot["rp"] = E_FIRST * higher
-        wr["rp"] = [("rp", None)]
-        ts(["rp", "opv", "ps8"], ["pvs"], T.pvs[:], T.pva[:, 0:16].indirect(T.opv[:, 0:1]), P(8), A.add)
+                lambda: ts(["xu", "pvs"], ["cm" + H], T.cm[:, b:b + n], T.xu[:, x:x + n], T.pvs[:, 4 * h:4 * h + 1], A.subtract, T.pvs[:, 4 * h + 1:4 * h + 2], A.is_ge),
+                lambda: tp(["cm" + H], ["ct" + H], T.ct[:, b:b + n], T.cm[:, b:b + n]),
+                lambda: scan(["ct" + H], ["cs" + H], T.cs[:, c + 1:c + 1 + n // 2], T.ct[:, b:b + n:2], T.ct[:, b + 1:b + n:2], 0.0, A.add, A.add),
+                lambda: tt(["cs" + H, "es0"], ["of" + H], T.of1[:, b // 32:(b + n) // 32], T.cs[:, c + 16:c + 1 + n // 2:16], T.cs[:, c:c + n // 2:16], A.subtract),
+                lambda: tt(["ti", "tia%d" % h, "of" + H, "xg"], ["eq" + H], T.eq[:, b // 2:(b + n) // 2], T.ti[:, 40 * h:40 * h + 33].indirect(T.of1[:, b // 32:(b + n) // 32]),
+                           T.xg[:, x // 2:(x + n) // 2], A.is_equal),
+                lambda: tp(["eq" + H], ["et"], T.et[:, u:n:2] if NP == 2 else T.et[:, b // 2:(b + n) // 2], T.eq[:, b // 2:(b + n) // 2], add=True)]
+        steps = [search(u) for u in (0, 1)]
+        copy(["rp", "pv0", "opv"], ["pvs"], T.pvs[:], T.pva[:, 0:128].indirect(T.opv[:, 0:1]))
+        if NP == 2: lanes()
         for k in range(6):
             steps[0][k]()
+            if k == 2: numbers()
             if k == 3: gap()
-            if NP == 2: steps[1][k]()
-            if k >= 4: gap()
+            steps[1][k]()
+        gap()
         if higher > 2: scan(["et"], ["es"], T.es[:, 1:n + 1], T.et[0:64, 0:n], T.et[64:128, 0:n], 0.0, A.add, A.add)
         else: n = 128; scan(["et"], ["es"], T.es[:, 1:n + 1], T.et[0:64, 0:256:2], T.et[0:64, 1:256:2], 0.0, A.add, A.add)
         w = n // 16
@@ -273,91 +309,81 @@ def rank_program(g, core, T, topo):
         now, before = (T.c4[:, 1:17], T.c4[:, 0:16]) if higher > 1 else (T.es[0:32, w:n + 1:w], T.es[0:32, 0:n:w])
         for a in (0, 1):
             tt(["c4", "es", "es0"], ["ks4"], T.ks4[32 * a:32 * a + 32, 1:17], now, before, A.is_equal, add=a > 0)
-        gap()
     else:
-        gap(3)
-    scan(["ks4", "d96", "plz"], ["pl"], T.pl[:, 32:49], kb, T.d96[:, 0:17], 0.0, A.add, A.max)
-    act(["ks4", "plz"], ["pln"], T.nj[:], kept, accum_out=T.pl[:, 16:17])
+        numbers()
+        gap(4)
+    gap(2)
+    scan(["ks4", "d96"], ["pl"], T.pl[:, 0:17], kb, T.d96[:, 0:17], 0.0, A.add, A.max)
+    act(["ks4"], ["pln"], T.nj[:], kept, accum_out=T.pl[:, 20:21])
+    tt(["ks4", "tr"], ["f1"], T.f1[:], kept, T.tr[:, 0:16], A.mult)
+    tt(["ks4", "tr"], ["nk"], T.nk[:, 1:17], kept, T.tr[:, 1:17], A.mult)
+    ts(["pl", "tri"], ["pm"], T.pt[:, 32:64], T.tri[:], T.pl[:, 16:17], A.mult)
+    lin(["pln", "tri"], ["pn"], T.pt[:, 0:32], T.tri[:], T.pl[:, 20:21], 0.0)
     constants()
-    ts(["ks4"], ["f1"], T.f1[:], kept, 0.0, A.is_equal)
-    tp(["pl", "pln"], ["pt"], T.pt[:], T.pl[:])
-    tt(["f1", "tr"], ["nk"], T.nk[:, 1:17], T.f1[:], T.tr[:], A.mult)
-    scan(["pt"], ["cc"], T.cc[:, 1:33], T.pt[:, 0:32], T.pt[:, 32:64], 0.0, A.add, A.max)
-    tt(["ks4", "nk"], ["d0a"], T.dd[:, 0:16], T.ks4[:, 0:16], T.nk[:, 1:17], A.add)
-    tt(["d96", "nk"], ["d1"], T.dd[:, 32:48], T.d96[:, 0:16], T.nk[:, 1:17], A.add)
-    tp(["cc"], ["cy"], T.cy[:], T.cc[:, 0:32])
-    tt(["d0a", "nk", "nkz"], ["d0"], T.dd[:, 16:32], T.dd[:, 0:16], T.nk[:, 0:16], A.subtract)
+    tt(["f1", "nk", "nkz"], ["d0a"], T.dd[:, 48:64], T.nk[:, 0:16], T.f1[:], A.subtract)
+    tt(["f1", "dtr"], ["d1"], T.dd[:, 96:112], T.tr[:, 48:64], T.f1[:], A.subtract)
+    tp(["pm"], ["dm"], T.dd[:, 64:96], T.pt[:, 32:64])
+    tt(["d0a", "trc", "trd"], ["d0"], T.dd[:, 32:48], T.dd[:, 48:64], T.tr[:, 32:48], A.add)
+    tp(["pn"], ["dn"], T.dd[:, 0:32], T.pt[:, 0:32])
     for a in (0, 1):
-        scan(["d0", "d1", "cy"], ["pw"], T.pw[64 * a:64 * a + 64, 8 - 8 * a:24 - 8 * a], T.dd[:, 16:32], T.dd[:, 32:48], T.cy[:, 16:17], A.add, A.max, add=True)
-    gap()
-    E("v", V.tensor_copy, ["pw", "val", "w2"], ["wi"], T.wi[:, 0:2368].indirect(T.pw[:, 8:16]), T.val[:])
+        scan(["d0", "d1", "dm", "dn"], ["pw"], T.pw[64 * a:64 * a + 64, 8 - 8 * a:56 - 8 * a], T.dd[:, 0:48], T.dd[:, 64:112], 0.0, A.add, A.max, add=True)
+    E("v", V.quantize_mx, ["zb", "zb2"], ["zc", "zs"], T.zc[:], T.zs[:], T.zb[:, 0:512])
+    D("y", "dz", T.lc[:, 0:16].bitcast(dt.uint8), T.zc[:, 0:16].bitcast(dt.uint8), ["zc"], ["lcz"])
+    D("y", "dz", T.ls[:, 0:16], T.zs[:, 0:16], ["zs"], ["lsz"])
+    E("v", V.tensor_copy, ["pw", "val"], ["wi"], T.wi[:, 0:2384].indirect(T.pw[:, 40:48]), T.val[:])
     tt(["im", "mh"], ["mo"], T.mo[:], T.im[:, 0:20], T.mh[:], A.add)
-    nb32 = 20 + odd
-    tp(["wi"], ["wt"], T.wt[:, 0:32 * nb32], T.wi[:, 0:32 * nb32])
-    scan(["wt"], ["hk"], T.hk[:, 4:4 + 4 * nb32], T.wt[0:64, 0:32 * nb32:8], T.wt[64:128, 0:32 * nb32:8], 0.0, A.add, A.add)
+    nb32, c = 20 + odd, 672 * (1 - odd)
+    for k in (1 - odd, odd):
+        tp(["wi"], ["wt%d" % k], T.wt[:, 672 * k:672 + 640 * k], T.wi[:, 16 * k:672 - 16 * k])
+    scan(["wt%d" % (1 - odd)], ["hk"], T.hk[:, 4:4 + 4 * nb32], T.wt[0:64, c:c + 32 * nb32:8], T.wt[64:128, c:c + 32 * nb32:8], 0.0, A.add, A.add)
     for k in (0, 1):
         tt(["hk"], ["qk"], T.qk[64 * k:64 * k + 64, 0:nb32], T.hk[:, 7:4 + 4 * nb32:4], T.hk[:, 3:4 * nb32:4], A.subtract, add=True)
-    scan(["wt"], ["qi"], T.qi[:, 4:4 + 4 * nb32], T.wt[0:64, 4:32 * nb32:8], T.wt[64:128, 4:32 * nb32:8], 0.0, A.add, A.add)
+    act(["wt0", "wt1", "ogt"], ["yy"], T.yy[:], T.wt[:, 0:1312].indirect(T.ogs[:, 10:15]))
     peers = [(s + i) % N for i in range(1, N)]
     keys = lambda d: (T.kx[:, 4 * slot(s, d):4 * slot(s, d) + 3], T.qk[:, (5 * d + odd) // 2:(5 * d + odd) // 2 + 3])
     fused([(T.cores[d],) + keys(d) for d in peers], "rx%d" % wave(s), [2] * len(peers), ["qk"])
     act(["qk"], ["kx%d" % wave(s)], *keys(s))
+    columns()
+    scan(["yy"], ["qi"], T.qi[:, 4:84], T.yy[0:64, :], T.yy[64:128, :], 0.0, A.add, A.add)
     for k in (0, 1):
-        tp(["qi"], ["xt"], T.xt[64 * k:64 * k + 64, :], T.qi[:, 3:128:4], add=True)
+        tt(["qi"], ["off"], T.off[64 * k:64 * k + 64, :], T.qi[:, 5:84:2], T.qi[:, 3:82:2], A.subtract, add=True)
     E("v", V.quantize_mx, ["wb"], ["wc", "wz"], T.wc[:], T.wz[:], T.wb[:])
-    copy(["xt", "ody"], ["yy"], T.yy[:], T.xt[:, 0:32].indirect(T.ody[:, 0:4]))
-    gap()
-    tp(["yy"], ["ot"], T.ot[:], T.yy[:])
-    gap()
-    for e in (0, 1):
-        c = 32 * e + (odd > e)
-        tt(["ot"], ["off"], T.off[:, (e + odd) % 2:40:2], T.ot[:, c + 1:c + 21], T.ot[:, c:c + 20], A.subtract, add=True)
-    gap()
-    halves = [1 - s // 4, s // 4]
+    near = s - s % 4
+    far = N // 2 - near
     codes_to = lambda d: (T.lc[:, 16 + 80 * slot(s, d):96 + 80 * slot(s, d)].bitcast(dt.uint8), T.qc[:, 80 * d:80 * d + 80].bitcast(dt.uint8))
     scales_to = lambda d: (T.ls[:, 16 + 80 * slot(s, d):96 + 80 * slot(s, d)], T.qs[:, 80 * d:80 * d + 80])
 
-    def send(a, b, to, sem, toks):
+    me, nb = s - odd, (s - odd) ^ 2
+    parts = {"0": (far, far + 4), "1": (me, me + 2), "2": (nb, nb + 2)}
+
+    def send(k, to, sem, toks):
+        a, b = parts[k]
         part = [d for d in range(a, b) if d != s]
         e = len(topo.engines(core, T.cores[part[0]])) // (b - a)
-        fused([(T.cores[d],) + to(d) for d in part], sem, [e] * len(part), toks)
-        if a <= s < b: D("y", "d" + sem[:2], *to(s), toks, ["o" + sem[:2]])
+        fused([(T.cores[d],) + to(d) for d in part], sem + k, [e] * len(part), toks)
+        if a <= s < b: D("y", "d" + sem, *to(s), toks, ["o" + sem])
 
-    far, near, me, nb = 4 * halves[0], 4 * halves[1], s - odd, (s - odd) ^ 2
+    def codes(k):
+        a, b = parts[k]
+        E("v", V.tensor_copy, ["off", "kcs"], ["qc" + k], T.qc[:, 80 * a:80 * b].bitcast(dt.uint32), T.kcs[:, 0:512].bitcast(dt.uint32).indirect(T.off[:, 5 * a:5 * b]))
+        send(k, codes_to, "rc", ["qc" + k])
 
-    def codes(a, b):
-        E("v", V.tensor_copy, ["off", "kcs"], ["qc%d" % a], T.qc[:, 80 * a:80 * b].bitcast(dt.uint32), T.kcs[:, 0:512].bitcast(dt.uint32).indirect(T.off[:, 5 * a:5 * b]))
-        send(a, b, codes_to, "rc", ["qc%d" % a])
+    def scales(k, move=act):
+        a, b = parts[k]
+        move(["off", "kss"], ["qs" + k], T.qs[:, 80 * a:80 * b], T.kss[:, 0:512].indirect(T.off[:, 5 * a:5 * b]))
+        send(k, scales_to, "rs", ["qs" + k])
 
-    def scales(a, b, sem):
-        act(["off", "kss"], ["qs%d" % a], T.qs[:, 80 * a:80 * b], T.kss[:, 0:512].indirect(T.off[:, 5 * a:5 * b]))
-        send(a, b, scales_to, sem, ["qs%d" % a])
-
-    codes(far, far + 4)
-    codes(me, me + 2)
-    if NP < 2:
-        scales(me, me + 2, "rs0")
-        codes(nb, nb + 2)
-        scales(nb, nb + 2, "rs1")
-    gap(len(later))
     for u in range(3):
         tot["rx%d" % u] = sum(2 for r in range(N) if r != s and wave(r) == u)
         wr["kx%d" % u] = wr.get("kx%d" % u, []) + [("rx%d" % u, None)]
-    kxr, kxs = ["mo", "ox6", "phi"], ["kx0", "kx1", "kx2"]
-    act(kxr + ["kx2"], ["mm2"], T.mm[:, 320:640], T.kx[:, 16:32].indirect(T.mo[:, 0:20]), AF.Identity, bias=P(20))
-    if NP == 2: scales(me, me + 2, "rs0")
-    if NP == 2: act(kxr + ["kx1"], ["mm1"], T.mm[:, 160:320], T.kx[:, 8:16].indirect(T.mo[:, 0:10]), AF.Identity, bias=P(20))
-    else: ts(kxr + ["kx1"], ["mm1"], T.mm[:, 160:320], T.kx[:, 8:16].indirect(T.mo[:, 0:10]), P(20), A.add)
-    act(kxr + ["kx0"], ["mm0"], T.mm[:, 0:160], T.kx[:, 0:8].indirect(T.mo[:, 0:10]), AF.Identity, bias=P(20))
-    tp(["mm2"], ["xf2"], T.xf[:, 320:640], T.mm[:, 320:640])
-    if NP < 2: tp(["mm1"], ["xf1"], T.xf[:, 160:320], T.mm[:, 160:320])
-    for out, tok in ((T.v6, "v6"), (T.v6b, "v6h")):
-        ts(kxr + kxs, [tok], out[:, 0:16], T.kx[:, 0:32].indirect(T.ox6[:, 0:1]), P(21), A.add, 0.5, A.max)
-    if NP == 2: tp(["mm1"], ["xf1"], T.xf[:, 160:320], T.mm[:, 160:320])
-    ts(["v6"], ["pd"], T.pd[:, 0:5], T.v6[:, 0:5], 1.0, A.is_lt)
-    tt(["v6", "v6h"], ["v6l"], T.v6b[:, 16:19], T.v6[:, 0:3], T.v6b[:, 0:3], A.subtract)
-    tp(["mm0"], ["xf0"], T.xf[:, 0:160], T.mm[:, 0:160])
     xs = ["xf0", "xf1", "xf2"]
+
+    def spread(u, q):
+        a, b = 160 * u, 160 * u + (320 if u == 2 else 160)
+        sides = T.mm[:, a:b], T.kx[:, 8 * u:8 * u + (b - a) // 20].indirect(T.mo[:, 0:(b - a) // 16])
+        if q == "s": act(["mo", "phi", "kx%d" % u], ["mm%d" % u], *sides, AF.Identity, bias=P(20))
+        else: ts(["mo", "phi", "kx%d" % u], ["mm%d" % u], *sides, P(20), A.add)
+        return lambda: tp(["mm%d" % u], [xs[u]], T.xf[:, a:b], T.mm[:, a:b])
 
     def signs(e, a, b, col):
         act(xs[a // 160:(b + 160) // 320 + 1] + ["v6"], ["jk%d" % col, "sm%d" % col], T.jk[:, 640 * e - 1920 + a:640 * e - 1920 + b], T.xf[:, a:b], AF.Sign,
@@ -366,62 +392,76 @@ def rank_program(g, core, T, topo):
     def larger(k, a, b):
         ts(xs[a // 160:(b + 160) // 320 + 1] + ["v6l"], ["cb%d" % k], T.cb[:, 640 * k + a:640 * k + b], T.xf[:, a:b], T.v6b[:, k:k + 1], A.subtract, T.v6b[:, 16 + k:17 + k], A.is_gt, add=True)
 
-    signs(3, 160, 640, 2)
-    lin(["pd", "jf"], ["jt3"], T.pd[:, 11:12], T.pd[:, 3:4], T.jf[:, 3:4], 320.0)
-    lin(["pd", "jf"], ["jt4"], T.pd[:, 12:13], T.pd[:, 4:5], T.jf[:, 4:5], 320.0)
-    tt(["pd", "jf"], ["pd2"], T.v6b[:, 20:23], T.pd[:, 0:3], T.jf[:, 0:3], A.mult)
-    signs(3, 0, 160, 3)
-    lin(["sm2", "jt3"], ["jt2"], T.pd[:, 10:11], T.sm[:, 2:3], -0.5, T.pd[:, 11:12])
-    signs(4, 0, 640, 4)
-    for e, c in ((3, 2), (4, 4)):
-        lin(["sm%d" % e, "jt%d" % c], ["pu%d" % e], T.pu[:, 958 + e:959 + e], T.sm[:, e:e + 1], -0.5, T.pd[:, 8 + c:9 + c])
-    for k in range(3): larger(k, 160, 640)
-    for k in range(3): larger(k, 0, 160)
-    for k in range(3):
-        scan(["cb%d" % k, "pd2"], ["pu"], T.pu[:, 1 + k:959 + k:3], T.cb[:, 640 * k:640 * k + 320], T.cb[:, 640 * k + 320:640 * k + 640], T.v6b[:, 20 + k:21 + k], A.add, A.add, add=True)
-    if NP == 2: codes(nb, nb + 2)
-    scales(far, far + 4, "rs2")
-    if NP == 2: scales(nb, nb + 2, "rs1")
-    act(xs + ["phi"], ["xkk"], T.xk[0:32, 16:656], T.xf[0:32, :], AF.Identity, bias=T.ps[0:32, 22:23])
-    E("v", V.tensor_copy, ["pu", "pu3", "pu4", "cst"], ["w2"], T.w2[:, 0:1664].indirect(T.pu[:, 958:963]), T.cst[:])
-    tp(["w2"], ["w2t"], T.w2t[:], T.w2[:, 0:512])
-    tt(["w2t"], ["c5"], T.c5[:], T.w2t[0:64, 0:512:8], T.w2t[64:128, 0:512:8], A.add)
+    gap(len(later))
+    turn = {}
+
+    def rows():
+        for out, tok in ((T.v6, "v6"), (T.v6b, "v6h")):
+            ts(["ox6", "phi", "kx0", "kx1", "kx2"], [tok], out[:, 0:16], T.kx[:, 0:32].indirect(T.ox6[:, 0:1]), P(21), A.add, 0.5, A.max)
+
+    def halves():
+        tt(["v6", "v6h"], ["v6l"], T.v6b[:, 16:20], T.v6[:, 0:4], T.v6b[:, 0:4], A.subtract)
+        ts(["v6"], ["pd"], T.pd[:, 0:5], T.v6[:, 0:5], 1.0, A.is_lt)
+
+    def aside(q):
+        for e in (3, 4):
+            ts(["pd", "jf"], ["jt%d" % e], T.pd[:, 8 + e:9 + e], T.pd[:, e:e + 1], T.jf[:, e:e + 1], A.mult, 80.0 * e, A.add)
+
+    step = {"c": codes, "s": scales, "v": lambda k: scales(k, copy), "m": lambda u: turn.update({u: spread(int(u), "s")}), "n": lambda u: turn.update({u: spread(int(u), "v")}), "t": lambda u: turn[u](),
+            "r": lambda _: rows(), "h": lambda _: halves(), "a": aside, "L": lambda k: larger(int(k), 0, 640),
+            "p": lambda _: tt(["pd", "jf"], ["pd2"], T.v6b[:, 20:23], T.pd[:, 0:3], T.jf[:, 0:3], A.mult),
+            "e": lambda k: larger(int(k), 160, 640), "l": lambda k: larger(int(k), 0, 160), "g": lambda e: signs(int(e), 0, 640, int(e)),
+            "f": lambda e: lin(["sm" + e, "jt" + e], ["pu" + e], T.pu[:, 958 + int(e):959 + int(e)], T.sm[:, int(e):int(e) + 1], -0.5, T.pd[:, 8 + int(e):9 + int(e)]),
+            "z": lambda k: scan(["cb" + k, "pd2"], ["pu"], T.pu[:, 1 + int(k):959 + int(k):3], T.cb[:, 640 * int(k):640 * int(k) + 320], T.cb[:, 640 * int(k) + 320:640 * int(k) + 640],
+                                T.v6b[:, 20 + int(k):21 + int(k)], A.add, A.add, add=True)}
+    step.update({"G": lambda _: signs(3, 160, 640, 3),
+                 "j": lambda _: scan(["cb3", "jt3"], ["jt2"], T.j3[:], T.cb[:, 1920:2000], T.cb[:, 2000:2080], T.pd[:, 11:12], A.add, A.add),
+                 "F": lambda _: lin(["sm3", "jt2"], ["pu3"], T.pu[:, 961:962], T.sm[:, 3:4], -0.5, T.j3[:, 79:80])})
+    step["x"] = lambda _: E("g", g.affine_select, xs, ["xkk"], T.xk[0:64, 16:656], T.xf[0:64, :], [[0, 640]], A.is_ge, 0.0, 0, 0)
+    step.update({"H": lambda _: signs(3, 0, 160, 2),
+                 "A": lambda _: [lin(["pd", "jf"], ["jt%d" % e], T.pd[:, 8 + e:9 + e], T.pd[:, e:e + 1], T.jf[:, e:e + 1], 320.0) for e in (3, 4)],
+                 "B": lambda _: [ts(["pd", "jf"], ["jt%d" % e], T.pd[:, 8 + e:9 + e], T.pd[:, e:e + 1], T.jf[:, e:e + 1], A.mult, 320.0, A.add) for e in (3, 4)],
+                 "J": lambda _: lin(["sm3", "jt3"], ["jt2"], T.pd[:, 10:11], T.sm[:, 3:4], -0.5, T.pd[:, 11:12]),
+                 "K": lambda _: lin(["sm2", "jt2"], ["pu3"], T.pu[:, 961:962], T.sm[:, 2:3], -0.5, T.pd[:, 10:11])})
+    for x in (ORDER if NP == 2 else EARLY).split():
+        step[x[0]](x[1:])
+    E("v", V.tensor_copy, ["pu", "pu3", "pu4", "cst"], ["w2"], T.w2[:, 16:1744].indirect(T.pu[:, 958:963]), T.cst[:])
+    for k in (0, 1):
+        tp(["w2"], ["w2t"], T.w2t[:, 672 * k:544 + 640 * k], T.w2[:, 16 * k:544 - 16 * k], add=True)
+    for n in ("rc0", "rs0", "rc1", "rs1", "rc2", "rs2"):
+        tot[n] = 8 if n[2] == "1" else 16
+        wr[n] = [(n, None)]
+    land, lands = ["rc0", "rc1", "rc2", "orc", "lcz"], ["rs0", "rs1", "rs2", "ors", "lsz"]
+
+    def product(k, move=act):
+        u, a = (("1", me), ("0", far), ("0", far + 2), ("2", nb))[k]
+        c = 16 + 80 * a
+        E("t", g.tensor.matmul_mx, ["rc" + u, "rs" + u, "wc", "wz"] + ["orc", "ors"] * (k == 0), ["acc%d" % k], T.acc[:, 512 * k:512 * k + 160], T.wc[:], T.wz[:], T.lc[:, c:c + 160], T.ls[:, c:c + 160], True, True)
+        move(["acc%d" % k], ["yf"], T.yf[:, c:c + 160], T.acc[:, 512 * k:512 * k + 160], add=True)
+
+    product(LAST[3])
+    copy(["w2t", "ogs"], ["sy"], T.sy[:], T.w2t[:, 0:1184].indirect(T.ogs[:, 0:8]))
+    for k in LAST[:2]: product(k)
+    scan(["sy"], ["cz"], T.cz[:, 4:132], T.sy[0:64, :], T.sy[64:128, :], 0.0, A.add, A.add)
     for a in (0, 1):
-        scan(["c5"], ["cz"], T.cz[32 * a:32 * a + 32, 4:68], T.c5[0:32, :], T.c5[32:64, :], 0.0, A.add, A.add, add=a > 0)
+        tt(["cz"], ["so"], T.so[32 * a:32 * a + 32, :], T.cz[0:32, 3:132:4], T.cz[32:64, 3:132:4], A.add, add=a > 0)
     for a in (0, 1):
-        tp(["cz"], ["sx"], T.sx[64 * a:64 * a + 64, :], T.cz[:, 3:128:4], add=True)
-    copy(["sx", "ody"], ["sy"], T.sy[:], T.sx[:, 0:32].indirect(T.ody[:, 0:4]))
-    tp(["sy"], ["so"], T.so[:], T.sy[:])
-    for e in (0, 1):
-        tt(["so"], ["of2"], T.of2[:, e:32:2], T.so[:, 32 * e + 1:32 * e + 17], T.so[:, 32 * e:32 * e + 16], A.subtract, add=True)
-    tot["rc"] = 8 + 16 + 16
-    wr["lca"] = [("rc", None)]
-    land, lands = ["lca", "orc", "lcz"], ["ls0", "ls1", "ls2", "ors", "lsz"]
-    for k in range(3):
-        tot["rs%d" % k] = 16 if k else 8
-        wr["ls%d" % k] = [("rs%d" % k, None)]
-    for k in ((0, 1, 2, 3) if far < near else (0, 2, 3, 1)):
-        c = 16 + 80 * (me, nb, far, far + 2)[k]
-        E("t", g.tensor.matmul_mx, land + ["ls%d" % min(k, 2), "ors", "wc", "wz"], ["acc%d" % k], T.acc[:, 512 * k:512 * k + 160], T.wc[:], T.wz[:], T.lc[:, c:c + 160], T.ls[:, c:c + 160], True, True)
-        act(["acc%d" % k], ["yf"], T.yf[:, c:c + 160], T.acc[:, 512 * k:512 * k + 160], add=True)
-    def codes_out(k, a, b):
+        tt(["so"], ["of2"], T.of2[64 * a:64 * a + 64, :], T.so[:, 1:33], T.so[:, 0:32], A.subtract, add=True)
+    need("s", lands + ["xkk", "xk0"], [])
+    product(LAST[2], act)
+    E("g", g.affine_select, ["of2"], ["o2f"], T.o2f[:], T.of2[:], [[0, 32]], A.is_ge, 0.0, 0, 0)
+    for k, (a, b) in enumerate(PIECES):
         E("v", V.tensor_copy, land + ["of2"], ["fc%d" % k], T.fc[:, a:b].bitcast(dt.uint32), T.lc[:, 0:656].bitcast(dt.uint32).indirect(T.of2[:, a // 16:b // 16]))
-        D("y", "doc%d" % k, T.oc[:, 4 * a:4 * b], T.fc[:, a:b].bitcast(dt.uint8), ["fc%d" % k], ["oc"])
-
-    def y_out(k, a, b, q):
         act(["yfz", "yf", "of2"], ["yo%d" % k], T.yo[:, a:b], T.yf[:, 0:656].indirect(T.of2[:, a // 16:b // 16]))
-        D(q, "dy%d" % k, T.y[:, a:b], T.yo[:, a:b], ["yo%d" % k], ["y"])
-
-    codes_out(0, 0, 192)
-    y_out(1, 0, 448, "y")
-    codes_out(1, 192, 512)
-    act(lands + ["of2"], ["fz"], T.fz[:], T.ls[:, 0:656].indirect(T.of2[:, 0:32]))
-    act(["yfz", "yf", "of2"], ["yo2"], T.yo[:, 448:512], T.yf[:, 0:656].indirect(T.of2[:, 28:32]))
+        D("y", "dout", T.oc[:, 4 * a:4 * b], T.fc[:, a:b].bitcast(dt.uint8), ["fc%d" % k], ["oc"])
+        D("y", "dout", T.y[:, a:b], T.yo[:, a:b], ["yo%d" % k], ["y"])
+        if k: copy(["o2f", "oq"], ["og"], T.og[:], T.o2f[:, 0:32].indirect(T.oq[:, 0:1]))
+    for move, a, b in ((copy, 0, 352), (act, 352, 512)):
+        move(lands + ["of2"], ["fz%d" % a], T.fz[:, a:b], T.ls[:, 0:656].indirect(T.of2[:, a // 16:b // 16]))
+    act(["xkk", "xk0", "og"], ["ko"], T.ko[:], T.xk[:, 0:656].indirect(T.og[:, 0:8]), AF.Identity, scale=-1.0, bias=P(22))
     for j in range(4):
-        D("ys"[j % 2], "dos", T.osc[4 * j:4 * j + 4, :], T.fz[32 * j:32 * j + 4, :], ["fz"], ["osc"])
-    D("s", "dy2", T.y[:, 448:512], T.yo[:, 448:512], ["yo2"], ["y"])
-    ts(["xkk", "xk0", "of2"], ["ko"], T.ko[:], T.xk[:, 0:656].indirect(T.of2[:, 0:32]), -1.0, A.mult)
-    D("y", "dok", T.ok[:], T.ko[0:64:32, :], ["ko"], ["ok"])
+        D("ys"[j // 2], "dout", T.osc[4 * j:4 * j + 4, :], T.fz[32 * j:32 * j + 4, :], ["fz0", "fz352"], ["osc"])
+    D("y", "dout", T.ok[:], T.ko[0:128:16, :], ["ko"], ["ok"])
     for n in SEMAPHORES:
         if tot[n]:
             g.wait_ge(T.sem[n], tot[n])

from concourse.bass import DstId, RemoteDMATransfer
from concourse.mybir import dt, AluOpType, AxisListType, ActivationFunctionType

SCRATCH = {"mykd": ("dram", [128, 8], "int32"), "kd": ("dram", [7, 128, 8], "int32"), "acc": ("psum", [128, 2048], "float32")}
SIZES = {
    (128, "float32"): "vf:16 ps:48 ix:96 im:40 mh:20 ic:80 i8:16 qk:24 j3:80 "
                      "spb:16 kx:32 xk:656 v6:32 pd:16 jf:24 sm:8 o2f:32 yf:656 yo:512 ko:128",
    (64, "bfloat16"): "d7:112 d7s:112 rs7:112 es:528", (32, "float32"): "spn:16 c4:20",
    (64, "float32"): "tr:64 d96:20 ks4:20 f1:16 nk:20 dd:112 pl:24 pt:64 tri:32 hk:88 qi:84 nj:16 so:33 cz:132",
    (128, "bfloat16"): "zw:64 mv:128 val:128 wi:2384 wt:1312 yy:80 sy:128 pvs:16 v6b:24 cm:1024 ct:1024 eq:512 et:512 zb:544 wb:512 jk:1280 cb:2080 w2:1744 w2t:1184 cst:80",
    (128, "float16"): "cs:544",
    (128, "int32"): "ti:80 pi:12 zt:32 pv:4 pva:128", (32, "int32"): "ld:32 spr:16",
    (128, "uint16"): "oq:2 og:16 opv:4 m0:512 xu:512 mg:256 xg:256 of1:32 mb:32 mo:20 omg:16 omv:8 ox6:4 ogs:16 pw:56 off:40 pu:964 of2:32 mm:640 xf:640",
    (128, "float8_e4m3fn_x4"): "zc:128 kcs:512 qc:640 lc:656 fc:512 wc:128",
    (128, "uint8"): "zs:128 kss:512 qs:640 ls:672 fz:512 wz:128"}
for (_p, _d), _l in SIZES.items():
    for _x in _l.split():
        SCRATCH[_x.split(":")[0]] = ("sbuf", [_p, int(_x.split(":")[1])], _d)
SEMAPHORES = ["gs", "dk", "dt", "dsp", "dpv", "lk", "rk", "rp", "dti0", "dti1", "dw", "dkc", "dz", "rx0", "rx1", "rx2", "drc", "drs", "rc0", "rs0", "rc1", "rs1", "rc2", "rs2",
              "loc", "ts", "vs", "ss", "dout"]
E_TABLE, E_FIRST = 4, 8
ORDER = "m2 c0 m1 c1 c2 t2 s1 t1 m0 r h t0 x G A e0 p H J g4 K f4 e1 e2 l0 l1 l2 z0 z1 z2 s0 s2"
EARLY = "c0 s1 c1 s2 c2 m2 s0 n1 t2 t1 m0 r h t0 x G A e0 p H J g4 K f4 e1 e2 l0 l1 l2 z0 z1 z2"
LAST = (1, 2, 3, 0)
TWO = 3
DOWN = (("table", 0, 1), ("first", 0, TWO), ("first", TWO, 7), ("table", 1, 7))
PIECES = ((0, 192), (192, 512))


def rank_program(g, core, T, topo):
    s = T.rank_of(core)
    if s is None:
        return
    A, N = AluOpType, len(T.cores)
    AF = ActivationFunctionType
    q_of = {"v": g.vector, "s": g.scalar, "t": g.tensor, "g": g, "y": g.sync}
    own = {"v": "vs", "s": "ss", "t": "ts", "g": "gs"}
    tot = {n: 0 for n in SEMAPHORES}
    seen = {q: {} for q in q_of}
    wr, rd = {}, {}

    def need(q, r, w, add=False):
        deps = [(d, 0) for t in r for d in wr.get(t, [])]
        deps += [(d, 1) for t in w for d in wr.get(t, []) + rd.get(t, [])]
        most = {}
        for (sem, n), order in deps:
            if not (order and add and own.get(q) == sem):
                most[sem] = max(most.get(sem, 0), tot[sem] if n is None else n)
        for sem in sorted(most, key=lambda x: x == own.get(q)):
            if seen[q].get(sem, 0) < most[sem]:
                q_of[q].wait_ge(T.sem[sem], most[sem])
                seen[q][sem] = most[sem]

    def note(me, r, w, add=False):
        for t in r:
            rd.setdefault(t, []).append(me)
        for t in w:
            wr[t] = wr.get(t, []) + [me] if add else [me]
            if not add:
                rd[t] = []

    def E(q, call, r, w, *args, add=False, **kw):
        need(q, r, w, add)
        sem = own[q]
        call(*args, **kw).then_inc(T.sem[sem], 1)
        tot[sem] += 1
        note((sem, tot[sem]), r, w, add)

    def D(q, sem, out, in_, r, w, par=True):
        need(q, r, [] if par else w)
        q_of[q].dma_start(out, in_).then_inc(T.sem[sem], 16)
        tot[sem] += 16
        note((sem, None), r, w, True)

    V, S = g.vector, g.scalar

    def copy(r, w, out, in_, add=False): E("v", V.tensor_copy, r, w, out, in_, add=add)
    def tt(r, w, out, a, b, op, add=False): E("v", V.tensor_tensor, r, w, out, a, b, op, add=add)
    def ts(r, w, out, a, s1, op, s2=None, op1=None, add=False):
        if op1 is None: E("v", V.tensor_scalar, r, w, out, a, s1, None, op, add=add)
        else: E("v", V.tensor_scalar, r, w, out, a, s1, s2, op, op1, add=add)
    def tp(r, w, out, in_, add=False): E("v", V.transpose, r, w, out, in_, add=add)
    def scan(r, w, out, a, b, init, o0, o1, add=False): E("v", V.tensor_tensor_scan, r, w, out, a, b, init, o0, o1, add=add)
    def fill(w, ap, c, add=False): E("v", V.memset, [], w, ap, c, add=add)
    def act(r, w, out, in_, fn=AF.Copy, add=False, **kw): E("s", S.activation, r, w, out, in_, fn, add=add, **kw)
    def lin(r, w, out, in_, scale, bias, add=False): act(r, w, out, in_, AF.Identity, add, scale=scale, bias=bias)
    def iota(w, ap, pat, base, mult=0):
        E("g", g.iota, [], w, ap, pat, base, mult, allow_small_or_imprecise_dtypes=True)

    later = []

    def gap(n=1):
        for _ in range(min(n, len(later))):
            later.pop(0)()

    def fused(pairs, sem, per, r):
        need("g", r, [])
        tr = []
        for i, (c, dst, src) in enumerate(pairs):
            rid, pid, _ = topo.addr(c)
            e = topo.engines(core, c)[sum(per[:i]):sum(per[:i + 1])]
            tr.append(RemoteDMATransfer(dst_ids=[DstId(rid=rid, pnc=pid)], dma_engine_mask=sum(1 << k for k in e),
                                        remote_sem=T.sem[sem], src=src, dst=dst))
        g.remote_dma_fused(tr, local_sem=T.sem.loc)
        tot["loc"] += sum(per)

    def to_lower(dst, src, sem, per, r, ranks):
        if not ranks: return
        need("g", r, [])
        ids = [DstId(rid=topo.addr(T.cores[d])[0], pnc=topo.addr(T.cores[d])[1]) for d in ranks]
        mask = sum(1 << k for k in topo.engines(core, T.cores[0])[:per])
        g.remote_dma_fused([RemoteDMATransfer(dst_ids=ids, dma_engine_mask=mask, remote_sem=T.sem[sem], srcs=[src],
                                              dsts=[dst(s - d - 1) for d in ranks])], local_sem=T.sem.lk)
        tot["lk"] += per

    higher = N - 1 - s
    lists = [n for n in (min(higher, 4), higher - 4) if n > 0]
    NP = len(lists)
    odd = s % 2
    slot = lambda src, dst: src ^ (dst % 2)
    P = lambda k: T.ps[:, k:k + 1]
    wave = lambda r: min(r // 2, 2)

    if s > 0:
        for k in (0, 1):
            D("ys"[k], "dk", T.mykd[64 * k:64 * k + 64, :], T.ky[:], [], ["mykd"])
        for a in range(4):
            D("ys"[a % 2], "dpv", T.pv[32 * a:32 * a + 32, 2:3], T.ky[0:1, :], [], ["pv"])
    for k in (0, 1):
        D("ys"[k], "dt", T.ld[8 * k:8 * k + 8, :], T.ky[:, 16 * k:16 * k + 16], [], ["ld"])
    D("y", "dt", T.ld[16:32, :], T.ky[:], [], ["ld"])
    D("s", "dsp", T.spr[0:1, :], T.sp[:], [], ["spr"])

    iota(["pi"], T.pi[:, 0:1], [[0, 1]], 0, 1)
    iota(["imb"], T.ix[:, 0:32], [[1, 8], [8, 2], [0, 2]], 0)
    iota(["img"], T.ix[:, 32:48], [[1, 16]], 16)
    iota(["imv"], T.ix[:, 64:72], [[1, 4], [8, 2]], 0)
    if NP:
        fill(["ti"], T.ti[:], -1)
        if NP == 2:
            for k in (4, 5): fill(["pv0"], T.pva[:, 32 * lists[1] + k:128:32], 0, add=True)
        elif higher < 4:
            fill(["pv0"], T.pva[:, 32 * higher:128], 0)
    fill(["rs7"], T.rs7[:], 1.0)
    for k, (sh, m) in enumerate(((0, 15), (4, 1), (5, 3), (4, 4), (0, 97 + 4 * (NP == 2)), (2, 1), (3, 1), (1, 24), (0, 3))):
        ts(["pi"], ["pi%d" % k], T.pi[:, 1 + k:2 + k], T.pi[:, 0:1], sh, A.logical_shift_right, m, A.bitwise_and)
    fill(["rs7"], T.rs7[:, 0:112:7], 0.0)
    fill(["es0"], T.es[:, 0:1], 0.0)
    copy(["pi%d" % k for k in range(9)], ["ps"], T.ps[:, 0:9], T.pi[:, 1:10])
    fill(["es0"], T.cs[:, 0:273:272], 0.0, add=True)
    fill(["zb"], T.zb[:, 0:256], 0.0)
    act(["imb"], ["mb"], T.mb[:], T.ix[:, 0:32])
    act(["img"], ["omg"], T.omg[:], T.ix[:, 32:48])
    act(["pi4"], ["opv"], T.opv[:, 0:1], T.pi[:, 5:6])
    if s > 0:
        for k, m in enumerate((0xFF00, 0xFF)):
            ts(["pv"], ["pvh"], T.pv[:, k:k + 1], T.pv[:, 2:3], m, A.bitwise_and, add=True)
        for what, a, b in DOWN:
            if what == "table": to_lower(lambda i: T.kd[i], T.mykd[:], "rk", E_TABLE, ["mykd"], range(s)[a:b])
            else: to_lower(lambda i: T.pva[:, 32 * (i % 4) + 4 * (i // 4):32 * (i % 4) + 4 * (i // 4) + 2], T.pv[:, 0:2], "rp", E_FIRST, ["pvh"], range(s)[a:b])
    sent = tot["lk"]
    iota(["idz"], T.ix[:, 80:96], [[256, 2], [2, 8]], -255)
    iota(["zw3"], T.zw[:, 48:64], [[256, 2], [0, 8]], 0)
    lin(["ps"], ["ps10"], P(10), P(5), 32.0, P(3))
    lin(["ps"], ["ps14"], P(14), P(0), 16.0, P(1))
    lin(["ps"], ["p85"], T.v6b[:, 23:24], P(5), 85.0, 0.0)
    for a in range(4):
        tp(["ld"], ["zt"], T.zt[32 * a:32 * a + 32, 0:32], T.ld[:], add=True)
    ts(["spr"], ["spn"], T.spn[0:1, :], T.spr[0:1, :], -1.0, A.mult, 0.5, A.add)
    if NP:
        act(["zt", "mb"], ["m0b"], T.m0[:, 256:512], T.zt[:, 0:32].indirect(T.mb[:, 16:32]))
        copy(["zt", "mb"], ["m0a"], T.m0[:, 0:256], T.zt[:, 0:32].indirect(T.mb[:, 0:16]))
    for out, tok in ((T.vf, "vf"), (T.zw, "zw0")):
        ts(["zt"], [tok], out[:, 0:16], T.zt[:, 0:16], -1.0, A.mult, 65536.0, A.add)
    if NP:
        tp(["m0a"], ["xu"], T.xu[:, 0:256], T.m0[:, 0:256], add=True)
        tp(["m0b"], ["xu"], T.xu[:, 256:512], T.m0[:, 256:512], add=True)
    tt(["vf", "zw0"], ["zw1"], T.zw[:, 16:32], T.vf[:], T.zw[:, 0:16], A.subtract)
    lin(["ps10"], ["ps11"], P(11), P(6), 16.0, P(10))
    if NP: act(["zt", "omg"], ["mg"], T.mg[:], T.zt[:, 0:32].indirect(T.omg[:, 0:16]))
    lin(["imv", "ps11"], ["omv"], T.omv[:], T.ix[:, 64:72], 1.0, P(11))
    if NP:
        tot["rp"] = E_FIRST * higher
        wr["rp"] = [("rp", None)]
    lin(["idz", "ps14"], ["zw2"], T.zw[:, 32:48], T.ix[:, 80:96], 1.0, P(14))
    act(["zw0", "zw1", "zw2", "zw3", "omv"], ["mv"], T.mv[:], T.zw[:, 0:64].indirect(T.omv[:, 0:8]))
    def first_fills():
        iota(["ks4"], T.ks4[:, 0:1], [[0, 1]], 0)
        if not NP:
            iota(["ks4"], T.ks4[:, 1:17], [[0, 16]], 1)
        for n, ap, c in (("d96", T.d96[:], 20), ("nkz", T.nk[:, 0:1], 1)):
            iota([n], ap, [[0, c]], 0)
        iota(["tri0"], T.tri[:], [[1, 32]], 0, -1)

    if s == 0: first_fills()
    E("g", g.partition_broadcast, ["spn"], ["spb"], T.spb[:], T.spn[0:1, :], 128)
    for e in range(N - 1):
        act(["zt", "spb"], ["d7"], T.d7[:, e:112:7], T.zt[0:64, 16:32], AF.Sign, True, bias=T.spb[0:64, e:e + 1])
    if s > 0: first_fills()
    iota(["tr"], T.tr[:, 0:17], [[1, 17]], 672, 16)
    iota(["trc"], T.tr[:, 32:33], [[0, 1]], 672, 16)
    iota(["trd"], T.tr[:, 33:48], [[0, 15]], 1)
    if NP:
        tot["rk"] = E_TABLE * higher
        wr["rk"] = [("rk", None)]
    iota(["zb2"], T.zb[:, 256:544], [[0, 288]], 0)
    iota(["i5"], T.i8[:, 10:15], [[128, 5]], -700)
    iota(["i8"], T.i8[:, 0:8], [[64, 8]], 0)
    iota(["im2"], T.im[:, 20:40], [[0, 2], [1, 5], [0, 2]], 0)
    iota(["ijf"], T.jf[:, 8:13], [[128, 5]], 512)
    iota(["ic"], T.ic[:], [[32, 5], [1, 16]], 0)
    iota(["im"], T.im[:, 0:20], [[8, 2], [1, 5], [0, 2]], 1)
    iota(["hk"], T.hk[:, 3:4], [[0, 1]], 0)
    iota(["qi"], T.qi[:, 3:4], [[0, 1]], 0)
    iota(["cz"], T.cz[:, 3:4], [[0, 1]], 0)
    iota(["xk0"], T.xk[:, 0:16], [[0, 16]], 1)
    iota(["yfz"], T.yf[:, 0:16], [[0, 16]], 0)
    iota(["xkk"], T.xk[:, 16:656], [[-2, 4], [1, 2], [0, 80]] if odd else [[-1, 8], [0, 80]], -odd)

    def numbers():
        for k, src, fn, scale, bias in ((27, 1, AF.Identity, 1.0, -2.5), (28, 0, AF.Identity, 8.0, 0.0), (19, 6, AF.Identity, -8.0, P(0)), (16, 5, AF.Identity, -1.0, P(1)),
                                        (29, 0, AF.Relu, -1.0, 4.0), (9, 8, AF.Relu, -1.0, 1.0), (17, 2, AF.Identity, 8.0, 5.0), (12, 1, AF.Identity, 16.0, 16.0),
                                        (23, 0, AF.Identity, 4.0, 676.0), (41, 2, AF.Identity, -32.0, 0.0)):
            act(["ps"], ["ps%d" % k], P(k), P(src), fn, scale=scale, bias=bias)
        for k, n, add in ((20, 128, -65536.0), (21, 128, -65535.5), (22, 64, 0.0)):
            if s < N - 1: lin(["spb"], ["phi"], T.ps[0:n, k:k + 1], T.spb[0:n, s:s + 1], -1.0, 0.5 + add, True)
            else: lin(["ps"], ["phi"], T.ps[0:n, k:k + 1], T.ps[0:n, 0:1], 0.0, 65536.0 + add, True)
        lin(["ps"], ["phi"], T.ps[64:128, 22:23], T.ps[64:128, 0:1], 0.0, 0.0, True)
        for a, b in ((0, 256), (256, 672)) * (NP // 2):
            lin(["p85", "zb", "zb2"][:2 + a // 256], ["wi"], T.wi[:, a:b], T.zb[:, 0:b - a], 1.0, T.v6b[:, 23:24], True)

    def first_slots():
        scan(["d7", "rs7"], ["d7s"], T.d7s[:], T.rs7[:], T.d7[:], 0.0, A.mult, A.add)
        lin(["d7s"], ["d96"], T.d96[:, 0:16], T.d7s[:, 6:112:7], 40.0, 296.0)

    def constants():
        act(["im2", "ps27"], ["mh"], T.mh[:], T.im[:, 20:40], AF.Sign, bias=P(27))
        lin(["ps23"], ["ps31"], P(31), P(8), 4.0, P(23))
        act(["ps"], ["ps35"], P(35), P(8), AF.Sign, bias=-1.5)
        lin(["ps"], ["ps36"], P(36), P(1), 1.0, -0.5)
        act(["ps27"], ["ps18"], P(18), P(0), AF.Sign, bias=P(27))
        lin(["ps31"], ["ps33"], P(33), P(1), -16.0, P(31))
        lin(["ps9"], ["ps32"], P(32), P(9), P(5), 0.0)
        act(["ps35", "ps36"], ["ps37"], P(37), P(35), AF.Square, scale=-0.5, bias=P(36))
        lin(["ps33", "ps12"], ["ps38"], P(38), P(33), 2.0, P(12))
        lin(["ps29", "ps17"], ["ps26"], P(26), P(29), -1.0, P(17))
        lin(["ps32"], ["ps15"], P(15), P(32), P(6), 0.0)
        lin(["ps38", "ps35"], ["ps39"], P(39), P(35), -8.0, P(38))
        lin(["ps12"], ["ps13"], P(13), P(2), 160.0, P(12))
        lin(["ps18", "ps26"], ["ox6"], T.ox6[:, 0:1], P(18), 1.0, P(26))
        lin(["ps39", "ps37"], ["ps40"], P(40), P(37), -656.0, P(39))
        lin(["ps15", "ps32"], ["ps24"], P(24), P(15), -1.0, P(32))
        lin(["ps13", "ps15"], ["ps25"], P(25), P(13), P(15), 0.0)
        lin(["i5", "ps40"], ["ogt"], T.ogs[:, 10:15], T.i8[:, 10:15], 1.0, P(40))
        act(["zb", "zb2"], ["w2"], T.w2[:, 0:544], T.zb[:])

    def columns():
        act(["ps16"], ["ps30"], P(30), P(16), AF.Square)
        lin(["ijf", "ps28"], ["jf"], T.jf[:, 0:5], T.jf[:, 8:13], 1.0, P(28))
        lin(["ps19"], ["oq"], T.oq[:, 0:1], P(19), 1.0, P(7))
        lin(["ps30", "ps33"], ["ps34"], P(34), P(30), -656.0, P(33))
        lin(["xk0", "phi"], ["xk0"], T.xk[:, 0:16], T.xk[:, 0:16], 1.0, P(22))
        lin(["ic", "ps24", "ps25"], ["cst"], T.cst[:], T.ic[:], P(24), P(25))
        lin(["i8", "ps34"], ["ogs"], T.ogs[:, 0:8], T.i8[:, 0:8], 1.0, P(34))

    lanes = lambda: tp(["mg"], ["xg"], T.xg[:], T.mg[:])
    values = lambda: tp(["mv"], ["val"], T.val[:], T.mv[:])
    aside = lambda: tt(["d96", "tr"], ["dtr"], T.tr[:, 48:64], T.d96[:, 0:16], T.tr[:, 0:16], A.add)
    if NP == 1: lanes()
    for a, b in ((0, 256), (256, 512), (512, 672)) * (NP < 2):
        ts(["p85", "zb"], ["wi"], T.wi[:, a:b], T.zb[:, 0:b - a], T.v6b[:, 23:24], A.add, add=True)
    later += [values, first_slots, aside, lambda: ts(["tri0", "ps41"], ["tri"], T.tri[:], T.tri[:], T.ps[0:64, 41:42], A.is_gt)]

    if NP:
        for h, n in enumerate(lists):
            D("y", "dti%d" % h, T.ti[0:32 * n, 40 * h + 1:40 * h + 33], T.kd[4 * h:4 * h + n], ["rk", "ti"], ["tia%d" % h])
    if sent:
        g.sync.wait_ge(T.sem.lk, sent)
    D("y", "dkc", T.kcs[:].bitcast(dt.uint8), T.kc[:], [], ["kcs"])
    D("y", "dkc", T.kss[:], T.ks[:], [], ["kss"])
    D("y", "dw", T.wb[:], T.w[:], [], ["wb"])
    kb, kept = T.ks4[:, 0:17], T.ks4[:, 1:17]
    if NP:
        n = 256 * NP
        def search(u):
            H, c, b, h, x = "%d" % u, 272 * u, n * u, u * (NP - 1), 256 * u * (2 - NP)
            return [
                lambda: ts(["xu", "pvs"], ["cm" + H], T.cm[:, b:b + n], T.xu[:, x:x + n], T.pvs[:, 4 * h:4 * h + 1], A.subtract, T.pvs[:, 4 * h + 1:4 * h + 2], A.is_ge),
                lambda: tp(["cm" + H], ["ct" + H], T.ct[:, b:b + n], T.cm[:, b:b + n]),
                lambda: scan(["ct" + H], ["cs" + H], T.cs[:, c + 1:c + 1 + n // 2], T.ct[:, b:b + n:2], T.ct[:, b + 1:b + n:2], 0.0, A.add, A.add),
                lambda: tt(["cs" + H, "es0"], ["of" + H], T.of1[:, b // 32:(b + n) // 32], T.cs[:, c + 16:c + 1 + n // 2:16], T.cs[:, c:c + n // 2:16], A.subtract),
                lambda: tt(["ti", "tia%d" % h, "of" + H, "xg"], ["eq" + H], T.eq[:, b // 2:(b + n) // 2], T.ti[:, 40 * h:40 * h + 33].indirect(T.of1[:, b // 32:(b + n) // 32]),
                           T.xg[:, x // 2:(x + n) // 2], A.is_equal),
                lambda: tp(["eq" + H], ["et"], T.et[:, u:n:2] if NP == 2 else T.et[:, b // 2:(b + n) // 2], T.eq[:, b // 2:(b + n) // 2], add=True)]
        steps = [search(u) for u in (0, 1)]
        copy(["rp", "pv0", "opv"], ["pvs"], T.pvs[:], T.pva[:, 0:128].indirect(T.opv[:, 0:1]))
        if NP == 2: lanes()
        for k in range(6):
            steps[0][k]()
            if k == 2: numbers()
            if k == 3: gap()
            steps[1][k]()
        gap()
        if higher > 2: scan(["et"], ["es"], T.es[:, 1:n + 1], T.et[0:64, 0:n], T.et[64:128, 0:n], 0.0, A.add, A.add)
        else: n = 128; scan(["et"], ["es"], T.es[:, 1:n + 1], T.et[0:64, 0:256:2], T.et[0:64, 1:256:2], 0.0, A.add, A.add)
        w = n // 16
        if higher > 1:
            tt(["es", "es0"], ["c4"], T.c4[:, 0:17], T.es[0:32, 0:n + 1:w], T.es[32:64, 0:n + 1:w], A.add)
        now, before = (T.c4[:, 1:17], T.c4[:, 0:16]) if higher > 1 else (T.es[0:32, w:n + 1:w], T.es[0:32, 0:n:w])
        for a in (0, 1):
            tt(["c4", "es", "es0"], ["ks4"], T.ks4[32 * a:32 * a + 32, 1:17], now, before, A.is_equal, add=a > 0)
    else:
        numbers()
        gap(4)
    gap(2)
    scan(["ks4", "d96"], ["pl"], T.pl[:, 0:17], kb, T.d96[:, 0:17], 0.0, A.add, A.max)
    act(["ks4"], ["pln"], T.nj[:], kept, accum_out=T.pl[:, 20:21])
    tt(["ks4", "tr"], ["f1"], T.f1[:], kept, T.tr[:, 0:16], A.mult)
    tt(["ks4", "tr"], ["nk"], T.nk[:, 1:17], kept, T.tr[:, 1:17], A.mult)
    ts(["pl", "tri"], ["pm"], T.pt[:, 32:64], T.tri[:], T.pl[:, 16:17], A.mult)
    lin(["pln", "tri"], ["pn"], T.pt[:, 0:32], T.tri[:], T.pl[:, 20:21], 0.0)
    constants()
    tt(["f1", "nk", "nkz"], ["d0a"], T.dd[:, 48:64], T.nk[:, 0:16], T.f1[:], A.subtract)
    tt(["f1", "dtr"], ["d1"], T.dd[:, 96:112], T.tr[:, 48:64], T.f1[:], A.subtract)
    tp(["pm"], ["dm"], T.dd[:, 64:96], T.pt[:, 32:64])
    tt(["d0a", "trc", "trd"], ["d0"], T.dd[:, 32:48], T.dd[:, 48:64], T.tr[:, 32:48], A.add)
    tp(["pn"], ["dn"], T.dd[:, 0:32], T.pt[:, 0:32])
    for a in (0, 1):
        scan(["d0", "d1", "dm", "dn"], ["pw"], T.pw[64 * a:64 * a + 64, 8 - 8 * a:56 - 8 * a], T.dd[:, 0:48], T.dd[:, 64:112], 0.0, A.add, A.max, add=True)
    E("v", V.quantize_mx, ["zb", "zb2"], ["zc", "zs"], T.zc[:], T.zs[:], T.zb[:, 0:512])
    D("y", "dz", T.lc[:, 0:16].bitcast(dt.uint8), T.zc[:, 0:16].bitcast(dt.uint8), ["zc"], ["lcz"])
    D("y", "dz", T.ls[:, 0:16], T.zs[:, 0:16], ["zs"], ["lsz"])
    E("v", V.tensor_copy, ["pw", "val"], ["wi"], T.wi[:, 0:2384].indirect(T.pw[:, 40:48]), T.val[:])
    tt(["im", "mh"], ["mo"], T.mo[:], T.im[:, 0:20], T.mh[:], A.add)
    nb32, c = 20 + odd, 672 * (1 - odd)
    for k in (1 - odd, odd):
        tp(["wi"], ["wt%d" % k], T.wt[:, 672 * k:672 + 640 * k], T.wi[:, 16 * k:672 - 16 * k])
    scan(["wt%d" % (1 - odd)], ["hk"], T.hk[:, 4:4 + 4 * nb32], T.wt[0:64, c:c + 32 * nb32:8], T.wt[64:128, c:c + 32 * nb32:8], 0.0, A.add, A.add)
    for k in (0, 1):
        tt(["hk"], ["qk"], T.qk[64 * k:64 * k + 64, 0:nb32], T.hk[:, 7:4 + 4 * nb32:4], T.hk[:, 3:4 * nb32:4], A.subtract, add=True)
    act(["wt0", "wt1", "ogt"], ["yy"], T.yy[:], T.wt[:, 0:1312].indirect(T.ogs[:, 10:15]))
    peers = [(s + i) % N for i in range(1, N)]
    keys = lambda d: (T.kx[:, 4 * slot(s, d):4 * slot(s, d) + 3], T.qk[:, (5 * d + odd) // 2:(5 * d + odd) // 2 + 3])
    fused([(T.cores[d],) + keys(d) for d in peers], "rx%d" % wave(s), [2] * len(peers), ["qk"])
    act(["qk"], ["kx%d" % wave(s)], *keys(s))
    columns()
    scan(["yy"], ["qi"], T.qi[:, 4:84], T.yy[0:64, :], T.yy[64:128, :], 0.0, A.add, A.add)
    for k in (0, 1):
        tt(["qi"], ["off"], T.off[64 * k:64 * k + 64, :], T.qi[:, 5:84:2], T.qi[:, 3:82:2], A.subtract, add=True)
    E("v", V.quantize_mx, ["wb"], ["wc", "wz"], T.wc[:], T.wz[:], T.wb[:])
    near = s - s % 4
    far = N // 2 - near
    codes_to = lambda d: (T.lc[:, 16 + 80 * slot(s, d):96 + 80 * slot(s, d)].bitcast(dt.uint8), T.qc[:, 80 * d:80 * d + 80].bitcast(dt.uint8))
    scales_to = lambda d: (T.ls[:, 16 + 80 * slot(s, d):96 + 80 * slot(s, d)], T.qs[:, 80 * d:80 * d + 80])

    me, nb = s - odd, (s - odd) ^ 2
    parts = {"0": (far, far + 4), "1": (me, me + 2), "2": (nb, nb + 2)}

    def send(k, to, sem, toks):
        a, b = parts[k]
        part = [d for d in range(a, b) if d != s]
        e = len(topo.engines(core, T.cores[part[0]])) // (b - a)
        fused([(T.cores[d],) + to(d) for d in part], sem + k, [e] * len(part), toks)
        if a <= s < b: D("y", "d" + sem, *to(s), toks, ["o" + sem])

    def codes(k):
        a, b = parts[k]
        E("v", V.tensor_copy, ["off", "kcs"], ["qc" + k], T.qc[:, 80 * a:80 * b].bitcast(dt.uint32), T.kcs[:, 0:512].bitcast(dt.uint32).indirect(T.off[:, 5 * a:5 * b]))
        send(k, codes_to, "rc", ["qc" + k])

    def scales(k, move=act):
        a, b = parts[k]
        move(["off", "kss"], ["qs" + k], T.qs[:, 80 * a:80 * b], T.kss[:, 0:512].indirect(T.off[:, 5 * a:5 * b]))
        send(k, scales_to, "rs", ["qs" + k])

    for u in range(3):
        tot["rx%d" % u] = sum(2 for r in range(N) if r != s and wave(r) == u)
        wr["kx%d" % u] = wr.get("kx%d" % u, []) + [("rx%d" % u, None)]
    xs = ["xf0", "xf1", "xf2"]

    def spread(u, q):
        a, b = 160 * u, 160 * u + (320 if u == 2 else 160)
        sides = T.mm[:, a:b], T.kx[:, 8 * u:8 * u + (b - a) // 20].indirect(T.mo[:, 0:(b - a) // 16])
        if q == "s": act(["mo", "phi", "kx%d" % u], ["mm%d" % u], *sides, AF.Identity, bias=P(20))
        else: ts(["mo", "phi", "kx%d" % u], ["mm%d" % u], *sides, P(20), A.add)
        return lambda: tp(["mm%d" % u], [xs[u]], T.xf[:, a:b], T.mm[:, a:b])

    def signs(e, a, b, col):
        act(xs[a // 160:(b + 160) // 320 + 1] + ["v6"], ["jk%d" % col, "sm%d" % col], T.jk[:, 640 * e - 1920 + a:640 * e - 1920 + b], T.xf[:, a:b], AF.Sign,
            scale=-1.0, bias=T.v6[:, e:e + 1], accum_out=T.sm[:, col:col + 1])

    def larger(k, a, b):
        ts(xs[a // 160:(b + 160) // 320 + 1] + ["v6l"], ["cb%d" % k], T.cb[:, 640 * k + a:640 * k + b], T.xf[:, a:b], T.v6b[:, k:k + 1], A.subtract, T.v6b[:, 16 + k:17 + k], A.is_gt, add=True)

    gap(len(later))
    turn = {}

    def rows():
        for out, tok in ((T.v6, "v6"), (T.v6b, "v6h")):
            ts(["ox6", "phi", "kx0", "kx1", "kx2"], [tok], out[:, 0:16], T.kx[:, 0:32].indirect(T.ox6[:, 0:1]), P(21), A.add, 0.5, A.max)

    def halves():
        tt(["v6", "v6h"], ["v6l"], T.v6b[:, 16:20], T.v6[:, 0:4], T.v6b[:, 0:4], A.subtract)
        ts(["v6"], ["pd"], T.pd[:, 0:5], T.v6[:, 0:5], 1.0, A.is_lt)

    def aside(q):
        for e in (3, 4):
            ts(["pd", "jf"], ["jt%d" % e], T.pd[:, 8 + e:9 + e], T.pd[:, e:e + 1], T.jf[:, e:e + 1], A.mult, 80.0 * e, A.add)

    step = {"c": codes, "s": scales, "v": lambda k: scales(k, copy), "m": lambda u: turn.update({u: spread(int(u), "s")}), "n": lambda u: turn.update({u: spread(int(u), "v")}), "t": lambda u: turn[u](),
            "r": lambda _: rows(), "h": lambda _: halves(), "a": aside, "L": lambda k: larger(int(k), 0, 640),
            "p": lambda _: tt(["pd", "jf"], ["pd2"], T.v6b[:, 20:23], T.pd[:, 0:3], T.jf[:, 0:3], A.mult),
            "e": lambda k: larger(int(k), 160, 640), "l": lambda k: larger(int(k), 0, 160), "g": lambda e: signs(int(e), 0, 640, int(e)),
            "f": lambda e: lin(["sm" + e, "jt" + e], ["pu" + e], T.pu[:, 958 + int(e):959 + int(e)], T.sm[:, int(e):int(e) + 1], -0.5, T.pd[:, 8 + int(e):9 + int(e)]),
            "z": lambda k: scan(["cb" + k, "pd2"], ["pu"], T.pu[:, 1 + int(k):959 + int(k):3], T.cb[:, 640 * int(k):640 * int(k) + 320], T.cb[:, 640 * int(k) + 320:640 * int(k) + 640],
                                T.v6b[:, 20 + int(k):21 + int(k)], A.add, A.add, add=True)}
    step.update({"G": lambda _: signs(3, 160, 640, 3),
                 "j": lambda _: scan(["cb3", "jt3"], ["jt2"], T.j3[:], T.cb[:, 1920:2000], T.cb[:, 2000:2080], T.pd[:, 11:12], A.add, A.add),
                 "F": lambda _: lin(["sm3", "jt2"], ["pu3"], T.pu[:, 961:962], T.sm[:, 3:4], -0.5, T.j3[:, 79:80])})
    step["x"] = lambda _: E("g", g.affine_select, xs, ["xkk"], T.xk[0:64, 16:656], T.xf[0:64, :], [[0, 640]], A.is_ge, 0.0, 0, 0)
    step.update({"H": lambda _: signs(3, 0, 160, 2),
                 "A": lambda _: [lin(["pd", "jf"], ["jt%d" % e], T.pd[:, 8 + e:9 + e], T.pd[:, e:e + 1], T.jf[:, e:e + 1], 320.0) for e in (3, 4)],
                 "B": lambda _: [ts(["pd", "jf"], ["jt%d" % e], T.pd[:, 8 + e:9 + e], T.pd[:, e:e + 1], T.jf[:, e:e + 1], A.mult, 320.0, A.add) for e in (3, 4)],
                 "J": lambda _: lin(["sm3", "jt3"], ["jt2"], T.pd[:, 10:11], T.sm[:, 3:4], -0.5, T.pd[:, 11:12]),
                 "K": lambda _: lin(["sm2", "jt2"], ["pu3"], T.pu[:, 961:962], T.sm[:, 2:3], -0.5, T.pd[:, 10:11])})
    for x in (ORDER if NP == 2 else EARLY).split():
        step[x[0]](x[1:])
    E("v", V.tensor_copy, ["pu", "pu3", "pu4", "cst"], ["w2"], T.w2[:, 16:1744].indirect(T.pu[:, 958:963]), T.cst[:])
    for k in (0, 1):
        tp(["w2"], ["w2t"], T.w2t[:, 672 * k:544 + 640 * k], T.w2[:, 16 * k:544 - 16 * k], add=True)
    for n in ("rc0", "rs0", "rc1", "rs1", "rc2", "rs2"):
        tot[n] = 8 if n[2] == "1" else 16
        wr[n] = [(n, None)]
    land, lands = ["rc0", "rc1", "rc2", "orc", "lcz"], ["rs0", "rs1", "rs2", "ors", "lsz"]

    def product(k, move=act):
        u, a = (("1", me), ("0", far), ("0", far + 2), ("2", nb))[k]
        c = 16 + 80 * a
        E("t", g.tensor.matmul_mx, ["rc" + u, "rs" + u, "wc", "wz"] + ["orc", "ors"] * (k == 0), ["acc%d" % k], T.acc[:, 512 * k:512 * k + 160], T.wc[:], T.wz[:], T.lc[:, c:c + 160], T.ls[:, c:c + 160], True, True)
        move(["acc%d" % k], ["yf"], T.yf[:, c:c + 160], T.acc[:, 512 * k:512 * k + 160], add=True)

    product(LAST[3])
    copy(["w2t", "ogs"], ["sy"], T.sy[:], T.w2t[:, 0:1184].indirect(T.ogs[:, 0:8]))
    for k in LAST[:2]: product(k)
    scan(["sy"], ["cz"], T.cz[:, 4:132], T.sy[0:64, :], T.sy[64:128, :], 0.0, A.add, A.add)
    for a in (0, 1):
        tt(["cz"], ["so"], T.so[32 * a:32 * a + 32, :], T.cz[0:32, 3:132:4], T.cz[32:64, 3:132:4], A.add, add=a > 0)
    for a in (0, 1):
        tt(["so"], ["of2"], T.of2[64 * a:64 * a + 64, :], T.so[:, 1:33], T.so[:, 0:32], A.subtract, add=True)
    need("s", lands + ["xkk", "xk0"], [])
    product(LAST[2], act)
    E("g", g.affine_select, ["of2"], ["o2f"], T.o2f[:], T.of2[:], [[0, 32]], A.is_ge, 0.0, 0, 0)
    for k, (a, b) in enumerate(PIECES):
        E("v", V.tensor_copy, land + ["of2"], ["fc%d" % k], T.fc[:, a:b].bitcast(dt.uint32), T.lc[:, 0:656].bitcast(dt.uint32).indirect(T.of2[:, a // 16:b // 16]))
        act(["yfz", "yf", "of2"], ["yo%d" % k], T.yo[:, a:b], T.yf[:, 0:656].indirect(T.of2[:, a // 16:b // 16]))
        D("y", "dout", T.oc[:, 4 * a:4 * b], T.fc[:, a:b].bitcast(dt.uint8), ["fc%d" % k], ["oc"])
        D("y", "dout", T.y[:, a:b], T.yo[:, a:b], ["yo%d" % k], ["y"])
        if k: copy(["o2f", "oq"], ["og"], T.og[:], T.o2f[:, 0:32].indirect(T.oq[:, 0:1]))
    for move, a, b in ((copy, 0, 352), (act, 352, 512)):
        move(lands + ["of2"], ["fz%d" % a], T.fz[:, a:b], T.ls[:, 0:656].indirect(T.of2[:, a // 16:b // 16]))
    act(["xkk", "xk0", "og"], ["ko"], T.ko[:], T.xk[:, 0:656].indirect(T.og[:, 0:8]), AF.Identity, scale=-1.0, bias=P(22))
    for j in range(4):
        D("ys"[j // 2], "dout", T.osc[4 * j:4 * j + 4, :], T.fz[32 * j:32 * j + 4, :], ["fz0", "fz352"], ["osc"])
    D("y", "dout", T.ok[:], T.ko[0:128:16, :], ["ko"], ["ok"])
    for n in SEMAPHORES:
        if tot[n]:
            g.wait_ge(T.sem[n], tot[n])
